import numpy as np, ml_dtypes
CORES = [66,74,82,90,194,202,210,218]
N = 8
BF = ml_dtypes.bfloat16
def gentries(a):
    return np.ascontiguousarray(a.reshape(8, 16, -1).transpose(0, 2, 1)).reshape(8, -1)
def gtable(e):
    e = np.asarray(e); return np.ascontiguousarray(e.reshape(8, -1, 16).transpose(0, 2, 1)).reshape(128, -1).astype(np.int32)
V, G, Q, LN, CAP, RO = 1024, 896, 2, 256, 32, 4
W = V + Q * G
def ghosts(a):
    return np.concatenate([a] + [np.roll(a, -d, axis=0)[..., :G] for d in range(1, Q + 1)], axis=-1)
def lists(rng, cl, share):
    cw = ghosts(cl); out = np.zeros((N, 8, 16, V), np.int64)
    for a in range(N):
        for g in range(8):
            c = cw[a, g]; o = np.argsort(c + rng.random(W)); cnt = np.bincount(c); s = np.add.accumulate(cnt) - cnt; m = cl[a, g]
            y = o[s[m] + (rng.random((16, V)) * cnt[m]).astype(np.int64)]
            out[a, g] = np.where(rng.random((16, V)) < share, rng.integers(0, W, (16, V)), y)
    return out
def front(rng, x, l, share):
    xw = ghosts(x).astype(np.int16)
    for a in range(N):
        for g in range(8):
            y = l[a, g]; e = np.sum(np.abs(xw[a, g][:, y] - xw[a, g][:, None, :V]), axis=0)
            k = np.argmin(np.where(y == np.arange(V), 9999, e), axis=0); w = np.nonzero(rng.random(V) < share[a, g])[0]
            old = y[0, w].copy(); y[0, w] = y[k[w], w]; y[k[w], w] = old
    return l
def parts(rng):
    kc = W // 24; cl = rng.integers(0, kc, (N, 8, V)); cen = rng.integers(0, 256, (8, kc, 16))
    x = cen[np.arange(8)[None, :, None], cl].transpose(0, 1, 3, 2) + rng.integers(-24, 25, (N, 8, 16, V))
    return np.clip(x, 0, 255), lists(rng, cl, 0.12)
def pack(x, l, p, th):
    return {"feat": np.ascontiguousarray(x.reshape(N, 128, V)).astype(np.float32).astype(BF), "hits": np.ascontiguousarray(l.reshape(N, 128, V)).astype(np.int32),
            "lane0": np.stack([gtable(a) for a in p]), "th": np.ascontiguousarray(np.reshape(th, (N, 8, 1))).astype(np.int32)}
def setup_inputs(rng):
    x, l = parts(rng); l = front(rng, x, l, rng.choice(np.array([0.3, 0.6, 0.9]), (N, 8)))
    return pack(x, l, rng.integers(0, V, (N, 8, LN)), rng.integers(60, 400, (N, 8)))
def setup_inputs_ends(rng):
    e = np.array([0, W - 1]); x = 255 * rng.integers(0, 2, (N, 8, 16, V)); x[:, 1::2] = x[:, 1::2, :1].copy()
    x[:, 1::2, :, 0] = 0; x[:, 1::2, :, G - 1] = 0; x[:, 1::2, :, G] = 0; x[:, 1::2, :, V - 4:] = 255
    l = np.zeros((N, 8, 16, V), np.int64); p = np.zeros((N, 8, LN), np.int64); k = 3 * LN // 5 + 1; n = LN - k - 3
    for a in range(N):
        for g in range(8):
            o = np.sort(rng.permutation(np.setdiff1d(np.arange(1, V - 4), np.array([G - 1, G])))[:2 * n].reshape(n, 2), axis=1)
            v = np.append(o[:, 0], V - 2); b = np.append(o[:, 1], V - 1); xx = x[a, g]
            if g % 2 == 1: xx[:, v] = 255
            xx[:, b] = xx[:, v]
            y = np.where(rng.random((16, V)) < 0.7, rng.choice(e, (16, V)), rng.integers(0, W, (16, V)))
            y[:, v] = rng.choice(e, (16, n + 1)); y[:, b] = rng.choice(e, (16, n + 1))
            y[rng.integers(0, 15, n + 1), v] = b; y[0, b] = v; y[15, V - 2] = W - 1; y[15, V - 1] = W - 1
            y[:, V - 3] = rng.choice(e, 16); y[0, V - 3] = W - 1; y[15, V - 3] = 0
            y[:, V - 4] = W - 1; y[7, V - 4] = G; y[15, V - 4] = G - 1
            l[a, g] = y
            p[a, g] = np.concatenate([rng.permutation(np.concatenate([rng.choice(np.array([0, V - 1]), k), o[:, 0]])), np.array([V - 4, V - 3, V - 2])])
    return pack(x, l, p, np.stack([rng.permutation(np.array([0, 4080] * 4)) for a in range(N)]))
def setup_inputs_corners(rng):
    x = rng.integers(0, 256, (N, 8, 16, V)); l = np.zeros((N, 8, 16, V), np.int64); p = np.zeros((N, 8, LN), np.int64)
    half = G // 2; me = np.arange(V); p1 = LN // 2; p2 = LN // 8
    for a in range(N):
        for g in range(8):
            even = g % 2 == 0; n = int(rng.choice(np.array([0, 1, CAP - 1, CAP, CAP + 1, p1])))
            if a == 0: n = (CAP, CAP + 1, p1, CAP - 1, 1, 0, CAP, CAP + 1)[g]
            u = G + 1 + rng.permutation(V - G - 2)[:2 * p2]
            if even: u[0] = G
            u = np.sort(u)
            lo = rng.permutation(half)[:p1]; hi = rng.permutation(np.setdiff1d(np.arange(half, V - 1), np.append(u, np.array([G - 1, G]))))[:p1]
            if even:
                lo[0] = G - 1; hi[0] = V - 1
            else:
                hi[0] = G - 1; hi[1] = G
            v = np.concatenate([lo, u[0::2]]); b = np.concatenate([hi, u[1::2]])
            rest = np.setdiff1d(me, np.concatenate([v, b]))
            y = np.where(rng.random((16, V)) < 0.5, (rng.random((16, V)) * me).astype(np.int64), rng.integers(V, W, (16, V)))
            y = np.where(rng.random(V) < 0.0625, me, y)
            z = rest[rng.random(rest.size) < 0.5]; y[rng.integers(0, 8, z.size), z] = V + G - 1
            if Q > 1:
                z = rest[rng.random(rest.size) < 0.5]; y[rng.integers(8, 16, z.size), z] = V + G
            y[:, v] = rng.integers(V, W, (16, v.size)); y[:, b] = rng.integers(V, W, (16, v.size))
            r = rng.integers(0, 16, v.size)
            if even: r[0] = 1 + r[0] % 15
            y[r, v] = b; y[0, b] = v
            if even:
                y[0, v[0]] = rng.integers(0, G - 1); y[r[0], b[0]] = rng.integers(0, G - 1)
            l[a, g] = y
            xx = x[a, g]; xx[:, b] = xx[:, v]
            f = rng.integers(0, 16, v.size); s = rng.integers(2, 4, v.size); xx[f, b] += np.where(xx[f, b] < 128, s, -s)
            w = rng.choice(rest, LN - n - p2)
            if g == 7: w[:] = rest[-1]
            o = np.concatenate([lo[:n], u[0::2], w]); k = 2 if n >= 2 and not even else 0
            p[a, g] = np.concatenate([o[:k], rng.permutation(o[k:])])
    return pack(x, l, p, rng.choice(np.array([0, 1, 200, 4079, 4080]), (N, 8)))
def setup_inputs_trees(rng):
    x, l = parts(rng); p = np.zeros((N, 8, LN), np.int64); j = np.arange(16)
    th = rng.choice(np.array([0, 100, 500, 4080]), (N, 8)); th[:, 1] = rng.choice(np.array([0, 100, 500]), N)
    at = 2 * (j & 1) + 8 * ((j >> 1) & 1) + 32 * ((j >> 2) & 1) + 128 * ((j >> 3) & 1)
    for a in range(N):
        for g in (0, 1, 3, 4, 5, 7):
            n = LN // 16 if g % 2 == 0 else LN // 32; k = 8 * (g % 2); c = rng.permutation(V)
            o = np.sort(c[:16 * n].reshape(n, 16), axis=1); xx, y = x[a, g], l[a, g]
            for i in range(n):
                xx[:, o[i]] = rng.integers(0, 86, (16, 1)) + at[None, :]
                y[:, o[i]] = rng.permutation(o[i])[:, None]
            s = np.sort(c[16 * n:16 * n + 3 * k].reshape(k, 3), axis=1); u, b, w = s[:, 0], s[:, 1], s[:, 2]
            xx[:, b] = xx[:, u] ^ 128; y[:, u] = b; y[:, b] = u; y[:, w] = b
            p[a, g] = rng.permutation(np.concatenate([o.reshape(-1), b, w, rng.integers(0, V, LN - 16 * n - 2 * k)]))
    for g in (2, 6):
        th[:, g] = np.where((np.arange(N) + g // 4) % 2 == 0, 4080, rng.integers(1000, 1500, N))
        x[:, g] = rng.integers(0, 256, (N, 16, V)); pr = np.zeros((N, 2 * CAP, 2), np.int64)
        for a in range(N): pr[a] = np.sort(rng.permutation(G - 1)[:4 * CAP].reshape(2 * CAP, 2), axis=1)
        for a in range(N):
            u, b = pr[a, :, 0], pr[a, :, 1]; xx, y = x[a, g], l[a, g]
            o = rng.permutation(np.setdiff1d(np.arange(V), np.concatenate([u, b, np.array([G - 1, G])]))); w = o[:CAP]; s = o[CAP:LN - 2 * CAP]
            xx[:, b] = np.clip(xx[:, u] + rng.integers(-8, 9, (16, 2 * CAP)), 0, 255)
            y[:, u] = b; y[:, b] = rng.choice(np.array([G - 1, G]), (16, 2 * CAP)); y[0, b] = u; y[:, w] = u[:CAP]
            d = rng.integers(0, Q, (16, s.size)); m = pr[(a + 1 + d) % N, rng.integers(0, 2 * CAP, d.shape), rng.integers(0, 2, d.shape)]
            y[:, s] = V + d * G + np.where(rng.random(d.shape) < 0.75, m, rng.integers(0, G, d.shape))
            p[a, g] = rng.permutation(np.concatenate([b, w, s]))
    return pack(x, l, p, th)
def setup_inputs_ties(rng):
    x = np.full((N, 8, 16, V), 100); x[:, :, 3] += rng.integers(0, 3, (N, 8, V)); x[:, :, 12] += rng.integers(0, 3, (N, 8, V))
    x[..., :] += rng.integers(0, 156 - 2, (N, 8, 1, 1)) * rng.integers(0, 2, (N, 8, 1, V))
    l = lists(rng, rng.integers(0, W // 24, (N, 8, V)), 0.1); l[:, ::2, 8:] = l[:, ::2, :8].copy()
    l = front(rng, x, l, np.full((N, 8), 0.6))
    p = rng.integers(0, V, (N, 8, LN)); p[:, 1::4] = rng.integers(0, 64, (N, 2, LN)); p[:, 3] = V - 1 - rng.integers(0, 128, (N, LN))
    th = rng.integers(0, 5, (N, 8)); th[:, 6] = 2049 + 2 * rng.integers(0, 1016, N); th[:, 7] = rng.choice(np.array([2049, 2051, 4077, 4079]), N)
    for a in range(N):
        for g in (6, 7):
            m = 4 * rng.permutation(V // 4)[:8]; o = rng.permutation(np.setdiff1d(np.arange(V), np.concatenate([m, m + 1])))[:72]
            n = o[:32]; s = np.sort(o[32:64].reshape(16, 2), axis=1); v, b = s[:, 0], s[:, 1]; xx, y = x[a, g], l[a, g]; t = int(th[a, g])
            xx[:, o[:64]] = 0; xx[:, m] = 128; xx[:, m + 1] = 128
            xx[:, o[64:68]] = ((t + np.arange(16)) // 16)[:, None]; xx[:, o[68:72]] = ((t + 1 + np.arange(16)) // 16)[:, None]
            j = rng.integers(0, 8, 32); y[:, n] = o[64 + rng.integers(0, 8, (16, 32))]; y[0, n] = m[j] + 1; y[15, n] = m[j]
            j = rng.integers(0, 8, 16); y[:, v] = m[j] + 1; y[:, b] = m[j]; y[0, v] = b; y[0, b] = v
            p[a, g] = rng.permutation(np.concatenate([n, v, rng.integers(0, V, LN - 48)]))
    return pack(x, l, p, th)
def setup_inputs_spread(rng):
    x = np.minimum((np.exp2(8 * rng.random((N, 8, 1, V))) * rng.random((N, 8, 16, V))).astype(np.int64), 255)
    l = lists(rng, ((W // 16) * rng.random((N, 8, V)) ** 2).astype(np.int64), 0.1); l = front(rng, x, l, rng.choice(np.array([0.5, 1.0]), (N, 8)))
    return pack(x, l, (V * rng.random((N, 8, LN)) ** 1.5).astype(np.int64), (4081 * rng.random((N, 8)) ** 2).astype(np.int64))
def check_inputs(d):
    bad = []
    for k, lo, hi in (("feat", 0, 255), ("hits", 0, W - 1), ("lane0", 0, V - 1), ("th", 0, 4080)):
        v = np.asarray(d[k]).astype(np.float64)
        if not (np.min(v) >= lo and np.max(v) <= hi): bad.append("range of " + k)
        elif np.any(v != np.floor(v)): bad.append("whole numbers of " + k)
    return bad
def at_names(tab, names):
    return np.take_along_axis(tab, names.reshape(N, 8, -1), 2).reshape(names.shape)
def far(x, names, y):
    s = np.zeros(names.shape, np.int64)
    for f in range(16): s += np.abs(at_names(x[:, :, f], names) - y[:, :, f][:, :, None, :])
    return s
def reference(feat, hits, lane0, th):
    x = ghosts(feat.astype(np.float32).astype(np.int64).reshape(N, 8, 16, V)); l = ghosts(hits.astype(np.int64).reshape(N, 8, 16, V))
    t = th.astype(np.int64).reshape(N, 8, 1, 1); p = np.stack([gentries(a) for a in lane0]).astype(np.int64)
    for d in range(1, Q + 1):
        off = V + (d - 1) * G; h = l[..., off:off + G]
        l[..., off:off + G] = np.where(h < G, off + h, off + np.arange(G))
    fw = np.tile(np.arange(W), (N, 8, 1)); best = l[:, :, 0, :V].copy()
    lower = np.arange(LN)[None, :] < np.arange(LN)[:, None]
    for rnd in range(RO):
        v = p; awake = ~np.any((v[..., :, None] == v[..., None, :]) & lower, axis=3)
        v4 = v[:, :, None, :]
        c = at_names(fw, np.take_along_axis(l, v4, 3)); xv = np.take_along_axis(x, v4, 3)
        e = np.where(c == v4, 4096, far(x, c, xv))
        b = np.min(e * 4096 + c, axis=2) & 4095; b4 = b[:, :, None, :]
        a, g, i = np.nonzero(awake); best[a, g, v[a, g, i]] = b[a, g, i]
        own = b < V
        back = at_names(fw, at_names(best, np.minimum(b, V - 1)))
        join = awake & own & (b > v) & (back == v)
        o = at_names(fw, np.take_along_axis(l, b4, 3)); xn = (xv + np.take_along_axis(x, b4, 3)) >> 1
        kc = np.where((c == v4) | (c == b4), 4096 * 4096 + v4, far(x, c, xn) * 4096 + c)
        ko = np.where((o == v4) | (o == b4), 4096 * 4096 + v4, far(x, o, xn) * 4096 + o)
        nl = np.where(join[:, :, None, :], np.minimum(kc, ko) & 4095, np.where(e > t, o, c))
        ct = c[:, :, rnd]
        to = np.where(join, v, np.where(own, b, np.where(ct < V, ct, v)))
        p = np.where(awake, to, v)
        a, g, i = np.nonzero(awake)
        l[a, g, :, v[a, g, i]] = nl[a, g, :, i]
        a, g, i = np.nonzero(join); x[a, g, :, v[a, g, i]] = xn[a, g, :, i]; fw[a, g, b[a, g, i]] = v[a, g, i]
        tell = join & (v < G); cnt = np.add.accumulate(tell.astype(np.int64), axis=2); tell = tell & (cnt <= CAP)
        a, g, i = np.nonzero(tell); m = v[a, g, i]; w = b[a, g, i]; y = nl[a, g, :, i]
        for d in range(1, Q + 1):
            off = V + (d - 1) * G; q = (a - d) % N
            x[q, g, :, off + m] = xn[a, g, :, i]; l[q, g, :, off + m] = np.where(y < G, off + y, (off + m)[:, None])
            s = w < G; fw[q[s], g[s], off + w[s]] = off + m[s]
        fw = np.take_along_axis(fw, fw, 2); p = at_names(fw, p)
    return {"yx": x[..., :V].reshape(N, 128, V).astype(np.float32).astype(BF), "yl": l[..., :V].reshape(N, 128, V).astype(np.float32), "yf": fw[..., :V].astype(np.float32)}

@@ -1,0 +1,743 @@
+from concourse.bass import DstId, RemoteDMATransfer
+from concourse.mybir import AluOpType as A, AxisListType, ActivationFunctionType as F
+
+V, GH, W, LN, RO = 1024, 896, 2816, 256, 4
+WD = W + LN
+BIG = float(2 ** 26)
+CLAMP = float(4080 * 4096)
+MAGIC = float(3 * 2 ** 22)
+ACT_SCATTER = True
+OPT = [0, 0, 0]
+OFF1, OFF2 = [1, 1, 1, 1], [0, 0, 0, 0]
+HOP, PASSES = 150.0, 12
+PLAN = []
+
+SCRATCH = {}
+
+
+def _buf(names, n, dtp, where="sbuf"):
+    for x in names.split():
+        SCRATCH[x] = (where, [128, n], dtp)
+
+
+_buf("X", WD, "bfloat16")
+_buf("NB MH", W, "bfloat16")
+_buf("L B M0 M1", WD, "float32")
+_buf("HI", V, "int32")
+_buf("GA", GH, "bfloat16")
+_buf("GB", GH, "float32")
+_buf("GL", GH, "uint16")
+_buf("LG", 2 * GH, "uint16")
+_buf("DC DO D0 D1 D2 E", 4096, "bfloat16")
+_buf("TRI XC", 2048, "bfloat16")
+_buf("HB", 512, "bfloat16")
+_buf("SA SY SP SX SN SS SM S32", 144, "bfloat16")
+_buf("Z0 IU", 144, "float32")
+_buf("RN BD32 BDC BD1 IBIG I24 I1 IM1 I014 IH WBH UP", 128, "bfloat16")
+_buf("WBL IG MT", 128, "float32")
+_buf("A1 A2 Y NL MB MZ", 272, "float32")
+_buf("Z1 Z2 SL", 512, "float32")
+_buf("MV", 272, "bfloat16")
+_buf("ZZ", 1024, "bfloat16")
+_buf("XV", 512, "bfloat16")
+_buf("CF OF KEY KC VT CT BJT XM ZS ZT LC", 256, "float32")
+_buf("HZ ONE I256 CR EQ1 EQ2 EQ3 EQ4 UPM NJT BB BK", 256, "bfloat16")
+_buf("RI RJ", 256, "int32")
+_buf("RU CU RU2 OU PR", 256, "uint16")
+_buf("FW", 176, "uint16")
+_buf("KT", 256, "float32")
+_buf("w", 768, "float32")
+_buf("c", 256, "float32")
+_buf("ci", 128, "int32")
+_buf("wi", 48, "int32")
+_buf("wb", 64, "bfloat16")
+_buf("u", 160, "uint16")
+_buf("cu", 96, "uint16")
+_buf("MS", 128, "bfloat16")
+_buf("VR", 128, "float32")
+_buf("q", 192, "float32")
+_buf("FG", V, "bfloat16")
+_buf("YF", V, "float32")
+_buf("ME0 ME1 ME2 LE0 LE1 LE2", 136, "float32")
+_buf("ML0 ML1 ML2 LL0 LL1 LL2", 64, "float32")
+_buf("PC PO PE PKC PKO PA PB PW", 512, "float32", "psum")
+
+SEMAPHORES = (["sv", "sa", "sp", "sg", "dx", "dh", "dl", "dt", "ox", "ol", "of", "tx", "rx", "tl", "rl"]
+              + ["%s%d" % (a, t) for a in ("te", "re", "tm", "rm") for t in range(RO - 1)])
+
+
+def S(name, lo=0, hi=None, st=1, p=None):
+    return (name, lo, SCRATCH[name][1][1] if hi is None else hi, st, p)
+
+
+def IND(win, off):
+    return ("*", win, off)
+
+
+def build(g, core, T, topo):
+    rank = T.rank_of(core)
+    n_ranks = len(T.cores)
+    nodes = []
+    eng = {"v": g.vector, "a": g.scalar, "p": g.tensor, "g": g, "s": g.sync}
+
+    def ap(x):
+        if not isinstance(x, tuple):
+            return x
+        if x[0] == "*":
+            return ap(x[1]).indirect(ap(x[2]))
+        ps = slice(None) if x[4] is None else slice(x[4][0], x[4][1])
+        return T[x[0]][ps, x[1]:x[2]:x[3]] if x[3] != 1 else T[x[0]][ps, x[1]:x[2]]
+
+    def cnt(x):
+        if x[0] == "*":
+            return 16 * (x[2][2] - x[2][1])
+        return (x[2] - x[1] + x[3] - 1) // x[3]
+
+    def dty(x):
+        return SCRATCH[x[1][0] if x[0] == "*" else x[0]][2]
+
+    def psum(x):
+        return x[0] != "*" and SCRATCH[x[0]][0] == "psum"
+
+    def node(e, cost, fn, outs, ins, lat=0, sem=None, inc=1, after=()):
+        rd, wr = [], []
+        for x in ins:
+            if isinstance(x, tuple):
+                rd += [x[1], x[2]] if x[0] == "*" else [x]
+        for x in outs:
+            if x[0] == "*":
+                wr.append(x[1])
+                rd.append(x[2])
+            else:
+                wr.append(x)
+        nodes.append(dict(e=e, cost=cost, fn=fn, rd=rd, wr=wr, lat=lat, sem=sem, inc=inc, after=list(after)))
+        return len(nodes) - 1
+
+    def vcost(out, i0, base):
+        n = cnt(out)
+        if out[0] == "*":
+            return 60 + 3.8 * n
+        if i0[0] == "*":
+            return 60 + 1.56 * n
+        return max(64, base * n) + 10
+
+    def narrow(*xs):
+        return 0.5 if all(dty(x) in ("bfloat16", "uint16") for x in xs) else 1.0
+
+    def cp(out, i0):
+        return node("v", vcost(out, i0, narrow(out, i0)), lambda: g.vector.tensor_copy(ap(out), ap(i0)), [out], [i0])
+
+    def tt(out, i0, i1, op):
+        return node("v", vcost(out, i0, 1.0 if psum(i0) or psum(i1) else 2.0),
+                    lambda: g.vector.tensor_tensor(ap(out), ap(i0), ap(i1), op), [out], [i0, i1])
+
+    def ts(out, i0, s1, op0, s2=None, op1=None):
+        if op1 is None:
+            fn = lambda: g.vector.tensor_scalar(ap(out), ap(i0), ap(s1), None, op0)
+        else:
+            fn = lambda: g.vector.tensor_scalar(ap(out), ap(i0), ap(s1), ap(s2), op0, op1)
+        return node("v", vcost(out, i0, narrow(out, i0)), fn, [out], [i0, s1, s2])
+
+    def mset(out, val):
+        return node("v", max(64, cnt(out) * narrow(out)), lambda: g.vector.memset(ap(out), val), [out], [])
+
+    def tr(out, i0):
+        return node("v", cnt(out) + 10, lambda: g.vector.transpose(ap(out), ap(i0)), [out], [i0])
+
+    def act(out, i0, bias=None, scale=None, func=F.Identity):
+        kw = {}
+        if bias is not None:
+            kw["bias"] = bias
+        if scale is not None:
+            kw["scale"] = scale
+        return node("a", vcost(out, i0, 1.0) + 20,
+                    lambda: g.scalar.activation(ap(out), ap(i0), func, **{k: ap(x) for k, x in kw.items()}),
+                    [out], [i0, bias, scale])
+
+    def scat(win, off, src):
+        if ACT_SCATTER:
+            return act(IND(win, off), src, func=F.Silu)
+        return cp(IND(win, off), src)
+
+    def mm(items, start, stop):
+        def fn():
+            r = None
+            for j, (o, l, x) in enumerate(items):
+                r = g.tensor.matmul(ap(o), ap(l), ap(x), start and j == 0, stop and j == len(items) - 1)
+            return r
+        cost = sum(0.6 * max(64, cnt(x)) * (4 if dty(x) == "float32" else 1) for o, l, x in items)
+        return node("p", cost, fn, [o for o, l, x in items], [y for o, l, x in items for y in (l, x)])
+
+    def sel(fam, r):
+        return S(fam, 15 - r, 143 - r)
+
+    def fold(out, fam, src, lo, n, start, stop):
+        return mm([(out, sel(fam, r), S(src, lo + r, lo + r + 16 * (n - 1) + 1, 16)) for r in range(16)], start, stop)
+
+    def iota(out, pat, base, cm=0):
+        if dty(out) == "int32":
+            fn = lambda: g.iota(ap(out), pat, base, cm)
+        else:
+            fn = lambda: g.iota(ap(out), pat, base, cm, allow_small_or_imprecise_dtypes=True)
+        return node("g", 160 + 2 * cnt(out), fn, [out], [])
+
+    def dma(e, out, in_, sem, lat, outs=(), ins=(), **kw):
+        return node(e, 100 if e != "g" else 1200, lambda: eng[e].dma_start(out(), in_(), **kw), list(outs), list(ins), lat=lat, sem=sem, inc=16)
+
+    def exchange(srcs, dsts, tsem, rsem, lat):
+        to = [T.cores[(rank - d) % n_ranks] for d in (1, 2)]
+        es = [e for e in topo.engines(core, to[0]) if e in topo.engines(core, to[1])]
+        h = len(es) // 2
+
+        def fn():
+            trs = []
+            for d in range(2):
+                rid, pid = topo.addr(to[d], core)
+                trs.append(RemoteDMATransfer(dst_ids=[DstId(rid=rid, pnc=pid)], dma_engine_mask=sum(1 << e for e in es[d * h:(d + 1) * h]),
+                                             remote_sem=T.sem[rsem], src=ap(srcs[d]), dst=ap(dsts[d])))
+            g.remote_dma_fused(trs, local_sem=T.sem[tsem])
+            return None
+        k = node("g", 600, fn, [], srcs, lat=lat, sem=tsem, inc=2 * h)
+        node("R", 0, None, dsts, [], lat=lat + 1500, sem=rsem, inc=2 * h, after=[k])
+
+    dma("s", lambda: T.X[:, 0:V], lambda: T.feat[:], "dx", 3500, outs=[S("X", 0, V)])
+    dma("a", lambda: T.HI[:], lambda: T.hits[:], "dh", 4500, outs=[S("HI")])
+    dma("s", lambda: T.wi[:, 32:48], lambda: T.lane0[:], "dl", 2500, outs=[S("wi", 32, 48)])
+    exchange([S("X", 0, GH)] * 2, [S("X", V, V + GH), S("X", V + GH, W)], "tx", "rx", 6000)
+
+    def c(j, n=1):
+        return S("c", j, j + n)
+
+    def ci(j, n=1):
+        return S("ci", j, j + n)
+    ROW, GRP, PAR, PID, G15, M0c, M1c, M4c, WN, WS, WM, W014, WH, THC, R4A, R4B, TMP, TMP2 = [c(j) for j in range(18)]
+    LT, HBI, DUMP, DUMS, DUMS1, D8, CD8, G8, TH8 = c(32, 16), c(48, 16), c(64, 16), c(80, 16), c(96, 16), c(112, 8), c(120, 8), c(128, 8), c(136, 8)
+    T16a, T16b, T16c, I16, I17 = c(144, 16), c(160, 16), c(176, 16), c(192, 16), c(208, 18)
+    OENT, ORET, OSEL, OBC = S("cu", 0, 16), S("cu", 16, 33), S("cu", 48, 64), S("cu", 64, 80)
+    iota(ci(0), [[0, 1]], 0, 1)
+    iota(S("IU"), [[1, 144]], 0)
+    iota(S("I256"), [[1, 256]], 0)
+    iota(S("IG"), [[1, 8], [0, 16]], 0)
+    iota(ci(16, 16), [[1, 16]], 0)
+    ts(ci(1), ci(0), 15, A.bitwise_and)
+    ts(ci(2), ci(0), 4, A.arith_shift_right)
+    ts(ci(3), ci(2), 1, A.bitwise_and)
+    cp(c(0, 3), ci(1, 3))
+    cp(PID, ci(0))
+    ts(G15, GRP, 16.0, A.mult, 15.0, A.add)
+    cp(I16, S("IU", 0, 16))
+    ts(c(224, 8), S("IU", 0, 8), ROW, A.is_equal)
+    mk = lambda j: c(224 + j)
+    ts(TMP, mk(0), 8.0, A.mult)
+    ts(TMP2, mk(1), 1.0 / 32, A.mult, TMP, A.add)
+    ts(WN, mk(4), 4.0, A.mult, TMP2, A.add)
+    ts(WS, mk(2), mk(3), A.add, -128.0, A.mult)
+    tt(WM, WN, WS, A.add)
+    ts(W014, mk(0), mk(1), A.add, mk(4), A.add)
+    tt(WH, mk(2), mk(3), A.subtract)
+    ts(R4A, mk(4), 32.0 * V / 128, A.mult)
+    ts(R4B, mk(4), 32.0 * (V + GH) / 128, A.mult)
+    tt(c(22), WN, WS, A.subtract)
+    for fam, wt in (("SN", WN), ("SY", 4096.0), ("SP", c(22)), ("SA", 8192.0), ("SX", -4096.0), ("SS", WS), ("SM", WM), ("S32", 32.0), ("Z0", mk(0))):
+        ts(S(fam), S("IU"), G15, A.is_equal, wt, A.mult)
+    for m, wt in (("RN", WN), ("BD32", 32.0), ("BDC", -float(2 ** 20)), ("BD1", 1.0)):
+        ts(S(m), S("IG"), GRP, A.is_equal, wt, A.mult)
+    for m, wt in (("IBIG", BIG), ("I1", 1.0), ("IM1", -1.0), ("I24", float(2 ** 24)), ("I014", W014), ("IH", WH)):
+        ts(S(m), S("IU", 0, 128), PID, A.is_equal, wt, A.mult)
+    ts(S("MT"), S("IU", 0, 128), PID, A.is_lt, -1.0, A.mult)
+    tt(S("UP"), S("MT"), S("BD1"), A.mult)
+    ts(S("WBL"), sel("Z0", 1), 32.0, A.mult)
+    ts(S("MT"), sel("Z0", 0), 1.0 / 256, A.mult)
+    tt(S("WBH"), S("MT"), sel("Z0", 1), A.subtract)
+    ts(LT, I16, ROW, A.is_gt)
+    for r in range(16):
+        act(S("TRI", 128 * r, 128 * r + 128), sel("SA", r), scale=c(32 + r))
+    ts(HBI, I16, mk(0), A.mult, 32.0, A.mult)
+    ts(c(21), mk(1), 32.0, A.mult)
+    for h in range(W // 256):
+        act(S("NB", 256 * h, 256 * h + 256), S("I256"), bias=c(48 + h), scale=c(21))
+    mset(S("ONE"), 1.0)
+    act(S("LC"), S("I256"), scale=32.0)
+    for b in ("MV", "MB"):
+        mset(S(b, 256, 272), 128.0)
+    for b in ("MZ", "NL"):
+        mset(S(b, 256, 272), 0.0)
+    mset(S("CR", 0, 16), 0.0)
+    ts(T16a, I16, 16.0, A.mult, ROW, A.add)
+    ts(DUMP, T16a, float(W), A.add)
+    ts(DUMS, T16a, float(LN), A.add)
+    ts(DUMS1, T16a, float(LN + 1), A.add)
+    for j in range(4):
+        ts(c(112 + 2 * j, 2), c(144, 2), float(W - V), A.add)
+    ts(c(120, 4), c(112, 4), -1.0, A.mult)
+    ts(c(124, 4), c(116, 4), -1.0, A.mult, float(GH), A.add)
+    ts(TMP2, ROW, 16.0, A.mult)
+    ts(S("c", 208, 224), I16, TMP2, A.add)
+    cp(S("c", 224 + 8, 224 + 9), TMP2)
+    cp(S("cu", 16, 32), S("c", 208, 224))
+    cp(S("cu", 32, 33), S("c", 232, 233))
+    ts(OBC, I16, 0.0, A.mult, ROW, A.add)
+    ts(ci(32, 16), ci(16, 16), PAR, A.add)
+    ts(ci(48, 16), ci(32, 16), 1, A.bitwise_and)
+    ts(ci(64, 16), ci(16, 16), 15.0, A.add)
+    ts(ci(80, 16), ci(64, 16), 15, A.bitwise_and)
+    tt(T16b, ci(80, 16), ci(16, 16), A.subtract)
+    ts(T16c, T16b, 16.0, A.mult, 256.0, A.add)
+    tt(T16b, T16c, ci(48, 16), A.mult)
+    tt(T16c, T16b, T16a, A.add)
+    cp(OSEL, T16c)
+    ts(T16b, I16, ROW, A.is_equal)
+    tt(S("c", 240, 256), T16b, T16c, A.mult)
+    node("v", 74, lambda: g.vector.tensor_reduce(ap(c(18)), ap(S("c", 240, 256)), AxisListType.X, A.add), [c(18)], [S("c", 240, 256)])
+    tt(c(19), c(18), ROW, A.subtract)
+    ts(OENT, I16, c(19), A.add)
+    dma("g", lambda: T.ci[0:1, 96:104], lambda: T.th[:], "dt", 3000, outs=[ci(96, 8)], allow_slow_non_contiguous=True)
+    node("g", 200, lambda: g.partition_broadcast(T.ci[:, 104:112], T.ci[0:1, 96:104], 128), [ci(104, 8)], [ci(96, 8)])
+    ts(G8, S("IU", 0, 8), GRP, A.is_equal)
+    tt(TH8, ci(104, 8), G8, A.mult)
+    node("v", 74, lambda: g.vector.tensor_reduce(ap(c(20)), ap(TH8), AxisListType.X, A.add), [c(20)], [TH8])
+    ts(THC, c(20), -4095.0, A.add, 4096.0, A.mult)
+    ts(S("wb", 48, 56), G8, WN, A.mult)
+
+    cp(S("L", 0, V), S("HI"))
+    act(S("GA"), S("L", 0, GH), bias=float(GH), scale=-1.0, func=F.Relu)
+    for bank, lo, hi in (("PKC", 0, 512), ("PKO", 512, GH)):
+        mm([(S(bank, 0, hi - lo), S("RN"), S("NB", lo, hi)), (S(bank, 0, hi - lo), S("IBIG"), S("GA", lo, hi))], True, True)
+        tt(S("GB", lo, hi), S(bank, 0, hi - lo), S("L", lo, hi), A.min)
+    cp(S("GL"), S("GB"))
+    exchange([S("GL")] * 2, [S("LG", 0, GH), S("LG", GH, 2 * GH)], "tl", "rl", 6000)
+    act(S("B", V, W), S("NB", V, W), bias=128.0, scale=0.0)
+    for lo in (0, 512):
+        act(S("HB"), S("L", lo, lo + 512), scale=32.0)
+        mm([(S("PA"), S("WBH"), S("HB")), (S("PA"), S("WBL"), S("L", lo, lo + 512))], True, True)
+        act(S("B", lo, lo + 512), S("PA"))
+
+    def pieces(out, names, x, hb, pa, pb):
+        n = cnt(out)
+        mm([(S(pa, 0, n), S("BD32"), x)], True, True)
+        act(hb, S(pa, 0, n), bias=-256.0, func=F.Relu)
+        mm([(S(pb, 0, n), S("I014"), names), (S(pb, 0, n), S("IH"), hb), (S(pb, 0, n), sel("S32", 3), x)], True, True)
+        act(out, S(pb, 0, n))
+
+    for lo in range(0, W, 512):
+        hi = min(lo + 512, W)
+        pieces(S("M0", lo, hi), S("NB", lo, hi), S("X", lo, hi), S("MH", lo, hi), "PC", "PO")
+
+    def w(j):
+        return S("w", 16 * j, 16 * j + 16)
+
+    def u(j, n=16):
+        return S("u", j, j + n)
+    VF, VA, AW, VD, BF, JN, G1, J1, THW, THA, BJ, NJ, OWN, VL, CTW = [w(j) for j in range(15)]
+    t0, t1, t2, t3, t4, t5, t6, t7 = [w(j) for j in range(16, 24)]
+    PU, VU, BU, OL, OJ, OB, BBU, OS, SU, GU = u(0), u(16), u(32), u(48), u(64), u(80), u(96), u(112), u(128, 4), u(136, 8)
+    cp(PU, S("wi", 32, 48))
+
+    def lanes(mwin):
+        act(S("MV", 0, LN), IND(mwin, PU))
+        fold(S("PW", 0, 16), "SN", "MV", 0, 16, True, True)
+        cp(VU, S("PW", 0, 16))
+        cp(VF, S("PW", 0, 16))
+        mm([(S("PA", 0, LN), S("RN"), S("MV", 0, LN))], True, True)
+        cp(S("PR"), S("PA", 0, LN))
+        for s in range(16):
+            ts(S("E", 272 * s, 256 * s + 256), S("PR", 16 * s, 256), S("w", s, s + 1), A.is_equal)
+        mm([(S("PA", 16 * s + 16, LN), S("BD1"), S("E", 272 * s + 16, 256 * s + 256)) for s in range(15)], True, True)
+        act(S("CR", 16, LN), S("PA", 16, LN))
+        fold(S("PW", 16, 32), "SA", "CR", 0, 16, True, False)
+        mm([(S("PW", 16, 32), S("TRI", 128 * r, 128 * r + 128), S("E", r, r + 272 * 15 + 1, 272)) for r in range(1, 16)], False, True)
+        tt(VA, S("PW", 16, 32), VF, A.add)
+        ts(AW, S("PW", 16, 32), 0.0, A.is_equal)
+        act(S("VT"), IND(VF, OBC))
+        act(S("CT"), IND(VF, OBC), bias=CLAMP)
+        tt(VD, VF, DUMP, A.subtract)
+        tt(w(24), VD, AW, A.mult)
+        tt(w(25), w(24), DUMP, A.add)
+        cp(OL, w(25))
+
+    def turn(buf, z):
+        tr(S(z, 0, 256), S(buf, 0, 256))
+        tr(S(z, 256, 512), S(buf, 16, 272))
+
+    def names(t, e, off, lwin, abuf, z, raw, outu, outf, dm, pn, chunks, mcur, each):
+        get = act if e == "a" else cp
+        get(S(abuf, 0, 256), IND(lwin, off))
+        get(S(abuf, 256, 272), IND(lwin, S(off[0], off[1], off[1] + 1)))
+        turn(abuf, z)
+        if t == 0:
+            cp(S(outu), IND(S(z), OENT))
+            act(S(outf), IND(S(z), OENT))
+        else:
+            cp(S(raw), IND(S(z), OENT))
+        k = 0
+        for n in chunks:
+            if t == 0:
+                act(S(dm, 256 * k, 256 * (k + n)), IND(S("X", 0, W), S(outu, 16 * k, 16 * (k + n))))
+            else:
+                act(S(dm, 256 * k, 256 * (k + n)), IND(mcur, S(raw, 16 * k, 16 * (k + n))))
+                fold(S(pn, 16 * k, 16 * (k + n)), "SN", dm, 256 * k, 16 * n, True, True)
+                cp(S(outu, 16 * k, 16 * (k + n)), S(pn, 16 * k, 16 * (k + n)))
+            k += n
+            if k % 4 == 0:
+                each(k // 4 - 1)
+
+    def far(buf, offs, y, j, n):
+        for k in range(4 * j, 4 * j + 4, n):
+            tt(S(buf, 256 * k, 256 * (k + n)), IND(S("X", 0, W), S(offs, 16 * k, 16 * (k + n))), S(y, 0, 256 * n), A.max)
+
+    def over(buf, offs, src, j):
+        lo = 1024 * j
+        if src is None:
+            src, lo = "XC", 1024 * (j % 2)
+            act(S(src, lo, lo + 1024), IND(S("X", 0, W), S(offs, 64 * j, 64 * j + 64)))
+        for h in (0, 512):
+            mm([(S("PE"), S("I1"), S("ZZ", 0, 512)), (S("PE"), S("IM1"), S(src, lo + h, lo + h + 512))], True, True)
+            act(S(buf, 1024 * j + h, 1024 * j + h + 512), S("PE"), func=F.Relu)
+
+    def quarter(bank, fam, src, j, stop=False):
+        fold(S(bank, 64 * j, 64 * j + 64), fam, src, 1024 * j, 64, False, stop)
+
+    def opening(bank):
+        mm([(S(bank, 0, LN), S("BDC"), S("ONE"))], True, False)
+
+    def pen(bank, tiles, stop=False):
+        mm([(S(bank, 0, LN), S("IBIG"), S(x)) for x in tiles], False, stop)
+
+    lanes(S("NB", 0, V))
+    mname = "M0"
+    for t in range(RO):
+        last = t == RO - 1
+        mcur = S("NB") if t == 0 else S(mname, 0, W)
+        cnum = S("CF") if t == 0 else S("PC", 0, LN)
+        onum = S("OF") if t == 0 else S("PO", 0, LN)
+        sfam, mfam, pfam = ("SX", "SX", "SY") if t == 0 else ("SS", "SM", "SP")
+        act(S("XV", 0, LN), IND(S("X", 0, V), VU))
+        act(S("XV", LN, 2 * LN), S("XV", 0, LN))
+        act(S("XM"), S("XV", 0, LN), bias=-0.5)
+        opening("PE")
+
+        def step1(j):
+            quarter("PE", sfam, "DC", j)
+            far("D0", "CU", "XV", j, 2)
+            if j < 3:
+                quarter("PE", "SA", "D0", j)
+        names(t, "a" if OPT[1] else "v", VU, S("L", 0, V), "A1", "Z1", "RU", "CU", "CF", "DC", "PC", [4, 4, 4, 4] if t == 0 else [2, 2, 4, 4, 4], mcur, step1)
+        if t > 0:
+            act(S("CF"), S("PC", 0, LN))
+        tt(S("EQ1"), cnum, S("VT"), A.is_equal)
+        mm([(S("PE", 0, LN), S("I24"), S("EQ1"))], False, False)
+        quarter("PE", "SA", "D0", 3, True)
+        fold(S("PB", 0, 16), "SA", "XV", 0, 16, True, True)
+        ts(THW, S("PB", 0, 16), 0.5, A.mult, THC, A.add)
+        if t > 0:
+            nf = 64 if last else 176
+            for lo in range(0, 16 * nf, 704):
+                act(S("MH", lo, min(lo + 704, 16 * nf)), S(mname, lo, min(lo + 704, 16 * nf)))
+            fold(S("PB", 0, nf), "SN", "MH", 0, nf, True, True)
+            cp(S("FW", 0, 64), S("PB", 0, 64))
+            if nf > 64:
+                ts(S("FW", 64, 176), S("PB", 64, 176), -float(V), A.add)
+        if t == 0:
+            for d in range(2):
+                ts(S("L", V + d * GH, V + (d + 1) * GH), S("LG", d * GH, (d + 1) * GH), float(V + d * GH), A.add)
+        else:
+            for d in range(2):
+                cp(IND(S("L", V, WD), u(136 + 4 * d, 2)), S("LL%d" % (t - 1), 32 * d, 32 * d + 32))
+        tt(S("KEY"), S("PE", 0, LN), S("CF"), A.add)
+        tt(S("KT", 0, 128), S("KEY", 0, 128), S("KEY", 128, 256), A.min)
+        tt(S("KT", 128, 192), S("KT", 0, 64), S("KT", 64, 128), A.min)
+        tt(S("KT", 192, 224), S("KT", 128, 160), S("KT", 160, 192), A.min)
+        tt(S("wi", 0, 16), S("KT", 192, 208), S("KT", 208, 224), A.min)
+        ts(S("wi", 16, 32), S("wi", 0, 16), 4095, A.bitwise_and)
+        cp(BU, S("wi", 16, 32))
+        cp(BF, S("wi", 16, 32))
+        tt(S("ZS"), IND(S("X", 0, W), BU), S("XM"), A.add)
+        if OPT[2]:
+            act(S("ZT"), S("ZS"), bias=MAGIC, scale=0.5)
+            act(S("ZZ", 0, LN), S("ZT"), bias=-MAGIC)
+        else:
+            ts(S("ZT"), S("ZS"), 0.5, A.mult, MAGIC, A.add)
+            ts(S("ZZ", 0, LN), S("ZT"), -MAGIC, A.add)
+        zz = S("ZZ", 0, LN)
+        act(S("ZZ", LN, 2 * LN), S("ZT"), bias=-MAGIC)
+        act(S("ZZ", 2 * LN, 4 * LN), S("ZZ", 0, 2 * LN))
+        act(S("MB", 0, LN), IND(mcur, BU))
+        scat(S("B"), OL, S("MB", 0, LN))
+        act(S("BB"), IND(S("B", 0, W), BU))
+        fold(S("PW", 0, 16), "SN", "BB", 0, 16, True, True)
+        if t > 0:
+            cp(BBU, S("PW", 0, 16))
+            act(S("BK"), IND(mcur, BBU))
+            fold(S("PW", 0, 16), "SN", "BK", 0, 16, True, True)
+        tt(J1, S("PW", 0, 16), VF, A.is_equal)
+        tt(G1, BF, VA, A.is_gt)
+        tt(JN, J1, G1, A.mult)
+        ts(NJ, JN, -1.0, A.mult, 1.0, A.add)
+        ts(t0, JN, BIG, A.mult)
+        tt(THA, t0, THW, A.add)
+        ts(t1, NJ, -8192.0, A.mult)
+        tt(BJ, t1, BF, A.add)
+        tt(t2, BF, DUMP, A.subtract)
+        tt(t4, VD, JN, A.mult)
+        tt(t5, t2, JN, A.mult)
+        tt(t6, t4, DUMP, A.add)
+        tt(t7, t5, DUMP, A.add)
+        cp(u(64, 32), S("w", 16 * 22, 16 * 24))
+        opening("PKC")
+        for j in range(4):
+            if j < 4 - OFF1[t]:
+                far("D1", "CU", "ZZ", j, 4 if j else 1)
+            else:
+                over("D1", "CU", "DC" if t == 0 else None, j)
+            quarter("PKC", "SA", "D1", j)
+            quarter("PKC", mfam if j < 4 - OFF1[t] else pfam, "DC", j)
+        names(t, "a", BU, S("L", 0, W), "A2", "Z2", "RU2", "OU", "OF", "DO", "PO", [4, 4, 4, 4], mcur, lambda j: None)
+        act(S("BJT"), IND(BJ, OBC))
+        tt(t3, THW, t0, A.subtract)
+        tt(S("NJT"), IND(t3, OBC), S("KEY"), A.is_gt)
+        tt(S("UPM"), IND(THA, OBC), S("KEY"), A.is_le)
+        tt(S("EQ2"), cnum, S("BJT"), A.is_equal)
+        tt(S("EQ3"), onum, S("VT"), A.is_equal)
+        tt(S("EQ4"), onum, S("BJT"), A.is_equal)
+        pen("PKC", ["EQ1", "EQ2", "UPM"], True)
+        if t == 0:
+            tt(S("ZS"), S("PKC", 0, LN), S("CF"), A.add)
+            tt(S("KC"), S("ZS"), S("CT"), A.min)
+        else:
+            tt(S("KC"), S("PKC", 0, LN), S("CT"), A.min)
+        opening("PKO")
+        if not last:
+            pieces(S("MZ", 0, LN), S("MV", 0, LN), zz, S("HZ"), "PA", "PB")
+            me, le, ml, ll = "ME%d" % t, "LE%d" % t, "ML%d" % t, "LL%d" % t
+            ts(VL, VF, float(GH), A.is_lt)
+            tl, inc = S("wb", 0, 16), S("wb", 16, 32)
+            tt(tl, JN, VL, A.mult)
+            node("v", 74, lambda: g.vector.tensor_tensor_scan(ap(inc), ap(S("ONE", 0, 16)), ap(tl), 0.0, A.mult, A.add), [inc], [S("ONE", 0, 16), tl])
+            mm([(S("PW", 0, 16), S("BD1"), inc), (S("PW", 0, 16), S("UP"), tl)], True, True)
+            tt(w(26), S("PW", 0, 16), DUMS1, A.subtract)
+            tt(w(27), w(26), tl, A.mult)
+            tt(w(28), w(27), DUMS, A.add)
+            cp(OS, w(28))
+            mset(S("SL", 0, 32), 32.0 * LN)
+            scat(S("SL"), OS, S("LC"))
+            act(S("MS", 0, 32), S("SL", 0, 32))
+            fold(S("PW", 0, 2), "SA", "MS", 0, 2, True, True)
+            ts(u(128, 2), S("PW", 0, 2), 2.0 ** -22, A.mult)
+            ts(u(130, 2), S("PW", 0, 2), 2.0 ** -22, A.mult)
+            s2 = u(128, 2)
+            for j, src in enumerate(("MV", "MB", "MV", "MB")):
+                act(S("MS", 32 * j, 32 * j + 32), IND(S(src), s2))
+            act(S(me, 0, 32), IND(S("ZZ", 0, 272), s2))
+            act(S(me, 104, 136), IND(S("ZZ", 0, 272), s2))
+            act(S(me, 32, 64), IND(S("MZ"), s2), bias=R4A)
+            act(S(me, 72, 104), IND(S("MZ"), s2), bias=R4B)
+            fold(S("PW", 0, 8), "SN", "MS", 0, 8, True, True)
+            ts(S("q", 0, 8), S("PW", 0, 8), float(GH), A.is_lt)
+            tt(S("q", 8, 16), S("PW", 0, 8), CD8, A.add)
+            tt(S("q", 16, 24), S("q", 0, 8), S("q", 8, 16), A.mult)
+            tt(S(me, 64, 72), S("q", 16, 24), D8, A.add)
+            exchange([S(me, 0, 68), S(me, 68, 136)], [S(le, 0, 68), S(le, 68, 136)], "te%d" % t, "re%d" % t, 2500)
+            mm([(S("PW", 0, 32), S("RN"), S("MS", 0, 32))], True, True)
+            act(S("VR", 0, 32), S("PW", 0, 32))
+            act(S("VR", 32, 64), S("PW", 0, 32))
+            act(S("VR", 64, 96), S("PW", 0, 32), bias=float(V))
+            act(S("VR", 96, 128), S("PW", 0, 32), bias=float(V + GH))
+            ct = S("CF", 16 * t, 16 * t + 16)
+            y = [w(j) for j in range(32, 42)]
+            ts(y[0], ct, float(V), A.is_lt)
+            tt(y[1], ct, VF, A.subtract)
+            tt(y[2], y[0], y[1], A.mult)
+            ts(OWN, BF, float(V), A.is_lt)
+            tt(y[3], BF, VF, A.subtract)
+            tt(y[4], y[3], y[2], A.subtract)
+            tt(y[5], y[4], OWN, A.mult)
+            tt(y[6], y[5], y[2], A.add)
+            tt(y[7], AW, JN, A.subtract)
+            tt(y[8], y[6], y[7], A.mult)
+            tt(y[9], y[8], VF, A.add)
+            cp(PU, y[9])
+            scat(S(mname), OJ, S("MZ", 0, LN))
+            scat(S(mname), OB, S("MZ", 0, LN))
+            cp(GU, S(le, 64, 72))
+            for d, lo in ((0, 32), (1, 72)):
+                scat(S(mname, V, WD), u(136 + 4 * d, 2), S(le, lo, lo + 32))
+                scat(S(mname, V, WD), u(138 + 4 * d, 2), S(le, lo, lo + 32))
+        else:
+            act(S("MZ", 0, LN), S("MV", 0, LN))
+            scat(S(mname), OB, S("MZ", 0, LN))
+            act(S("FG"), IND(S(mname, 0, V), S("FW", 0, 64)))
+            for h, bank in enumerate(("PA", "PB")):
+                mm([(S(bank, 0, 512, 1, (0, 8)), S("wb", 48, 56), S("FG", 512 * h, 512 * h + 512))], True, True)
+                act(S("YF", 512 * h, 512 * h + 512, 1, (0, 8)), S(bank, 0, 512, 1, (0, 8)))
+            dma("s", lambda: T.yf[:], lambda: T.YF[0:8, :], "of", 2500, ins=[S("YF")])
+        for j in range(4):
+            if j >= OFF2[t]:
+                far("D2", "OU", "ZZ", j, 4)
+            else:
+                over("D2", "OU", "DO" if t == 0 else None, j)
+            if j == 3:
+                pen("PKO", ["EQ3", "EQ4", "NJT"])
+            quarter("PKO", "SA", "D2", j)
+            quarter("PKO", mfam if j >= OFF2[t] else pfam, "DO", j, j == 3)
+        if t == 0:
+            tt(S("ZS"), S("PKO", 0, LN), S("OF"), A.add)
+            tt(S("RI"), S("ZS"), S("KC"), A.min)
+        else:
+            tt(S("RI"), S("PKO", 0, LN), S("KC"), A.min)
+        ts(S("RJ"), S("RI"), 4095, A.bitwise_and)
+        cp(S("Y"), IND(S("RJ"), ORET))
+        turn("Y", "Z1")
+        (act if OPT[0] else cp)(S("NL", 0, LN), IND(S("Z1"), OSEL))
+        cp(IND(S("L"), OL), S("NL", 0, LN))
+        cp(IND(S("X"), OJ), zz)
+        if last:
+            break
+        for d, lo in ((0, 0), (1, 104)):
+            cp(IND(S("X", V, WD), u(136 + 4 * d, 2)), S(le, lo, lo + 32))
+        ts(S("q", 0, 64), IND(S("NL"), SU), float(GH), A.is_lt)
+        tt(S("q", 64, 128), IND(S("NL"), SU), S("VR", 0, 64), A.subtract)
+        tt(S("q", 128, 192), S("q", 0, 64), S("q", 64, 128), A.mult)
+        tt(S(ml), S("q", 128, 192), S("VR", 64, 128), A.add)
+        exchange([S(ml, 0, 32), S(ml, 32, 64)], [S(ll, 0, 32), S(ll, 32, 64)], "tm%d" % t, "rm%d" % t, 2500)
+        lanes(S(mname, 0, V))
+        if t > 0:
+            nxt = "M1" if mname == "M0" else "M0"
+            act(S(nxt, 0, V), IND(S(mname, 0, V), S("FW", 0, 64)))
+            act(S(nxt, V, W), IND(S(mname, V, W), S("FW", 64, 176)))
+            mname = nxt
+    dma("s", lambda: T.yl[:], lambda: T.L[:, 0:V], "ol", 4000, ins=[S("L", 0, V)])
+    dma("a", lambda: T.yx[:], lambda: T.X[:, 0:V], "ox", 3000, ins=[S("X", 0, V)])
+    return nodes, eng
+
+
+def order(nodes):
+    n = len(nodes)
+    hist = {}
+    deps = []
+    for i, x in enumerate(nodes):
+        d = {}
+        acc = [(y, False) for y in x["rd"]] + [(y, True) for y in x["wr"]]
+        for y, wr in acc:
+            bank = SCRATCH[y[0]][0] == "psum"
+            for (j, lo, hi, w2) in hist.get(y[0], ()):
+                meet = lo < y[2] and y[1] < hi
+                if SCRATCH[y[0]][0] == "sbuf" and (nodes[j]["sem"] or x["sem"]) and wr and w2:
+                    meet = lo - 8 < y[2] and y[1] - 8 < hi
+                if bank and (nodes[j]["e"] != x["e"] or wr or w2):
+                    d[j] = d.get(j, False) or (w2 and not wr and meet)
+                elif meet and (wr or w2):
+                    d[j] = True
+        for y, wr in acc:
+            h = hist.setdefault(y[0], [])
+            if SCRATCH[y[0]][0] == "psum":
+                h[:] = [z for z in h if z[0] == i or (not wr and (z[3] or nodes[z[0]]["e"] == x["e"]))]
+            elif wr and y[3] == 1 and y[4] is None:
+                h[:] = [z for z in h if z[0] == i or not (y[1] <= z[1] and z[2] <= y[2])]
+            h.append((i, y[1], y[2], wr))
+        d.pop(i, None)
+        deps.append(d)
+    pre = [[] for _ in range(n)]
+    suc = [[] for _ in range(n)]
+    for i in range(n):
+        for j in set(list(deps[i]) + nodes[i]["after"]):
+            same = nodes[i]["e"] == nodes[j]["e"] and not deps[i].get(j, False)
+            dl = nodes[j]["lat"] + (0.0 if same else HOP)
+            pre[i].append((j, dl))
+            suc[j].append((i, dl))
+    cost = [max(1.0, x["cost"]) for x in nodes]
+
+    def place(lst, before, tail):
+        at = [0.0] * n
+        busy = {}
+        for k in lst:
+            st = max([at[j] + cost[j] + dl for j, dl in before[k]] + [tail[k]])
+            b = busy.setdefault(nodes[k]["e"], [])
+            lo, hi = 0, len(b)
+            while lo < hi:
+                mid = (lo + hi) // 2
+                if b[mid][1] <= st:
+                    lo = mid + 1
+                else:
+                    hi = mid
+            while lo < len(b) and b[lo][0] < st + cost[k]:
+                st = max(st, b[lo][1])
+                lo += 1
+            b.insert(lo, (st, st + cost[k]))
+            at[k] = st
+        return at
+    prio = [0.0] * n
+    for i in range(n - 1, -1, -1):
+        prio[i] = cost[i] + max([prio[k] + dl for k, dl in suc[i]] + [nodes[i]["lat"]])
+    lst = sorted(range(n), key=lambda i: -prio[i])
+    best = None
+    for it in range(PASSES):
+        at = place(lst, pre, [0.0] * n)
+        end = max(at[i] + cost[i] + nodes[i]["lat"] for i in range(n))
+        if best is None or end < best[0]:
+            best = (end, at)
+        back = place(sorted(range(n), key=lambda i: -at[i] - cost[i]), suc, [x["lat"] for x in nodes])
+        lst = sorted(range(n), key=lambda i: -back[i] - cost[i])
+    times = best[1]
+    return deps, sorted(range(n), key=lambda i: times[i]), times
+
+
+def rank_program(g, core, T, topo):
+    if T.rank_of(core) is None:
+        return
+    nodes, eng = build(g, core, T, topo)
+    if not PLAN:
+        PLAN.append(order(nodes))
+    deps, seq, times = PLAN[0]
+    qsem = {"v": "sv", "a": "sa", "p": "sp", "g": "sg"}
+    pos = {k: j for j, k in enumerate(seq)}
+    know = {e: {} for e in "vapgs"}
+    snap = {}
+    waits = {}
+    for k in seq:
+        x = nodes[k]
+        e = x["e"]
+        if e == "R":
+            snap[k] = {}
+            continue
+        need = []
+        for j, hard in sorted(deps[k].items(), key=lambda z: -pos[z[0]]):
+            y = nodes[j]
+            if y["e"] == e and not hard:
+                continue
+            key = y["sem"] or y["e"]
+            if know[e].get(key, -1) >= pos[j]:
+                continue
+            need.append(j)
+            know[e][key] = pos[j]
+            for a, b in snap[j].items():
+                if know[e].get(a, -1) < b:
+                    know[e][a] = b
+        waits[k] = need
+        snap[k] = dict(know[e])
+    marked = set(j for k in waits for j in waits[k])
+    lastof = {}
+    for k in seq:
+        if not nodes[k]["sem"]:
+            lastof[nodes[k]["e"]] = k
+    marked |= set(lastof.values())
+    count = {}
+    val = {}
+    for k in seq:
+        x = nodes[k]
+        if x["sem"]:
+            val[k] = (x["sem"], x["inc"])
+        elif k in marked:
+            count[x["e"]] = count.get(x["e"], 0) + 1
+            val[k] = (qsem[x["e"]], count[x["e"]])
+    for k in seq:
+        x = nodes[k]
+        if x["e"] == "R":
+            continue
+        for j in waits[k]:
+            eng[x["e"]].wait_ge(T.sem[val[j][0]], val[j][1])
+        r = x["fn"]()
+        if r is not None and k in val:
+            r.then_inc(T.sem[val[k][0]], 16 if x["sem"] else 1)
+    for k in seq:
+        if nodes[k]["sem"] or k in lastof.values():
+            g.wait_ge(T.sem[val[k][0]], val[k][1])

@@ -7,9 +7,10 @@ BIG = float(2 ** 26)
 CLAMP = float(4080 * 4096)
 MAGIC = float(3 * 2 ** 22)
 ACT_SCATTER = True
-OPT = [0, 0, 0]
-OFF1, OFF2 = [1, 1, 1, 1], [0, 0, 0, 0]
-HOP, PASSES = 150.0, 12
+OPT = [0, 0, 0, 0, 1]
+CH = [2, 2, 4, 4, 4]
+OFF1, OFF2 = [2, 1, 1, 1], [0, 0, 0, 0]
+HOP, PASSES, AMP, SPAN = 150.0, 4000, 1000.0, 9000.0
 PLAN = []
 
 SCRATCH = {}
@@ -31,10 +32,11 @@ _buf("LG", 2 * GH, "uint16")
 _buf("DC DO D0 D1 D2 E", 4096, "bfloat16")
 _buf("TRI XC", 2048, "bfloat16")
 _buf("HB", 512, "bfloat16")
-_buf("SA SY SP SX SN SS SM S32", 144, "bfloat16")
+_buf("SA SY SP SX SN SQ SM S32", 144, "bfloat16")
 _buf("Z0 IU", 144, "float32")
 _buf("RN BD32 BDC BD1 IBIG I24 I1 IM1 I014 IH WBH UP", 128, "bfloat16")
-_buf("WBL IG MT", 128, "float32")
+_buf("WBL IG MT I1F", 128, "float32")
+_buf("CS", 256, "float32")
 _buf("A1 A2 Y NL MB MZ", 272, "float32")
 _buf("Z1 Z2 SL", 512, "float32")
 _buf("MV", 272, "bfloat16")
@@ -58,7 +60,7 @@ _buf("VR", 128, "float32")
 _buf("q", 192, "float32")
 _buf("FG", V, "bfloat16")
 _buf("YF", V, "float32")
-_buf("ME0 ME1 ME2 LE0 LE1 LE2", 136, "float32")
+_buf("ME0 ME1 ME2 LE0 LE1 LE2", 200, "float32")
 _buf("ML0 ML1 ML2 LL0 LL1 LL2", 64, "float32")
 _buf("PC PO PE PKC PKO PA PB PW", 512, "float32", "psum")
 
@@ -238,11 +240,12 @@ def build(g, core, T, topo):
     ts(R4A, mk(4), 32.0 * V / 128, A.mult)
     ts(R4B, mk(4), 32.0 * (V + GH) / 128, A.mult)
     tt(c(22), WN, WS, A.subtract)
-    for fam, wt in (("SN", WN), ("SY", 4096.0), ("SP", c(22)), ("SA", 8192.0), ("SX", -4096.0), ("SS", WS), ("SM", WM), ("S32", 32.0), ("Z0", mk(0))):
+    ts(c(23), WS, -2.0, A.mult)
+    for fam, wt in (("SN", WN), ("SQ", c(23)), ("SY", 4096.0), ("SP", c(22)), ("SA", 8192.0), ("SX", -4096.0), ("SM", WM), ("S32", 32.0), ("Z0", mk(0))):
         ts(S(fam), S("IU"), G15, A.is_equal, wt, A.mult)
     for m, wt in (("RN", WN), ("BD32", 32.0), ("BDC", -float(2 ** 20)), ("BD1", 1.0)):
         ts(S(m), S("IG"), GRP, A.is_equal, wt, A.mult)
-    for m, wt in (("IBIG", BIG), ("I1", 1.0), ("IM1", -1.0), ("I24", float(2 ** 24)), ("I014", W014), ("IH", WH)):
+    for m, wt in (("IBIG", BIG), ("I1", 1.0), ("I1F", 1.0), ("IM1", -1.0), ("I24", float(2 ** 24)), ("I014", W014), ("IH", WH)):
         ts(S(m), S("IU", 0, 128), PID, A.is_equal, wt, A.mult)
     ts(S("MT"), S("IU", 0, 128), PID, A.is_lt, -1.0, A.mult)
     tt(S("UP"), S("MT"), S("BD1"), A.mult)
@@ -267,8 +270,8 @@ def build(g, core, T, topo):
     ts(DUMP, T16a, float(W), A.add)
     ts(DUMS, T16a, float(LN), A.add)
     ts(DUMS1, T16a, float(LN + 1), A.add)
-    for j in range(4):
-        ts(c(112 + 2 * j, 2), c(144, 2), float(W - V), A.add)
+    for j in range(2):
+        ts(c(112 + 4 * j, 4), c(144, 4), float(W - V), A.add)
     ts(c(120, 4), c(112, 4), -1.0, A.mult)
     ts(c(124, 4), c(116, 4), -1.0, A.mult, float(GH), A.add)
     ts(TMP2, ROW, 16.0, A.mult)
@@ -374,7 +377,7 @@ def build(g, core, T, topo):
             if t == 0:
                 act(S(dm, 256 * k, 256 * (k + n)), IND(S("X", 0, W), S(outu, 16 * k, 16 * (k + n))))
             else:
-                act(S(dm, 256 * k, 256 * (k + n)), IND(mcur, S(raw, 16 * k, 16 * (k + n))))
+                (cp if k == 0 and OPT[4] and dm == "DC" else act)(S(dm, 256 * k, 256 * (k + n)), IND(mcur, S(raw, 16 * k, 16 * (k + n))))
                 fold(S(pn, 16 * k, 16 * (k + n)), "SN", dm, 256 * k, 16 * n, True, True)
                 cp(S(outu, 16 * k, 16 * (k + n)), S(pn, 16 * k, 16 * (k + n)))
             k += n
@@ -417,16 +420,20 @@ def build(g, core, T, topo):
         opening("PE")
 
         def step1(j):
-            quarter("PE", sfam, "DC", j)
+            if j == 0 and t == 0:
+                mm([(S("PKO", 0, LN), S("I1F"), S("CF"))], True, False)
+            fold(S("PKO", 64 * j, 64 * j + 64), mfam, "DC", 1024 * j, 64, t > 0, t > 0 or j == 3)
             far("D0", "CU", "XV", j, 2)
             if j < 3:
                 quarter("PE", "SA", "D0", j)
-        names(t, "a" if OPT[1] else "v", VU, S("L", 0, V), "A1", "Z1", "RU", "CU", "CF", "DC", "PC", [4, 4, 4, 4] if t == 0 else [2, 2, 4, 4, 4], mcur, step1)
-        if t > 0:
-            act(S("CF"), S("PC", 0, LN))
+        names(t, "a" if OPT[1] else "v", VU, S("L", 0, V), "A1", "Z1", "RU", "CU", "CF", "DC", "PC", [4, 4, 4, 4] if t == 0 else CH, mcur, step1)
+        act(S("CS"), S("PKO", 0, LN))
+        if t > 0 and not last:
+            act(S("CF", 16 * t, 16 * t + 16), S("PC", 16 * t, 16 * t + 16))
         tt(S("EQ1"), cnum, S("VT"), A.is_equal)
-        mm([(S("PE", 0, LN), S("I24"), S("EQ1"))], False, False)
-        quarter("PE", "SA", "D0", 3, True)
+        mm([(S("PE", 0, 192), S("I24"), S("EQ1", 0, 192))], False, True)
+        mm([(S("PKC", 0, 64), S("BDC"), S("ONE", 0, 64)), (S("PKC", 0, 64), S("I24"), S("EQ1", 192, 256))], True, False)
+        fold(S("PKC", 0, 64), "SA", "D0", 3072, 64, False, True)
         fold(S("PB", 0, 16), "SA", "XV", 0, 16, True, True)
         ts(THW, S("PB", 0, 16), 0.5, A.mult, THC, A.add)
         if t > 0:
@@ -443,9 +450,11 @@ def build(g, core, T, topo):
         else:
             for d in range(2):
                 cp(IND(S("L", V, WD), u(136 + 4 * d, 2)), S("LL%d" % (t - 1), 32 * d, 32 * d + 32))
-        tt(S("KEY"), S("PE", 0, LN), S("CF"), A.add)
-        tt(S("KT", 0, 128), S("KEY", 0, 128), S("KEY", 128, 256), A.min)
-        tt(S("KT", 128, 192), S("KT", 0, 64), S("KT", 64, 128), A.min)
+        tt(S("KEY", 0, 192), S("PE", 0, 192), S("CS", 0, 192), A.add)
+        tt(S("KT", 0, 64), S("KEY", 0, 64), S("KEY", 64, 128), A.min)
+        tt(S("KT", 64, 128), S("KT", 0, 64), S("KEY", 128, 192), A.min)
+        tt(S("KEY", 192, 256), S("PKC", 0, 64), S("CS", 192, 256), A.add)
+        tt(S("KT", 128, 192), S("KT", 64, 128), S("KEY", 192, 256), A.min)
         tt(S("KT", 192, 224), S("KT", 128, 160), S("KT", 160, 192), A.min)
         tt(S("wi", 0, 16), S("KT", 192, 208), S("KT", 208, 224), A.min)
         ts(S("wi", 16, 32), S("wi", 0, 16), 4095, A.bitwise_and)
@@ -490,7 +499,8 @@ def build(g, core, T, topo):
             else:
                 over("D1", "CU", "DC" if t == 0 else None, j)
             quarter("PKC", "SA", "D1", j)
-            quarter("PKC", mfam if j < 4 - OFF1[t] else pfam, "DC", j)
+            if j >= 4 - OFF1[t]:
+                quarter("PKC", "SA" if t == 0 else "SQ", "DC", j)
         names(t, "a", BU, S("L", 0, W), "A2", "Z2", "RU2", "OU", "OF", "DO", "PO", [4, 4, 4, 4], mcur, lambda j: None)
         act(S("BJT"), IND(BJ, OBC))
         tt(t3, THW, t0, A.subtract)
@@ -500,11 +510,8 @@ def build(g, core, T, topo):
         tt(S("EQ3"), onum, S("VT"), A.is_equal)
         tt(S("EQ4"), onum, S("BJT"), A.is_equal)
         pen("PKC", ["EQ1", "EQ2", "UPM"], True)
-        if t == 0:
-            tt(S("ZS"), S("PKC", 0, LN), S("CF"), A.add)
-            tt(S("KC"), S("ZS"), S("CT"), A.min)
-        else:
-            tt(S("KC"), S("PKC", 0, LN), S("CT"), A.min)
+        tt(S("ZS"), S("PKC", 0, LN), S("CS"), A.add)
+        tt(S("KC"), S("ZS"), S("CT"), A.min)
         opening("PKO")
         if not last:
             pieces(S("MZ", 0, LN), S("MV", 0, LN), zz, S("HZ"), "PA", "PB")
@@ -528,15 +535,15 @@ def build(g, core, T, topo):
             for j, src in enumerate(("MV", "MB", "MV", "MB")):
                 act(S("MS", 32 * j, 32 * j + 32), IND(S(src), s2))
             act(S(me, 0, 32), IND(S("ZZ", 0, 272), s2))
-            act(S(me, 104, 136), IND(S("ZZ", 0, 272), s2))
-            act(S(me, 32, 64), IND(S("MZ"), s2), bias=R4A)
-            act(S(me, 72, 104), IND(S("MZ"), s2), bias=R4B)
+            act(S(me, 168, 200), IND(S("ZZ", 0, 272), s2))
+            act(S(me, 32, 96), IND(S("MZ"), SU), bias=R4A)
+            act(S(me, 104, 168), IND(S("MZ"), SU), bias=R4B)
             fold(S("PW", 0, 8), "SN", "MS", 0, 8, True, True)
             ts(S("q", 0, 8), S("PW", 0, 8), float(GH), A.is_lt)
             tt(S("q", 8, 16), S("PW", 0, 8), CD8, A.add)
             tt(S("q", 16, 24), S("q", 0, 8), S("q", 8, 16), A.mult)
-            tt(S(me, 64, 72), S("q", 16, 24), D8, A.add)
-            exchange([S(me, 0, 68), S(me, 68, 136)], [S(le, 0, 68), S(le, 68, 136)], "te%d" % t, "re%d" % t, 2500)
+            tt(S(me, 96, 104), S("q", 16, 24), D8, A.add)
+            exchange([S(me, 0, 100), S(me, 100, 200)], [S(le, 0, 100), S(le, 100, 200)], "te%d" % t, "re%d" % t, 2500)
             mm([(S("PW", 0, 32), S("RN"), S("MS", 0, 32))], True, True)
             act(S("VR", 0, 32), S("PW", 0, 32))
             act(S("VR", 32, 64), S("PW", 0, 32))
@@ -558,10 +565,9 @@ def build(g, core, T, topo):
             cp(PU, y[9])
             scat(S(mname), OJ, S("MZ", 0, LN))
             scat(S(mname), OB, S("MZ", 0, LN))
-            cp(GU, S(le, 64, 72))
-            for d, lo in ((0, 32), (1, 72)):
-                scat(S(mname, V, WD), u(136 + 4 * d, 2), S(le, lo, lo + 32))
-                scat(S(mname, V, WD), u(138 + 4 * d, 2), S(le, lo, lo + 32))
+            cp(GU, S(le, 96, 104))
+            for d, lo in ((0, 32), (1, 104)):
+                scat(S(mname, V, WD), u(136 + 4 * d, 4), S(le, lo, lo + 64))
         else:
             act(S("MZ", 0, LN), S("MV", 0, LN))
             scat(S(mname), OB, S("MZ", 0, LN))
@@ -575,16 +581,24 @@ def build(g, core, T, topo):
                 far("D2", "OU", "ZZ", j, 4)
             else:
                 over("D2", "OU", "DO" if t == 0 else None, j)
-            if j == 3:
-                pen("PKO", ["EQ3", "EQ4", "NJT"])
-            quarter("PKO", "SA", "D2", j)
-            quarter("PKO", mfam if j >= OFF2[t] else pfam, "DO", j, j == 3)
+            if j < 3:
+                quarter("PKO", "SA", "D2", j)
+                quarter("PKO", mfam if j >= OFF2[t] else pfam, "DO", j)
+        mm([(S("PKO", 0, 192), S("IBIG"), S(x, 0, 192)) for x in ("EQ3", "EQ4", "NJT")], False, True)
         if t == 0:
-            tt(S("ZS"), S("PKO", 0, LN), S("OF"), A.add)
-            tt(S("RI"), S("ZS"), S("KC"), A.min)
+            tt(S("ZS", 0, 192), S("PKO", 0, 192), S("OF", 0, 192), A.add)
+            tt(S("RI", 0, 192), S("ZS", 0, 192), S("KC", 0, 192), A.min)
+            mm([(S("PO", 0, 64), S("I1F"), S("OF", 192, 256))], True, False)
         else:
-            tt(S("RI"), S("PKO", 0, LN), S("KC"), A.min)
-        ts(S("RJ"), S("RI"), 4095, A.bitwise_and)
+            tt(S("RI", 0, 192), S("PKO", 0, 192), S("KC", 0, 192), A.min)
+        ts(S("RJ", 0, 192), S("RI", 0, 192), 4095, A.bitwise_and)
+        fold(S("PO", 0, 64), mfam, "DO", 3072, 64, t > 0, True)
+        act(S("KT", 0, 64), S("PO", 0, 64))
+        mm([(S("PC", 0, 64), S("BDC"), S("ONE", 0, 64))] + [(S("PC", 0, 64), S("IBIG"), S(x, 192, 256)) for x in ("EQ3", "EQ4", "NJT")], True, False)
+        fold(S("PC", 0, 64), "SA", "D2", 3072, 64, False, True)
+        tt(S("KT", 64, 128), S("PC", 0, 64), S("KT", 0, 64), A.add)
+        tt(S("RI", 192, 256), S("KT", 64, 128), S("KC", 192, 256), A.min)
+        ts(S("RJ", 192, 256), S("RI", 192, 256), 4095, A.bitwise_and)
         cp(S("Y"), IND(S("RJ"), ORET))
         turn("Y", "Z1")
         (act if OPT[0] else cp)(S("NL", 0, LN), IND(S("Z1"), OSEL))
@@ -592,7 +606,7 @@ def build(g, core, T, topo):
         cp(IND(S("X"), OJ), zz)
         if last:
             break
-        for d, lo in ((0, 0), (1, 104)):
+        for d, lo in ((0, 0), (1, 168)):
             cp(IND(S("X", V, WD), u(136 + 4 * d, 2)), S(le, lo, lo + 32))
         ts(S("q", 0, 64), IND(S("NL"), SU), float(GH), A.is_lt)
         tt(S("q", 64, 128), IND(S("NL"), SU), S("VR", 0, 64), A.subtract)
@@ -603,7 +617,8 @@ def build(g, core, T, topo):
         if t > 0:
             nxt = "M1" if mname == "M0" else "M0"
             act(S(nxt, 0, V), IND(S(mname, 0, V), S("FW", 0, 64)))
-            act(S(nxt, V, W), IND(S(mname, V, W), S("FW", 64, 176)))
+            act(S(nxt, V, V + GH), IND(S(mname, V, W), S("FW", 64, 120)))
+            (cp if OPT[3] else act)(S(nxt, V + GH, W), IND(S(mname, V, W), S("FW", 120, 176)))
             mname = nxt
     dma("s", lambda: T.yl[:], lambda: T.L[:, 0:V], "ol", 4000, ins=[S("L", 0, V)])
     dma("a", lambda: T.yx[:], lambda: T.X[:, 0:V], "ox", 3000, ins=[S("X", 0, V)])
@@ -670,11 +685,28 @@ def order(nodes):
         prio[i] = cost[i] + max([prio[k] + dl for k, dl in suc[i]] + [nodes[i]["lat"]])
     lst = sorted(range(n), key=lambda i: -prio[i])
     best = None
+    rnd = [12345]
+
+    def shaken(at, amp):
+        key = [0.0] * n
+        rnd[0] = (rnd[0] * 1103515245 + 12345) % 2147483648
+        mid = best[0] * (rnd[0] / 2147483648.0)
+        amp = amp * (1 + rnd[0] // 1024 % 4)
+        for i in range(n):
+            x = at[i]
+            if abs(x - mid) < SPAN:
+                rnd[0] = (rnd[0] * 1103515245 + 12345) % 2147483648
+                x += amp * (rnd[0] / 2147483648.0 - 0.5)
+            key[i] = max([x] + [key[j] + 1.0 for j, dl in pre[i]])
+        return sorted(range(n), key=lambda i: key[i])
     for it in range(PASSES):
         at = place(lst, pre, [0.0] * n)
         end = max(at[i] + cost[i] + nodes[i]["lat"] for i in range(n))
-        if best is None or end < best[0]:
+        if best is None or end <= best[0]:
             best = (end, at)
+        if it % 2 == 1:
+            lst = shaken(best[1], AMP)
+            continue
         back = place(sorted(range(n), key=lambda i: -at[i] - cost[i]), suc, [x["lat"] for x in nodes])
         lst = sorted(range(n), key=lambda i: -back[i] - cost[i])
     times = best[1]

@@ -2,15 +2,19 @@ from concourse.bass import DstId, RemoteDMATransfer
 from concourse.mybir import AluOpType as A, AxisListType, ActivationFunctionType as F
 
 V, GH, W, LN, RO = 1024, 896, 2816, 256, 4
-WD = W + LN
+WD = W + LN + 128
 BIG = float(2 ** 26)
 CLAMP = float(4080 * 4096)
 MAGIC = float(3 * 2 ** 22)
-ACT_SCATTER = True
-OPT = [0, 0, 0, 0, 1]
-CH = [2, 2, 4, 4, 4]
-OFF1, OFF2 = [2, 1, 1, 1], [0, 0, 0, 0]
-HOP, PASSES, AMP, SPAN = 150.0, 4000, 1000.0, 9000.0
+NX = 4
+SUB = [(), (1,), (1,), (1,)]
+RELU = (1,)
+OPT = dict(z="v", kt="a", vf="a")
+CH0 = [[(4, "v"), (4, "a"), (4, "a"), (4, "a")], [(4, "a")] * 4]
+CH = [[(4, "v"), (4, "a"), (8, "a")], [(8, "a"), (8, "a")]]
+CO = [[(8, "a"), (8, "a")], [(8, "a"), (8, "a")]]
+OFF1, OFF2 = (3,), ()
+HOP, PEC, PASSES, AMP, SPAN = 150.0, 0.55, 4000, 1000.0, 9000.0
 PLAN = []
 
 SCRATCH = {}
@@ -22,49 +26,51 @@ def _buf(names, n, dtp, where="sbuf"):
 
 
 _buf("X", WD, "bfloat16")
-_buf("NB MH", W, "bfloat16")
-_buf("L B M0 M1", WD, "float32")
+_buf("NB", W, "bfloat16")
+_buf("MH ZZ XV", V, "bfloat16")
+_buf("L M B", WD, "float32")
 _buf("HI", V, "int32")
 _buf("GA", GH, "bfloat16")
 _buf("GB", GH, "float32")
 _buf("GL", GH, "uint16")
 _buf("LG", 2 * GH, "uint16")
-_buf("DC DO D0 D1 D2 E", 4096, "bfloat16")
-_buf("TRI XC", 2048, "bfloat16")
-_buf("HB", 512, "bfloat16")
-_buf("SA SY SP SX SN SQ SM S32", 144, "bfloat16")
+_buf("LM", 2 * GH, "bfloat16")
+_buf("DC DO D0 D1 D2 E XC", 4096, "bfloat16")
+_buf("ROWS", 2048, "bfloat16")
+_buf("HB EU EO PN ONE", 512, "bfloat16")
+_buf("SA SX SN SM SP S32 WG", 144, "bfloat16")
 _buf("Z0 IU", 144, "float32")
-_buf("RN BD32 BDC BD1 IBIG I24 I1 IM1 I014 IH WBH UP", 128, "bfloat16")
+_buf("RN BD32 BDC BD1 IBIG I24 I1 IM1 I014 IH WBH I13 IM13 BDW BDB BJM IMG IMH", 128, "bfloat16")
 _buf("WBL IG MT I1F", 128, "float32")
-_buf("CS", 256, "float32")
-_buf("A1 A2 Y NL MB MZ", 272, "float32")
-_buf("Z1 Z2 SL", 512, "float32")
+_buf("BJ", 384, "bfloat16")
+_buf("NL MB MZ", 272, "float32")
+_buf("A1 A2 FG", 320, "float32")
+_buf("Z", 576, "float32")
 _buf("MV", 272, "bfloat16")
-_buf("ZZ", 1024, "bfloat16")
-_buf("XV", 512, "bfloat16")
-_buf("CF OF KEY KC VT CT BJT XM ZS ZT LC", 256, "float32")
-_buf("HZ ONE I256 CR EQ1 EQ2 EQ3 EQ4 UPM NJT BB BK", 256, "bfloat16")
+_buf("CF KC VT CL ZS ZT RF", 256, "float32")
+_buf("RZ PW2 I256 CR EQ BB BK BY TH MC NN CN SG", 256, "bfloat16")
 _buf("RI RJ", 256, "int32")
 _buf("RU CU RU2 OU PR", 256, "uint16")
-_buf("FW", 176, "uint16")
-_buf("KT", 256, "float32")
+_buf("FW", 64, "uint16")
+_buf("fw", 160, "uint16")
+_buf("KT", 448, "float32")
 _buf("w", 768, "float32")
 _buf("c", 256, "float32")
 _buf("ci", 128, "int32")
 _buf("wi", 48, "int32")
-_buf("wb", 64, "bfloat16")
-_buf("u", 160, "uint16")
-_buf("cu", 96, "uint16")
+_buf("wb", 32, "bfloat16")
+_buf("u", 128, "uint16")
+_buf("cu", 32, "uint16")
 _buf("MS", 128, "bfloat16")
-_buf("VR", 128, "float32")
-_buf("q", 192, "float32")
-_buf("FG", V, "bfloat16")
+_buf("VR", 32, "float32")
+_buf("q", 200, "float32")
 _buf("YF", V, "float32")
 _buf("ME0 ME1 ME2 LE0 LE1 LE2", 200, "float32")
-_buf("ML0 ML1 ML2 LL0 LL1 LL2", 64, "float32")
-_buf("PC PO PE PKC PKO PA PB PW", 512, "float32", "psum")
+_buf("ML0 ML1 ML2", 32, "float32")
+_buf("LL0 LL1 LL2", 64, "float32")
+_buf("PC K0 UE UX KK0 KK1 PA PW", 512, "float32", "psum")
 
-SEMAPHORES = (["sv", "sa", "sp", "sg", "dx", "dh", "dl", "dt", "ox", "ol", "of", "tx", "rx", "tl", "rl"]
+SEMAPHORES = (["sv", "sa", "sp", "sg", "dx", "dn", "dm", "dh", "dl", "dt", "ox", "ol", "of", "tx", "rx", "tl", "rl", "tp", "rp"]
               + ["%s%d" % (a, t) for a in ("te", "re", "tm", "rm") for t in range(RO - 1)])
 
 
@@ -140,26 +146,32 @@ def build(g, core, T, topo):
             fn = lambda: g.vector.tensor_scalar(ap(out), ap(i0), ap(s1), ap(s2), op0, op1)
         return node("v", vcost(out, i0, narrow(out, i0)), fn, [out], [i0, s1, s2])
 
+    def scan(out, d0, d1, first, op0, op1):
+        return node("v", vcost(out, d1, 1.0), lambda: g.vector.tensor_tensor_scan(ap(out), ap(d0), ap(d1), first, op0, op1), [out], [d0, d1])
+
+    def total(out, i0):
+        return node("v", 74, lambda: g.vector.tensor_reduce(ap(out), ap(i0), AxisListType.X, A.add), [out], [i0])
+
     def mset(out, val):
         return node("v", max(64, cnt(out) * narrow(out)), lambda: g.vector.memset(ap(out), val), [out], [])
 
     def tr(out, i0):
         return node("v", cnt(out) + 10, lambda: g.vector.transpose(ap(out), ap(i0)), [out], [i0])
 
-    def act(out, i0, bias=None, scale=None, func=F.Identity):
+    def act(out, i0, bias=None, scale=None, func=F.Identity, accum=None):
         kw = {}
         if bias is not None:
             kw["bias"] = bias
         if scale is not None:
             kw["scale"] = scale
-        return node("a", vcost(out, i0, 1.0) + 20,
+        if accum is not None:
+            kw["accum_out"] = accum
+        return node("a", vcost(out, i0, 1.0) + (20 if accum is None else 45),
                     lambda: g.scalar.activation(ap(out), ap(i0), func, **{k: ap(x) for k, x in kw.items()}),
-                    [out], [i0, bias, scale])
+                    [out] + ([] if accum is None else [accum]), [i0, bias, scale])
 
     def scat(win, off, src):
-        if ACT_SCATTER:
-            return act(IND(win, off), src, func=F.Silu)
-        return cp(IND(win, off), src)
+        return act(IND(win, off), src, func=F.Silu)
 
     def mm(items, start, stop):
         def fn():
@@ -167,7 +179,7 @@ def build(g, core, T, topo):
             for j, (o, l, x) in enumerate(items):
                 r = g.tensor.matmul(ap(o), ap(l), ap(x), start and j == 0, stop and j == len(items) - 1)
             return r
-        cost = sum(0.6 * max(64, cnt(x)) * (4 if dty(x) == "float32" else 1) for o, l, x in items)
+        cost = sum(PEC * max(64, cnt(x)) * (4 if dty(x) == "float32" else 1) for o, l, x in items)
         return node("p", cost, fn, [o for o, l, x in items], [y for o, l, x in items for y in (l, x)])
 
     def sel(fam, r):
@@ -176,12 +188,12 @@ def build(g, core, T, topo):
     def fold(out, fam, src, lo, n, start, stop):
         return mm([(out, sel(fam, r), S(src, lo + r, lo + r + 16 * (n - 1) + 1, 16)) for r in range(16)], start, stop)
 
-    def iota(out, pat, base, cm=0):
+    def iota(out, pat, base, cm=0, after=()):
         if dty(out) == "int32":
             fn = lambda: g.iota(ap(out), pat, base, cm)
         else:
             fn = lambda: g.iota(ap(out), pat, base, cm, allow_small_or_imprecise_dtypes=True)
-        return node("g", 160 + 2 * cnt(out), fn, [out], [])
+        return node("g", 160 + 2 * cnt(out), fn, [out], [], after=after)
 
     def dma(e, out, in_, sem, lat, outs=(), ins=(), **kw):
         return node(e, 100 if e != "g" else 1200, lambda: eng[e].dma_start(out(), in_(), **kw), list(outs), list(ins), lat=lat, sem=sem, inc=16)
@@ -200,27 +212,31 @@ def build(g, core, T, topo):
             g.remote_dma_fused(trs, local_sem=T.sem[tsem])
             return None
         k = node("g", 600, fn, [], srcs, lat=lat, sem=tsem, inc=2 * h)
-        node("R", 0, None, dsts, [], lat=lat + 1500, sem=rsem, inc=2 * h, after=[k])
+        node("R", 0, None, dsts, [], lat=1500, sem=rsem, inc=2 * h, after=[k])
+        return k
 
     dma("s", lambda: T.X[:, 0:V], lambda: T.feat[:], "dx", 3500, outs=[S("X", 0, V)])
     dma("a", lambda: T.HI[:], lambda: T.hits[:], "dh", 4500, outs=[S("HI")])
     dma("s", lambda: T.wi[:, 32:48], lambda: T.lane0[:], "dl", 2500, outs=[S("wi", 32, 48)])
-    exchange([S("X", 0, GH)] * 2, [S("X", V, V + GH), S("X", V + GH, W)], "tx", "rx", 6000)
+    sent = exchange([S("X", 0, GH)] * 2, [S("X", V, V + GH), S("X", V + GH, W)], "tx", "rx", 6000)
 
     def c(j, n=1):
         return S("c", j, j + n)
 
     def ci(j, n=1):
         return S("ci", j, j + n)
-    ROW, GRP, PAR, PID, G15, M0c, M1c, M4c, WN, WS, WM, W014, WH, THC, R4A, R4B, TMP, TMP2 = [c(j) for j in range(18)]
-    LT, HBI, DUMP, DUMS, DUMS1, D8, CD8, G8, TH8 = c(32, 16), c(48, 16), c(64, 16), c(80, 16), c(96, 16), c(112, 8), c(120, 8), c(128, 8), c(136, 8)
-    T16a, T16b, T16c, I16, I17 = c(144, 16), c(160, 16), c(176, 16), c(192, 16), c(208, 18)
-    OENT, ORET, OSEL, OBC = S("cu", 0, 16), S("cu", 16, 33), S("cu", 48, 64), S("cu", 64, 80)
-    iota(ci(0), [[0, 1]], 0, 1)
-    iota(S("IU"), [[1, 144]], 0)
-    iota(S("I256"), [[1, 256]], 0)
-    iota(S("IG"), [[1, 8], [0, 16]], 0)
-    iota(ci(16, 16), [[1, 16]], 0)
+
+    def wg(j, n=1):
+        return S("WG", 8 * j, 8 * (j + n))
+    ROW, GRP, PAR, PID, G15, WN, WS, WM, W014, WH, R4A, R4B, TMP, TMP2, WP, TC2, TC3 = [c(j) for j in range(17)]
+    DUMP, D8, CD8, G8, TH8, T16a, I16 = c(64, 32), c(112, 8), c(120, 8), c(128, 8), c(136, 8), c(144, 16), c(192, 16)
+    OENT, OBC = S("cu", 0, 8), S("cu", 16, 32)
+    first = [iota(ci(0), [[0, 1]], 0, 1), iota(S("IU"), [[1, 144]], 0), iota(S("IG"), [[1, 8], [0, 16]], 0)]
+    iota(S("I256"), [[32, 256]], 0)
+    iota(S("NB", 0, V), [[32, V // 256], [0, 256]], 0, after=first)
+    iota(S("NB", V, W), [[32, (W - V) // 256], [0, 256]], 32 * V // 256, after=[sent])
+    dma("s", lambda: T.NB[1::16, 0:V], lambda: T.I256[0:32, :], "dn", 2500, outs=[S("NB", 0, V)], ins=[S("I256")])
+    dma("s", lambda: T.NB[1::16, V:W], lambda: T.I256[0:56, :], "dm", 2500, outs=[S("NB", V, W)], ins=[S("I256")])
     ts(ci(1), ci(0), 15, A.bitwise_and)
     ts(ci(2), ci(0), 4, A.arith_shift_right)
     ts(ci(3), ci(2), 1, A.bitwise_and)
@@ -228,314 +244,415 @@ def build(g, core, T, topo):
     cp(PID, ci(0))
     ts(G15, GRP, 16.0, A.mult, 15.0, A.add)
     cp(I16, S("IU", 0, 16))
-    ts(c(224, 8), S("IU", 0, 8), ROW, A.is_equal)
+    ts(c(224, 16), S("IU", 0, 16), ROW, A.is_equal)
     mk = lambda j: c(224 + j)
-    ts(TMP, mk(0), 8.0, A.mult)
+    ts(TMP, mk(0), 4.0, A.mult)
     ts(TMP2, mk(1), 1.0 / 32, A.mult, TMP, A.add)
     ts(WN, mk(4), 4.0, A.mult, TMP2, A.add)
     ts(WS, mk(2), mk(3), A.add, -128.0, A.mult)
     tt(WM, WN, WS, A.add)
+    tt(WP, WN, WS, A.subtract)
     ts(W014, mk(0), mk(1), A.add, mk(4), A.add)
     tt(WH, mk(2), mk(3), A.subtract)
     ts(R4A, mk(4), 32.0 * V / 128, A.mult)
     ts(R4B, mk(4), 32.0 * (V + GH) / 128, A.mult)
-    tt(c(22), WN, WS, A.subtract)
-    ts(c(23), WS, -2.0, A.mult)
-    for fam, wt in (("SN", WN), ("SQ", c(23)), ("SY", 4096.0), ("SP", c(22)), ("SA", 8192.0), ("SX", -4096.0), ("SM", WM), ("S32", 32.0), ("Z0", mk(0))):
+    for fam, wt in (("SN", WN), ("SA", 8192.0), ("SX", -4096.0), ("SM", WM), ("SP", WP), ("S32", 32.0), ("Z0", mk(0))):
         ts(S(fam), S("IU"), G15, A.is_equal, wt, A.mult)
-    for m, wt in (("RN", WN), ("BD32", 32.0), ("BDC", -float(2 ** 20)), ("BD1", 1.0)):
+    for m, wt in (("RN", WN), ("BDC", -float(2 ** 20)), ("BD1", 1.0)):
         ts(S(m), S("IG"), GRP, A.is_equal, wt, A.mult)
-    for m, wt in (("IBIG", BIG), ("I1", 1.0), ("I1F", 1.0), ("IM1", -1.0), ("I24", float(2 ** 24)), ("I014", W014), ("IH", WH)):
+    for m, wt in (("IBIG", BIG), ("I1", 1.0), ("I1F", 1.0), ("IM1", -1.0), ("I24", float(2 ** 24)), ("I014", W014), ("IH", WH),
+                  ("I13", 8192.0), ("IM13", -8192.0)):
         ts(S(m), S("IU", 0, 128), PID, A.is_equal, wt, A.mult)
-    ts(S("MT"), S("IU", 0, 128), PID, A.is_lt, -1.0, A.mult)
-    tt(S("UP"), S("MT"), S("BD1"), A.mult)
+    ts(S("RZ", 0, 128), S("RN"), -1.0, A.mult)
+    mset(S("RZ", 128, 256), 0.0)
+    ts(S("IMG"), S("IH"), 1.5 * 2 ** 32, A.mult)
+    ts(S("IMH"), S("IH"), -1.5 * 2 ** 32, A.mult)
+    ts(S("IH"), S("IH"), -240.0, A.mult)
+    tt(S("BD32"), sel("S32", 2), sel("S32", 3), A.subtract)
     ts(S("WBL"), sel("Z0", 1), 32.0, A.mult)
-    ts(S("MT"), sel("Z0", 0), 1.0 / 256, A.mult)
+    ts(S("MT"), sel("Z0", 0), 1.0 / 128, A.mult)
     tt(S("WBH"), S("MT"), sel("Z0", 1), A.subtract)
-    ts(LT, I16, ROW, A.is_gt)
     for r in range(16):
-        act(S("TRI", 128 * r, 128 * r + 128), sel("SA", r), scale=c(32 + r))
-    ts(HBI, I16, mk(0), A.mult, 32.0, A.mult)
-    ts(c(21), mk(1), 32.0, A.mult)
-    for h in range(W // 256):
-        act(S("NB", 256 * h, 256 * h + 256), S("I256"), bias=c(48 + h), scale=c(21))
+        ts(S("ROWS", 128 * r, 128 * r + 128), S("BD1"), mk(r), A.mult)
+    mset(c(32, 16), 0.5)
+    scan(S("PW2", 0, 16), c(32, 16), c(32, 16), 131072.0, A.mult, A.max)
+    for n in (16, 32, 64, 128):
+        cp(S("PW2", n, 2 * n), S("PW2", 0, n))
+    tt(c(48, 16), S("PW2", 0, 16), c(224, 16), A.mult)
+    total(c(21), c(48, 16))
+    ts(S("BDW"), S("BD1"), c(21), A.mult, 0.5, A.mult)
+    ts(S("BDB"), S("BD1"), 65536.0, A.mult)
+    ts(S("BY", 0, 128), S("BD1"), -1.0, A.mult)
+    cp(S("BY", 128, 256), S("BD1"))
+    ts(S("BJ", 0, 128), S("BD1"), 1.0 / 16, A.mult)
+    ts(S("BJM"), S("BD1"), -1.0 / 16, A.mult)
+    ts(S("BJ", 128, 256), S("BD1"), 1.0 / 8, A.mult)
+    ts(S("BJ", 256, 384), S("BD1"), 1.0 / 8, A.mult)
+    ts(G8, S("IU", 0, 8), GRP, A.is_equal)
+    ts(TMP, WS, 1.0 / 4096, A.mult)
+    ts(TMP2, WS, -1.0 / 4096, A.mult)
+    for j, wt in enumerate((WN, WN, TMP, TMP2, -1.0, 1.0, 2.0, -2.0, 8192.0, WM, WP, -4096.0, 4096.0, WN, WN, TMP2, TMP)):
+        ts(wg(j), G8, wt, A.mult)
     mset(S("ONE"), 1.0)
-    act(S("LC"), S("I256"), scale=32.0)
     for b in ("MV", "MB"):
         mset(S(b, 256, 272), 128.0)
     for b in ("MZ", "NL"):
         mset(S(b, 256, 272), 0.0)
-    mset(S("CR", 0, 16), 0.0)
+    for b in ("A1", "A2"):
+        for lo, hi in ((0, 16), (144, 176), (304, 320)):
+            mset(S(b, lo, hi), 0.0)
+    mset(S("M", W, WD), 0.0)
+    mset(S("B", V, V + 8), 128.0)
     ts(T16a, I16, 16.0, A.mult, ROW, A.add)
-    ts(DUMP, T16a, float(W), A.add)
-    ts(DUMS, T16a, float(LN), A.add)
-    ts(DUMS1, T16a, float(LN + 1), A.add)
-    for j in range(2):
-        ts(c(112 + 4 * j, 4), c(144, 4), float(W - V), A.add)
+    ts(c(64, 16), T16a, float(W), A.add)
+    ts(c(80, 16), T16a, float(W), A.add)
+    ts(D8, c(144, 8), float(W - V + LN), A.add)
     ts(c(120, 4), c(112, 4), -1.0, A.mult)
     ts(c(124, 4), c(116, 4), -1.0, A.mult, float(GH), A.add)
-    ts(TMP2, ROW, 16.0, A.mult)
-    ts(S("c", 208, 224), I16, TMP2, A.add)
-    cp(S("c", 224 + 8, 224 + 9), TMP2)
-    cp(S("cu", 16, 32), S("c", 208, 224))
-    cp(S("cu", 32, 33), S("c", 232, 233))
-    ts(OBC, I16, 0.0, A.mult, ROW, A.add)
-    ts(ci(32, 16), ci(16, 16), PAR, A.add)
-    ts(ci(48, 16), ci(32, 16), 1, A.bitwise_and)
-    ts(ci(64, 16), ci(16, 16), 15.0, A.add)
-    ts(ci(80, 16), ci(64, 16), 15, A.bitwise_and)
-    tt(T16b, ci(80, 16), ci(16, 16), A.subtract)
-    ts(T16c, T16b, 16.0, A.mult, 256.0, A.add)
-    tt(T16b, T16c, ci(48, 16), A.mult)
-    tt(T16c, T16b, T16a, A.add)
-    cp(OSEL, T16c)
-    ts(T16b, I16, ROW, A.is_equal)
-    tt(S("c", 240, 256), T16b, T16c, A.mult)
-    node("v", 74, lambda: g.vector.tensor_reduce(ap(c(18)), ap(S("c", 240, 256)), AxisListType.X, A.add), [c(18)], [S("c", 240, 256)])
-    tt(c(19), c(18), ROW, A.subtract)
-    ts(OENT, I16, c(19), A.add)
+    ts(c(18, 2), c(144, 2), 0.5, A.add)
+    ts(ci(4), ci(0), 7, A.bitwise_and)
+    ts(ci(5), ci(1), 3, A.arith_shift_right)
+    tt(ci(6), ci(1), ci(3), A.add)
+    ts(ci(7), ci(6), 1, A.bitwise_and)
+    cp(c(24, 4), ci(4, 4))
+    ts(TMP, c(24), 16.0, A.mult, c(25), A.add)
+    ts(TMP2, c(27), 144.0, A.mult, TMP, A.add)
+    ts(OENT, c(192, 8), 2.0, A.mult, TMP2, A.add)
+    ts(S("cu", 16, 24), c(192, 8), 0.0, A.mult, c(24), A.add)
+    ts(c(28), c(24), 8.0, A.add)
+    ts(S("cu", 24, 32), c(192, 8), 0.0, A.mult, c(28), A.add)
     dma("g", lambda: T.ci[0:1, 96:104], lambda: T.th[:], "dt", 3000, outs=[ci(96, 8)], allow_slow_non_contiguous=True)
     node("g", 200, lambda: g.partition_broadcast(T.ci[:, 104:112], T.ci[0:1, 96:104], 128), [ci(104, 8)], [ci(96, 8)])
-    ts(G8, S("IU", 0, 8), GRP, A.is_equal)
     tt(TH8, ci(104, 8), G8, A.mult)
-    node("v", 74, lambda: g.vector.tensor_reduce(ap(c(20)), ap(TH8), AxisListType.X, A.add), [c(20)], [TH8])
-    ts(THC, c(20), -4095.0, A.add, 4096.0, A.mult)
-    ts(S("wb", 48, 56), G8, WN, A.mult)
+    total(c(20), TH8)
+    cp(ci(8), c(20))
+    ts(ci(9), ci(8), 15, A.bitwise_and)
+    ts(ci(10), ci(8), 4080, A.bitwise_and)
+    ts(c(22), ci(9), 0.5, A.add, mk(1), A.mult)
+    ts(c(23), ci(10), mk(0), A.mult, c(22), A.add)
+    ts(c(29), mk(2), -16384.0, A.mult)
+    tt(TC2, c(29), c(23), A.subtract)
+    tt(TC3, c(29), c(23), A.add)
+    ts(S("TH", 0, 128), S("BD1"), TC2, A.mult)
+    ts(S("TH", 128, 256), S("BD1"), TC3, A.mult)
 
     cp(S("L", 0, V), S("HI"))
     act(S("GA"), S("L", 0, GH), bias=float(GH), scale=-1.0, func=F.Relu)
-    for bank, lo, hi in (("PKC", 0, 512), ("PKO", 512, GH)):
+    for bank, lo, hi in (("KK0", 0, 512), ("KK1", 512, GH)):
         mm([(S(bank, 0, hi - lo), S("RN"), S("NB", lo, hi)), (S(bank, 0, hi - lo), S("IBIG"), S("GA", lo, hi))], True, True)
         tt(S("GB", lo, hi), S(bank, 0, hi - lo), S("L", lo, hi), A.min)
     cp(S("GL"), S("GB"))
     exchange([S("GL")] * 2, [S("LG", 0, GH), S("LG", GH, 2 * GH)], "tl", "rl", 6000)
-    act(S("B", V, W), S("NB", V, W), bias=128.0, scale=0.0)
     for lo in (0, 512):
         act(S("HB"), S("L", lo, lo + 512), scale=32.0)
-        mm([(S("PA"), S("WBH"), S("HB")), (S("PA"), S("WBL"), S("L", lo, lo + 512))], True, True)
-        act(S("B", lo, lo + 512), S("PA"))
+        mm([(S("KK0"), S("WBH"), S("HB")), (S("KK0"), S("WBL"), S("L", lo, lo + 512))], True, True)
+        act(S("B", lo, lo + 512), S("KK0"))
 
-    def pieces(out, names, x, hb, pa, pb):
-        n = cnt(out)
-        mm([(S(pa, 0, n), S("BD32"), x)], True, True)
-        act(hb, S(pa, 0, n), bias=-256.0, func=F.Relu)
-        mm([(S(pb, 0, n), S("I014"), names), (S(pb, 0, n), S("IH"), hb), (S(pb, 0, n), sel("S32", 3), x)], True, True)
-        act(out, S(pb, 0, n))
+    def pieces(out, names, x, o):
+        one = S("ONE", 0, cnt(out))
+        mm([(o, S("I014"), names), (o, S("IH"), one), (o, S("BD32"), x), (o, S("IMG"), one), (o, S("IMH"), one), (o, sel("S32", 3), x)], True, True)
+        act(out, o)
 
-    for lo in range(0, W, 512):
-        hi = min(lo + 512, W)
-        pieces(S("M0", lo, hi), S("NB", lo, hi), S("X", lo, hi), S("MH", lo, hi), "PC", "PO")
+    for lo in (0, 512):
+        pieces(S("MH", lo, lo + 512), S("NB", lo, lo + 512), S("X", lo, lo + 512), S("KK1"))
+    cp(S("M", 0, V), S("MH"))
+    exchange([S("MH", 0, GH)] * 2, [S("LM", 0, GH), S("LM", GH, 2 * GH)], "tp", "rp", 6000)
 
-    def w(j):
-        return S("w", 16 * j, 16 * j + 16)
+    def w(j, n=1):
+        return S("w", 16 * j, 16 * (j + n))
 
     def u(j, n=16):
         return S("u", j, j + n)
-    VF, VA, AW, VD, BF, JN, G1, J1, THW, THA, BJ, NJ, OWN, VL, CTW = [w(j) for j in range(15)]
-    t0, t1, t2, t3, t4, t5, t6, t7 = [w(j) for j in range(16, 24)]
-    PU, VU, BU, OL, OJ, OB, BBU, OS, SU, GU = u(0), u(16), u(32), u(48), u(64), u(80), u(96), u(112), u(128, 4), u(136, 8)
-    cp(PU, S("wi", 32, 48))
+    VF, VA, AW, VM, BF, JN, G1, J1, OWN, VL, CT = [w(j) for j in range(11)]
+    PU, VU, BU, OL, BBU, BC, SU, GU = u(0), u(16), u(32), u(48), u(64), u(80), u(96, 4), u(104, 8)
+    NJ, TL = S("wb", 0, 16), S("wb", 16, 32)
 
-    def lanes(mwin):
-        act(S("MV", 0, LN), IND(mwin, PU))
-        fold(S("PW", 0, 16), "SN", "MV", 0, 16, True, True)
-        cp(VU, S("PW", 0, 16))
-        cp(VF, S("PW", 0, 16))
+    def pair(b):
+        return S(b, 384, 640)
+
+    def rep(b, h, n):
+        return S(b, 512 - 128 * n, 512) if h == 0 else S(b, 512, 512 + 128 * n)
+
+    def repeat(b, h, n):
+        if n >= 2:
+            act(S(b, 256 + 384 * h, 384 + 384 * h), rep(b, h, 1))
+        if n >= 4:
+            act(S(b, 768 * h, 768 * h + 256), rep(b, h, 2))
+
+    def lanes(t):
+        if t == 0:
+            cp(VU, S("wi", 32, 48))
+            cp(VF, S("wi", 32, 48))
+            act(S("MV", 0, LN), IND(S("NB", 0, V), VU))
+        else:
+            act(S("MV", 0, LN), IND(S("M", 0, V), PU))
+            fold(S("PW", 0, 16), "SN", "MV", 0, 16, True, True)
+            cp(VU, S("PW", 0, 16))
+            (act if OPT["vf"] == "a" else cp)(VF, S("PW", 0, 16))
         mm([(S("PA", 0, LN), S("RN"), S("MV", 0, LN))], True, True)
         cp(S("PR"), S("PA", 0, LN))
+        mm([(S("PA", 128 * h, 128 * h + 128), S("MV", 128 * h, 128 * h + 128), S("RN")) for h in range(2)], True, True)
+        act(S("CL"), S("PA", 0, LN), bias=CLAMP)
         for s in range(16):
             ts(S("E", 272 * s, 256 * s + 256), S("PR", 16 * s, 256), S("w", s, s + 1), A.is_equal)
-        mm([(S("PA", 16 * s + 16, LN), S("BD1"), S("E", 272 * s + 16, 256 * s + 256)) for s in range(15)], True, True)
-        act(S("CR", 16, LN), S("PA", 16, LN))
-        fold(S("PW", 16, 32), "SA", "CR", 0, 16, True, False)
-        mm([(S("PW", 16, 32), S("TRI", 128 * r, 128 * r + 128), S("E", r, r + 272 * 15 + 1, 272)) for r in range(1, 16)], False, True)
+        mm([(S("PA", 0, LN), S("BJM"), S("PW2"))], True, False)
+        for q in range(0, 16, 4):
+            mm([(S("PA", 16 * s, 16 * s + 16), S("BDW"), S("E", 272 * s, 272 * s + 16)) for s in range(q, q + 4)]
+               + [(S("PA", 16 * s + 16, LN), S("BDB"), S("E", 272 * s + 16, 256 * s + 256)) for s in range(q, min(q + 4, 15))], False, q == 12)
+        act(S("CR"), S("PA", 0, LN), bias=1.0, func=F.Relu)
+        fold(S("PW", 16, 32), "SA", "CR", 0, 16, True, True)
         tt(VA, S("PW", 16, 32), VF, A.add)
-        ts(AW, S("PW", 16, 32), 0.0, A.is_equal)
+        tt(VM, VA, c(64, 16), A.min)
+        cp(OL, VM)
+        ts(AW, VM, float(V), A.is_lt)
         act(S("VT"), IND(VF, OBC))
-        act(S("CT"), IND(VF, OBC), bias=CLAMP)
-        tt(VD, VF, DUMP, A.subtract)
-        tt(w(24), VD, AW, A.mult)
-        tt(w(25), w(24), DUMP, A.add)
-        cp(OL, w(25))
 
-    def turn(buf, z):
-        tr(S(z, 0, 256), S(buf, 0, 256))
-        tr(S(z, 256, 512), S(buf, 16, 272))
-
-    def names(t, e, off, lwin, abuf, z, raw, outu, outf, dm, pn, chunks, mcur, each):
-        get = act if e == "a" else cp
-        get(S(abuf, 0, 256), IND(lwin, off))
-        get(S(abuf, 256, 272), IND(lwin, S(off[0], off[1], off[1] + 1)))
-        turn(abuf, z)
+    def names(t, h, off, lwin, abuf, raw, outu, outf, dm, pn, chunks, each):
+        a, z, o = 160 * h, 288 * h, 128 * h
+        act(S(abuf, a + 16, a + 144), IND(lwin, S(off[0], off[1] + 8 * h, off[1] + 8 * h + 8)))
+        tr(S("Z", z, z + 128), S(abuf, a + 16, a + 144))
+        tr(S("Z", z + 128, z + 288), S(abuf, a, a + 160))
         if t == 0:
-            cp(S(outu), IND(S(z), OENT))
-            act(S(outf), IND(S(z), OENT))
+            cp(S(outu, o, o + 128), IND(S("Z", z, z + 288), OENT))
+            if outf:
+                act(S(outf, o, o + 128), IND(S("Z", z, z + 288), OENT))
         else:
-            cp(S(raw), IND(S(z), OENT))
-        k = 0
-        for n in chunks:
+            cp(S(raw, o, o + 128), IND(S("Z", z, z + 288), OENT))
+        k = 16 * h
+        for n, e in chunks:
+            get = cp if e == "v" else act
             if t == 0:
-                act(S(dm, 256 * k, 256 * (k + n)), IND(S("X", 0, W), S(outu, 16 * k, 16 * (k + n))))
+                get(S(dm, 128 * k, 128 * (k + n)), IND(S("X", 0, W), S(outu, 8 * k, 8 * (k + n))))
             else:
-                (cp if k == 0 and OPT[4] and dm == "DC" else act)(S(dm, 256 * k, 256 * (k + n)), IND(mcur, S(raw, 16 * k, 16 * (k + n))))
-                fold(S(pn, 16 * k, 16 * (k + n)), "SN", dm, 256 * k, 16 * n, True, True)
-                cp(S(outu, 16 * k, 16 * (k + n)), S(pn, 16 * k, 16 * (k + n)))
+                get(S(dm, 128 * k, 128 * (k + n)), IND(S("M", 0, W), S(raw, 8 * k, 8 * (k + n))))
+                fold(S("PC", pn + 8 * k, pn + 8 * (k + n)), "SN", dm, 128 * k, 8 * n, True, True)
+                cp(S(outu, 8 * k, 8 * (k + n)), S("PC", pn + 8 * k, pn + 8 * (k + n)))
+            each(k, k + n)
             k += n
-            if k % 4 == 0:
-                each(k // 4 - 1)
 
-    def far(buf, offs, y, j, n):
-        for k in range(4 * j, 4 * j + 4, n):
-            tt(S(buf, 256 * k, 256 * (k + n)), IND(S("X", 0, W), S(offs, 16 * k, 16 * (k + n))), S(y, 0, 256 * n), A.max)
+    def far(buf, offs, y, lo, hi, n):
+        for k in range(lo, hi, n):
+            tt(S(buf, 128 * k, 128 * (k + n)), IND(S("X", 0, W), S(offs, 8 * k, 8 * (k + n))), rep(y, k // 16, n), A.max)
 
-    def over(buf, offs, src, j):
-        lo = 1024 * j
-        if src is None:
-            src, lo = "XC", 1024 * (j % 2)
-            act(S(src, lo, lo + 1024), IND(S("X", 0, W), S(offs, 64 * j, 64 * j + 64)))
-        for h in (0, 512):
-            mm([(S("PE"), S("I1"), S("ZZ", 0, 512)), (S("PE"), S("IM1"), S(src, lo + h, lo + h + 512))], True, True)
-            act(S(buf, 1024 * j + h, 1024 * j + h + 512), S("PE"), func=F.Relu)
+    def near(buf, src, lo, hi):
+        for k in range(lo, hi, 2):
+            tt(S(buf, 128 * k, 128 * k + 256), S(src, 128 * k, 128 * k + 256), S("PC", 256 * (k // 16), 256 * (k // 16) + 256), A.max)
 
-    def quarter(bank, fam, src, j, stop=False):
-        fold(S(bank, 64 * j, 64 * j + 64), fam, src, 1024 * j, 64, False, stop)
+    def less(lo, hi, n):
+        for k in range(lo, hi, n):
+            d, r = S("XC", 128 * k, 128 * (k + n)), S("D0", 128 * k, 128 * (k + n))
+            tt(d, IND(S("X", 0, W), S("CU", 8 * k, 8 * (k + n))), rep("XV", k // 16, n), A.subtract)
+            if k // 8 in RELU:
+                act(r, d, scale=-1.0, func=F.Relu)
+            else:
+                ts(r, d, -1.0, A.mult, 0.0, A.max)
 
-    def opening(bank):
-        mm([(S(bank, 0, LN), S("BDC"), S("ONE"))], True, False)
+    def again(j):
+        for x in (1024 * j, 1024 * j + 512):
+            mm([(S("K0"), S("I1"), rep("ZZ", j // 2, 4)), (S("K0"), S("IM1"), rep("XV", j // 2, 4)), (S("K0"), S("IM1"), S("XC", x, x + 512))], True, True)
+            act(S("D1", x, x + 512), S("K0"), func=F.Relu)
 
-    def pen(bank, tiles, stop=False):
-        mm([(S(bank, 0, LN), S("IBIG"), S(x)) for x in tiles], False, stop)
+    def over(buf, src, j):
+        for x in (1024 * j, 1024 * j + 512):
+            mm([(S("K0"), S("I1"), rep("ZZ", j // 2, 4)), (S("K0"), S("IM1"), S(src, x, x + 512))], True, True)
+            act(S(buf, x, x + 512), S("K0"), func=F.Relu)
 
-    lanes(S("NB", 0, V))
-    mname = "M0"
+    def lift(bank, lo, src, j, wts, stop=False):
+        n = cnt(wts)
+        return mm([(S(bank, lo + k % 16, lo + k % 16 + 16 * (n - 1) + 1, 16), S(src, 128 * k, 128 * k + 128), wts) for k in range(8 * j, 8 * j + 8)], False, stop)
+
+    def spread(bank, lo, src, h, wts, start=False, stop=False):
+        return mm([(S(bank, lo, lo + cnt(wts)), S(src[0], src[1] + 128 * h, src[1] + 128 * h + 128), wts)], start, stop)
+
+    lanes(0)
     for t in range(RO):
         last = t == RO - 1
-        mcur = S("NB") if t == 0 else S(mname, 0, W)
-        cnum = S("CF") if t == 0 else S("PC", 0, LN)
-        onum = S("OF") if t == 0 else S("PO", 0, LN)
-        sfam, mfam, pfam = ("SX", "SX", "SY") if t == 0 else ("SS", "SM", "SP")
-        act(S("XV", 0, LN), IND(S("X", 0, V), VU))
-        act(S("XV", LN, 2 * LN), S("XV", 0, LN))
-        act(S("XM"), S("XV", 0, LN), bias=-0.5)
-        opening("PE")
+        mcur = S("NB") if t == 0 else S("M", 0, W)
+        cnum = "CF" if t == 0 else "PC"
+        OJ, OB = S("fw", 40 * t, 40 * t + 16), S("fw", 40 * t + 20, 40 * t + 36)
+        for h in range(2):
+            act(rep("XV", h, 1), IND(S("X", 0, V), u(16 + 8 * h, 8)))
+            repeat("XV", h, NX if t else 2)
+            if t == 0:
+                mm([(S("PC", 256 * h, 256 * h + 256), S("I1"), rep("XV", h, 2))], True, True)
+            spread("UX", 256 * h, ("ONE", 0), 0, S("TH"), start=h == 0)
+            spread("UX", 256 * h, pair("XV"), h, S("BY"))
+            spread("UE", 256 * h, ("MV", 0), h, S("RZ"), start=h == 0)
 
-        def step1(j):
-            if j == 0 and t == 0:
-                mm([(S("PKO", 0, LN), S("I1F"), S("CF"))], True, False)
-            fold(S("PKO", 64 * j, 64 * j + 64), mfam, "DC", 1024 * j, 64, t > 0, t > 0 or j == 3)
-            far("D0", "CU", "XV", j, 2)
-            if j < 3:
-                quarter("PE", "SA", "D0", j)
-        names(t, "a" if OPT[1] else "v", VU, S("L", 0, V), "A1", "Z1", "RU", "CU", "CF", "DC", "PC", [4, 4, 4, 4] if t == 0 else CH, mcur, step1)
-        act(S("CS"), S("PKO", 0, LN))
-        if t > 0 and not last:
-            act(S("CF", 16 * t, 16 * t + 16), S("PC", 16 * t, 16 * t + 16))
-        tt(S("EQ1"), cnum, S("VT"), A.is_equal)
-        mm([(S("PE", 0, 192), S("I24"), S("EQ1", 0, 192))], False, True)
-        mm([(S("PKC", 0, 64), S("BDC"), S("ONE", 0, 64)), (S("PKC", 0, 64), S("I24"), S("EQ1", 192, 256))], True, False)
-        fold(S("PKC", 0, 64), "SA", "D0", 3072, 64, False, True)
-        fold(S("PB", 0, 16), "SA", "XV", 0, 16, True, True)
-        ts(THW, S("PB", 0, 16), 0.5, A.mult, THC, A.add)
-        if t > 0:
-            nf = 64 if last else 176
-            for lo in range(0, 16 * nf, 704):
-                act(S("MH", lo, min(lo + 704, 16 * nf)), S(mname, lo, min(lo + 704, 16 * nf)))
-            fold(S("PB", 0, nf), "SN", "MH", 0, nf, True, True)
-            cp(S("FW", 0, 64), S("PB", 0, 64))
-            if nf > 64:
-                ts(S("FW", 64, 176), S("PB", 64, 176), -float(V), A.add)
+            def step1(lo, hi):
+                sub = lo // 8 in SUB[t]
+                if t == 0:
+                    near("D0", "DC", lo, hi)
+                elif sub:
+                    less(lo, hi, min(NX, hi - lo))
+                else:
+                    far("D0", "CU", "XV", lo, hi, min(NX, hi - lo))
+                if hi % 8:
+                    return
+                j = hi // 8 - 1
+                k0 = S("KK%d" % h if j % 2 else "K0", 0, 64)
+                fam = ("SP" if sub else "SM") if t else "SX"
+                tt(S("EQ", 64 * j, 64 * j + 64), S(cnum, 64 * j, 64 * j + 64), S("VT", 64 * j, 64 * j + 64), A.is_equal)
+                if t:
+                    lift("UE", 256 * h, "DC", j, wg(0, 2))
+                lift("UX", 256 * h, "DC", j, wg((15 if sub else 2) if t else 4, 2))
+                put = act if OPT["kt"] == "a" else cp
+                if j == 3:
+                    cs = S("K0", 256, 320)
+                    fold(cs, fam, "DC", 3072, 64, True, t > 0)
+                    if t == 0:
+                        mm([(cs, S("I1F"), S("CF", 192, 256))], False, True)
+                    put(S("KT", 128, 192), cs)
+                mm([(k0, S("BDC"), S("ONE", 0, 64)), (k0, S("I24"), S("EQ", 64 * j, 64 * j + 64))], True, False)
+                fold(k0, "SA", "D0", 1024 * j, 64, False, j == 3)
+                if j < 3:
+                    fold(k0, fam, "DC", 1024 * j, 64, False, t > 0)
+                    if t == 0:
+                        mm([(k0, S("I1F"), S("CF", 64 * j, 64 * j + 64))], False, True)
+                if j % 2 == 0:
+                    put(S("KT", 32 * j, 32 * j + 64), k0)
+                lift("UX", 256 * h, "D0", j, wg(6, 2))
+            names(t, h, VU, S("L", 0, V), "A1", "RU", "CU", "CF", "DC", 0, CH0[h] if t == 0 else CH[h], step1)
+            if t == 0:
+                for lo in (0, 128):
+                    spread("UE", 256 * h + lo, ("A1", 16 + 32 * h), h, S("I1F"))
+            kt = lambda lo, n: S("KT", 192 + 128 * h + lo, 192 + 128 * h + lo + n)
+            if h == 0:
+                tt(kt(0, 64), S("KK0", 0, 64), S("KT", 0, 64), A.min)
+            else:
+                tt(S("KT", 0, 64), S("KK1", 0, 64), S("KT", 128, 192), A.add)
+                tt(kt(0, 64), S("KT", 0, 64), S("KT", 64, 128), A.min)
+            tt(kt(64, 32), kt(0, 32), kt(32, 32), A.min)
+            tt(kt(96, 16), kt(64, 16), kt(80, 16), A.min)
+            tt(S("wi", 8 * h, 8 * h + 8), kt(96, 8), kt(104, 8), A.min)
+            ts(S("wi", 16 + 8 * h, 24 + 8 * h), S("wi", 8 * h, 8 * h + 8), 4095, A.bitwise_and)
+            cp(u(32 + 8 * h, 8), S("wi", 16 + 8 * h, 24 + 8 * h))
+            if not last:
+                act(S("w", 160 + 8 * h, 168 + 8 * h), S(cnum, 128 * h + 8 * t, 128 * h + 8 * t + 8))
+        cp(BF, S("wi", 16, 32))
+        ts(BC, S("wi", 16, 32), float(V), A.min)
+        if last:
+            act(S("MH"), S("M", 0, V))
+            fold(S("PA", 0, 64), "SN", "MH", 0, 64, True, True)
+            cp(S("FW"), S("PA", 0, 64))
         if t == 0:
             for d in range(2):
                 ts(S("L", V + d * GH, V + (d + 1) * GH), S("LG", d * GH, (d + 1) * GH), float(V + d * GH), A.add)
         else:
             for d in range(2):
-                cp(IND(S("L", V, WD), u(136 + 4 * d, 2)), S("LL%d" % (t - 1), 32 * d, 32 * d + 32))
-        tt(S("KEY", 0, 192), S("PE", 0, 192), S("CS", 0, 192), A.add)
-        tt(S("KT", 0, 64), S("KEY", 0, 64), S("KEY", 64, 128), A.min)
-        tt(S("KT", 64, 128), S("KT", 0, 64), S("KEY", 128, 192), A.min)
-        tt(S("KEY", 192, 256), S("PKC", 0, 64), S("CS", 192, 256), A.add)
-        tt(S("KT", 128, 192), S("KT", 64, 128), S("KEY", 192, 256), A.min)
-        tt(S("KT", 192, 224), S("KT", 128, 160), S("KT", 160, 192), A.min)
-        tt(S("wi", 0, 16), S("KT", 192, 208), S("KT", 208, 224), A.min)
-        ts(S("wi", 16, 32), S("wi", 0, 16), 4095, A.bitwise_and)
-        cp(BU, S("wi", 16, 32))
-        cp(BF, S("wi", 16, 32))
-        tt(S("ZS"), IND(S("X", 0, W), BU), S("XM"), A.add)
-        if OPT[2]:
-            act(S("ZT"), S("ZS"), bias=MAGIC, scale=0.5)
-            act(S("ZZ", 0, LN), S("ZT"), bias=-MAGIC)
-        else:
-            ts(S("ZT"), S("ZS"), 0.5, A.mult, MAGIC, A.add)
-            ts(S("ZZ", 0, LN), S("ZT"), -MAGIC, A.add)
-        zz = S("ZZ", 0, LN)
-        act(S("ZZ", LN, 2 * LN), S("ZT"), bias=-MAGIC)
-        act(S("ZZ", 2 * LN, 4 * LN), S("ZZ", 0, 2 * LN))
-        act(S("MB", 0, LN), IND(mcur, BU))
-        scat(S("B"), OL, S("MB", 0, LN))
-        act(S("BB"), IND(S("B", 0, W), BU))
+                ts(IND(S("L", V, WD), u(104 + 4 * d, 2)), S("LL%d" % (t - 1), 32 * d, 32 * d + 32), 1.0, A.mult, float(V + d * GH), A.add)
+        for h in range(2):
+            o = 128 * h
+            tt(S("ZS", o, o + 128), IND(S("X", 0, W), u(32 + 8 * h, 8)), rep("XV", h, 1), A.add)
+            if OPT["z"] == "a":
+                act(S("ZT", o, o + 128), S("ZS", o, o + 128), scale=0.5 - 2.0 ** -11, bias=MAGIC)
+            else:
+                ts(S("ZT", o, o + 128), S("ZS", o, o + 128), 0.5 - 2.0 ** -11, A.mult, MAGIC, A.add)
+            if OPT["z"] != "v":
+                act(rep("ZZ", h, 1), S("ZT", o, o + 128), bias=-MAGIC)
+            else:
+                ts(rep("ZZ", h, 1), S("ZT", o, o + 128), -MAGIC, A.add)
+            repeat("ZZ", h, 4)
+            if t == 0:
+                mm([(S("PC", 256 * h, 256 * h + 256), S("I1"), rep("ZZ", h, 2))], True, True)
+        zz = pair("ZZ")
+        for h in range(2):
+            act(S("MB", 128 * h, 128 * h + 128), IND(mcur, u(32 + 8 * h, 8)))
+            scat(S("B"), u(48 + 8 * h, 8), S("MB", 128 * h, 128 * h + 128))
+        act(S("BB"), IND(S("B", 0, V + 8), BC))
+        act(S("MC"), S("MB", 0, LN))
         fold(S("PW", 0, 16), "SN", "BB", 0, 16, True, True)
         if t > 0:
             cp(BBU, S("PW", 0, 16))
             act(S("BK"), IND(mcur, BBU))
             fold(S("PW", 0, 16), "SN", "BK", 0, 16, True, True)
+        tt(G1, BF, VM, A.is_gt)
         tt(J1, S("PW", 0, 16), VF, A.is_equal)
-        tt(G1, BF, VA, A.is_gt)
         tt(JN, J1, G1, A.mult)
-        ts(NJ, JN, -1.0, A.mult, 1.0, A.add)
-        ts(t0, JN, BIG, A.mult)
-        tt(THA, t0, THW, A.add)
-        ts(t1, NJ, -8192.0, A.mult)
-        tt(BJ, t1, BF, A.add)
-        tt(t2, BF, DUMP, A.subtract)
-        tt(t4, VD, JN, A.mult)
-        tt(t5, t2, JN, A.mult)
-        tt(t6, t4, DUMP, A.add)
-        tt(t7, t5, DUMP, A.add)
-        cp(u(64, 32), S("w", 16 * 22, 16 * 24))
-        opening("PKC")
-        for j in range(4):
-            if j < 4 - OFF1[t]:
-                far("D1", "CU", "ZZ", j, 4 if j else 1)
-            else:
-                over("D1", "CU", "DC" if t == 0 else None, j)
-            quarter("PKC", "SA", "D1", j)
-            if j >= 4 - OFF1[t]:
-                quarter("PKC", "SA" if t == 0 else "SQ", "DC", j)
-        names(t, "a", BU, S("L", 0, W), "A2", "Z2", "RU2", "OU", "OF", "DO", "PO", [4, 4, 4, 4], mcur, lambda j: None)
-        act(S("BJT"), IND(BJ, OBC))
-        tt(t3, THW, t0, A.subtract)
-        tt(S("NJT"), IND(t3, OBC), S("KEY"), A.is_gt)
-        tt(S("UPM"), IND(THA, OBC), S("KEY"), A.is_le)
-        tt(S("EQ2"), cnum, S("BJT"), A.is_equal)
-        tt(S("EQ3"), onum, S("VT"), A.is_equal)
-        tt(S("EQ4"), onum, S("BJT"), A.is_equal)
-        pen("PKC", ["EQ1", "EQ2", "UPM"], True)
-        tt(S("ZS"), S("PKC", 0, LN), S("CS"), A.add)
-        tt(S("KC"), S("ZS"), S("CT"), A.min)
-        opening("PKO")
+        ts(NJ, JN, -8192.0, A.mult, 8192.0, A.add)
         if not last:
-            pieces(S("MZ", 0, LN), S("MV", 0, LN), zz, S("HZ"), "PA", "PB")
-            me, le, ml, ll = "ME%d" % t, "LE%d" % t, "ML%d" % t, "LL%d" % t
             ts(VL, VF, float(GH), A.is_lt)
-            tl, inc = S("wb", 0, 16), S("wb", 16, 32)
-            tt(tl, JN, VL, A.mult)
-            node("v", 74, lambda: g.vector.tensor_tensor_scan(ap(inc), ap(S("ONE", 0, 16)), ap(tl), 0.0, A.mult, A.add), [inc], [S("ONE", 0, 16), tl])
-            mm([(S("PW", 0, 16), S("BD1"), inc), (S("PW", 0, 16), S("UP"), tl)], True, True)
-            tt(w(26), S("PW", 0, 16), DUMS1, A.subtract)
-            tt(w(27), w(26), tl, A.mult)
-            tt(w(28), w(27), DUMS, A.add)
-            cp(OS, w(28))
-            mset(S("SL", 0, 32), 32.0 * LN)
-            scat(S("SL"), OS, S("LC"))
-            act(S("MS", 0, 32), S("SL", 0, 32))
-            fold(S("PW", 0, 2), "SA", "MS", 0, 2, True, True)
-            ts(u(128, 2), S("PW", 0, 2), 2.0 ** -22, A.mult)
-            ts(u(130, 2), S("PW", 0, 2), 2.0 ** -22, A.mult)
-            s2 = u(128, 2)
+            tt(TL, JN, VL, A.mult)
+        nb = 1 if last else 2
+        mm([(S("PA", r, r + 16 * (16 * nb - 1) + 1, 16), S("ROWS", 128 * r, 128 * r + 128), S("wb", 0, 16 * nb)) for r in range(16)], True, True)
+        if not last:
+            scan(S("CN"), S("ONE", 0, LN), S("PA", LN, 2 * LN), 0.0, A.mult, A.add)
+        act(S("NN"), S("PA", 0, LN))
+        tt(w(16), NJ, VF, A.add)
+        tt(w(17), NJ, BF, A.add)
+        tt(w(18, 2), w(16, 2), DUMP, A.min)
+        cp(OJ, w(18))
+        cp(OB, w(19))
+        mm([(S("KK0", 0, 384), S("BDC"), S("ONE", 0, 384))], True, False)
+        for h in range(2):
+            for j in (2 * h, 2 * h + 1):
+                off = j in (SUB[t] if t else OFF1)
+                if t == 0:
+                    over("D1", "DC", j) if off else near("D1", "DC", 8 * j, 8 * j + 8)
+                elif off:
+                    again(j)
+                elif j % 2:
+                    far("D1", "CU", "ZZ", 8 * j, 8 * j + 8, 4)
+                else:
+                    for lo, n in ((0, 1), (1, 1), (2, 2), (4, 4)):
+                        far("D1", "CU", "ZZ", 8 * j + lo, 8 * j + lo + n, n)
+                lift("KK0", 128 * h, "D1", j, wg(8))
+                lift("KK0", 128 * h, "DC", j, wg((10 if off else 9) if t else (12 if off else 11)))
+            if t == 0:
+                spread("KK0", 128 * h, ("A1", 16 + 32 * h), h, S("I1F"))
+        for h in range(2):
+            spread("UE", 256 * h + 128, ("MC", 0), h, S("RZ", 0, 128))
+        for h in range(2):
+            spread("UE", 256 * h + 128, ("NN", 0), h, S("BJ", 0, 128), stop=h == 1)
+            spread("UX", 256 * h, ("NN", 0), h, S("BJ", 128, 384))
+        ts(S("EU"), S("UE"), 0.0, A.is_equal)
+        mm([(S("UX", o + lo, o + lo + 128), S(m), S("EU", o, o + 128)) for o in (0, 256) for lo, m in ((0, "I13"), (128, "IM13"))], False, True)
+        act(S("PN"), S("UX"), scale=2 * BIG, func=F.Relu)
+        ko = (("KK0", 256), ("K0", 0))
+
+        def pens(bank, lo, e, i, h):
+            return [(S(bank, lo, lo + 128), S(m), S(x, 256 * h + o, 256 * h + o + 128)) for m, x, o in (("IBIG", e, 0), ("IBIG", e, 128), ("I1", "PN", 128 * i))]
+
+        def masks(h):
+            o = 256 * h
+            spread("KK1", o, ("MV", 0), h, S("RZ", 0, 128), start=True)
+            spread("KK1", o + 128, ("MC", 0), h, S("RZ", 0, 128))
+            if t:
+                for j in (2 * h, 2 * h + 1):
+                    lift("KK1", o, "DO", j, wg(0, 2))
+            else:
+                for lo in (0, 128):
+                    spread("KK1", o + lo, ("A2", 16 + 32 * h), h, S("I1F"))
+            spread("KK1", o + 128, ("NN", 0), h, S("BJ", 0, 128), stop=True)
+            ts(S("EO", o, o + 256), S("KK1", o, o + 256), 0.0, A.is_equal)
+
+        def chosen(h):
+            o = 128 * h
+            tt(S("RI", o, o + 128), S(ko[h][0], ko[h][1], ko[h][1] + 128), S("KC", o, o + 128), A.min)
+            ts(S("RJ", o, o + 128), S("RI", o, o + 128), 4095, A.bitwise_and)
+            cp(S("RF", o, o + 128), S("RJ", o, o + 128))
+            mm([(S("UE", o, o + 128), S("RF", o, o + 128), S("I1F"))], True, True)
+            act(S("NL", o, o + 128), S("UE", o, o + 128))
+            cp(IND(S("L"), u(48 + 8 * h, 8)), S("NL", o, o + 128))
+
+        for h in range(2):
+            names(t, h, BU, S("L", 0, W), "A2", "RU2", "OU", None, "DO", 256, CO[h], lambda lo, hi: None)
+            masks(h)
+        if t == 0:
+            for d, r4 in enumerate((R4A, R4B)):
+                act(S("M", V + d * GH, V + (d + 1) * GH), S("LM", d * GH, (d + 1) * GH), bias=r4)
+        if not last:
+            pieces(S("MZ", 0, LN), S("MV", 0, LN), zz, S("PW", 256, 512))
+            me, le, ml, ll = "ME%d" % t, "LE%d" % t, "ML%d" % t, "LL%d" % t
+            for j in range(2):
+                act(S("SG"), S("CN"), bias=c(18 + j), scale=-1.0, func=F.Sign, accum=S("q", 192 + j, 193 + j))
+            ts(u(96, 2), S("q", 192, 194), 0.5, A.mult, 128.0, A.add)
+            ts(u(98, 2), S("q", 192, 194), 0.5, A.mult, 128.0, A.add)
+            s2 = u(96, 2)
             for j, src in enumerate(("MV", "MB", "MV", "MB")):
                 act(S("MS", 32 * j, 32 * j + 32), IND(S(src), s2))
-            act(S(me, 0, 32), IND(S("ZZ", 0, 272), s2))
-            act(S(me, 168, 200), IND(S("ZZ", 0, 272), s2))
+            act(S(me, 0, 32), IND(S("ZZ", 384, 656), s2))
+            act(S(me, 168, 200), IND(S("ZZ", 384, 656), s2))
             act(S(me, 32, 96), IND(S("MZ"), SU), bias=R4A)
             act(S(me, 104, 168), IND(S("MZ"), SU), bias=R4B)
             fold(S("PW", 0, 8), "SN", "MS", 0, 8, True, True)
@@ -545,14 +662,10 @@ def build(g, core, T, topo):
             tt(S(me, 96, 104), S("q", 16, 24), D8, A.add)
             exchange([S(me, 0, 100), S(me, 100, 200)], [S(le, 0, 100), S(le, 100, 200)], "te%d" % t, "re%d" % t, 2500)
             mm([(S("PW", 0, 32), S("RN"), S("MS", 0, 32))], True, True)
-            act(S("VR", 0, 32), S("PW", 0, 32))
-            act(S("VR", 32, 64), S("PW", 0, 32))
-            act(S("VR", 64, 96), S("PW", 0, 32), bias=float(V))
-            act(S("VR", 96, 128), S("PW", 0, 32), bias=float(V + GH))
-            ct = S("CF", 16 * t, 16 * t + 16)
+            act(S("VR"), S("PW", 0, 32))
             y = [w(j) for j in range(32, 42)]
-            ts(y[0], ct, float(V), A.is_lt)
-            tt(y[1], ct, VF, A.subtract)
+            ts(y[0], CT, float(V), A.is_lt)
+            tt(y[1], CT, VF, A.subtract)
             tt(y[2], y[0], y[1], A.mult)
             ts(OWN, BF, float(V), A.is_lt)
             tt(y[3], BF, VF, A.subtract)
@@ -563,63 +676,61 @@ def build(g, core, T, topo):
             tt(y[8], y[6], y[7], A.mult)
             tt(y[9], y[8], VF, A.add)
             cp(PU, y[9])
-            scat(S(mname), OJ, S("MZ", 0, LN))
-            scat(S(mname), OB, S("MZ", 0, LN))
+            scat(S("M"), OJ, S("MZ", 0, LN))
+            scat(S("M"), OB, S("MZ", 0, LN))
+            for e in range(t - 1, -1, -1):
+                act(S("FG", 0, LN), IND(S("M"), S("fw", 40 * e, 40 * e + 16)))
+                scat(S("M"), S("fw", 40 * e + 20, 40 * e + 36), S("FG", 0, LN))
             cp(GU, S(le, 96, 104))
             for d, lo in ((0, 32), (1, 104)):
-                scat(S(mname, V, WD), u(136 + 4 * d, 4), S(le, lo, lo + 64))
+                scat(S("M", V, WD), u(104 + 4 * d, 4), S(le, lo, lo + 64))
+            if t < RO - 2:
+                for d in range(2):
+                    cp(S("fw", 40 * t + 16 + 2 * d, 40 * t + 18 + 2 * d), S(le, 96 + 4 * d, 98 + 4 * d))
+                    cp(S("fw", 40 * t + 36 + 2 * d, 40 * t + 38 + 2 * d), S(le, 98 + 4 * d, 100 + 4 * d))
         else:
             act(S("MZ", 0, LN), S("MV", 0, LN))
-            scat(S(mname), OB, S("MZ", 0, LN))
-            act(S("FG"), IND(S(mname, 0, V), S("FW", 0, 64)))
-            for h, bank in enumerate(("PA", "PB")):
-                mm([(S(bank, 0, 512, 1, (0, 8)), S("wb", 48, 56), S("FG", 512 * h, 512 * h + 512))], True, True)
+            scat(S("M"), OB, S("MZ", 0, LN))
+            act(S("MH"), IND(S("M", 0, V), S("FW")))
+            for h, bank in enumerate(("PA", "PW")):
+                mm([(S(bank, 0, 512, 1, (0, 8)), wg(0), S("MH", 512 * h, 512 * h + 512))], True, True)
                 act(S("YF", 512 * h, 512 * h + 512, 1, (0, 8)), S(bank, 0, 512, 1, (0, 8)))
             dma("s", lambda: T.yf[:], lambda: T.YF[0:8, :], "of", 2500, ins=[S("YF")])
         for j in range(4):
-            if j >= OFF2[t]:
-                far("D2", "OU", "ZZ", j, 4)
+            kk, lo = ko[j // 2]
+            if j == 2:
+                mm([(S(kk, 0, 128), S("BDC"), S("ONE", 0, 128))], True, False)
+            if j == 3:
+                mm(pens(kk, lo, "EO", 1, 1), False, False)
+            if t:
+                far("D2", "OU", "ZZ", 8 * j, 8 * j + 8, 4)
+            elif j in OFF2:
+                over("D2", "DO", j)
             else:
-                over("D2", "OU", "DO" if t == 0 else None, j)
-            if j < 3:
-                quarter("PKO", "SA", "D2", j)
-                quarter("PKO", mfam if j >= OFF2[t] else pfam, "DO", j)
-        mm([(S("PKO", 0, 192), S("IBIG"), S(x, 0, 192)) for x in ("EQ3", "EQ4", "NJT")], False, True)
-        if t == 0:
-            tt(S("ZS", 0, 192), S("PKO", 0, 192), S("OF", 0, 192), A.add)
-            tt(S("RI", 0, 192), S("ZS", 0, 192), S("KC", 0, 192), A.min)
-            mm([(S("PO", 0, 64), S("I1F"), S("OF", 192, 256))], True, False)
-        else:
-            tt(S("RI", 0, 192), S("PKO", 0, 192), S("KC", 0, 192), A.min)
-        ts(S("RJ", 0, 192), S("RI", 0, 192), 4095, A.bitwise_and)
-        fold(S("PO", 0, 64), mfam, "DO", 3072, 64, t > 0, True)
-        act(S("KT", 0, 64), S("PO", 0, 64))
-        mm([(S("PC", 0, 64), S("BDC"), S("ONE", 0, 64))] + [(S("PC", 0, 64), S("IBIG"), S(x, 192, 256)) for x in ("EQ3", "EQ4", "NJT")], True, False)
-        fold(S("PC", 0, 64), "SA", "D2", 3072, 64, False, True)
-        tt(S("KT", 64, 128), S("PC", 0, 64), S("KT", 0, 64), A.add)
-        tt(S("RI", 192, 256), S("KT", 64, 128), S("KC", 192, 256), A.min)
-        ts(S("RJ", 192, 256), S("RI", 192, 256), 4095, A.bitwise_and)
-        cp(S("Y"), IND(S("RJ"), ORET))
-        turn("Y", "Z1")
-        (act if OPT[0] else cp)(S("NL", 0, LN), IND(S("Z1"), OSEL))
-        cp(IND(S("L"), OL), S("NL", 0, LN))
+                near("D2", "DO", 8 * j, 8 * j + 8)
+            lift(kk, lo, "D2", j, wg(8))
+            lift(kk, lo, "DO", j, wg(9 if t else 12 if j in OFF2 else 11), stop=t > 0 and j == 3)
+            if t == 0 and j % 2:
+                spread(kk, lo, ("A2", 16 + 32 * (j // 2)), j // 2, S("I1F"), stop=j == 3)
+            if j == 1:
+                mm(pens(kk, 0, "EU", 0, 0) + pens(kk, 128, "EU", 0, 1) + pens(kk, lo, "EO", 1, 0), False, True)
+                tt(S("KC"), S(kk, 0, 256), S("CL"), A.min)
+                chosen(0)
+        chosen(1)
         cp(IND(S("X"), OJ), zz)
         if last:
             break
         for d, lo in ((0, 0), (1, 168)):
-            cp(IND(S("X", V, WD), u(136 + 4 * d, 2)), S(le, lo, lo + 32))
-        ts(S("q", 0, 64), IND(S("NL"), SU), float(GH), A.is_lt)
-        tt(S("q", 64, 128), IND(S("NL"), SU), S("VR", 0, 64), A.subtract)
-        tt(S("q", 128, 192), S("q", 0, 64), S("q", 64, 128), A.mult)
-        tt(S(ml), S("q", 128, 192), S("VR", 64, 128), A.add)
-        exchange([S(ml, 0, 32), S(ml, 32, 64)], [S(ll, 0, 32), S(ll, 32, 64)], "tm%d" % t, "rm%d" % t, 2500)
-        lanes(S(mname, 0, V))
-        if t > 0:
-            nxt = "M1" if mname == "M0" else "M0"
-            act(S(nxt, 0, V), IND(S(mname, 0, V), S("FW", 0, 64)))
-            act(S(nxt, V, V + GH), IND(S(mname, V, W), S("FW", 64, 120)))
-            (cp if OPT[3] else act)(S(nxt, V + GH, W), IND(S(mname, V, W), S("FW", 120, 176)))
-            mname = nxt
+            cp(IND(S("X", V, WD), u(104 + 4 * d, 2)), S(le, lo, lo + 32))
+        ts(S("q", 0, 32), IND(S("NL"), s2), float(GH), A.is_lt)
+        tt(S("q", 64, 96), IND(S("NL"), s2), S("VR"), A.subtract)
+        tt(S("q", 128, 160), S("q", 0, 32), S("q", 64, 96), A.mult)
+        tt(S(ml), S("q", 128, 160), S("VR"), A.add)
+        exchange([S(ml)] * 2, [S(ll, 0, 32), S(ll, 32, 64)], "tm%d" % t, "rm%d" % t, 2500)
+        lanes(t + 1)
+        for e in range(t - 1, -1, -1):
+            act(S("FG", 256, 320), IND(S("M", V, WD), S("fw", 40 * e + 16, 40 * e + 20)))
+            scat(S("M", V, WD), S("fw", 40 * e + 36, 40 * e + 40), S("FG", 256, 320))
     dma("s", lambda: T.yl[:], lambda: T.L[:, 0:V], "ol", 4000, ins=[S("L", 0, V)])
     dma("a", lambda: T.yx[:], lambda: T.X[:, 0:V], "ox", 3000, ins=[S("X", 0, V)])
     return nodes, eng
@@ -637,7 +748,8 @@ def order(nodes):
             for (j, lo, hi, w2) in hist.get(y[0], ()):
                 meet = lo < y[2] and y[1] < hi
                 if SCRATCH[y[0]][0] == "sbuf" and (nodes[j]["sem"] or x["sem"]) and wr and w2:
-                    meet = lo - 8 < y[2] and y[1] - 8 < hi
+                    q = 8 if SCRATCH[y[0]][2] in ("bfloat16", "uint16") else 4
+                    meet = lo // q * q < y[2] and y[1] // q * q < hi
                 if bank and (nodes[j]["e"] != x["e"] or wr or w2):
                     d[j] = d.get(j, False) or (w2 and not wr and meet)
                 elif meet and (wr or w2):
@@ -656,7 +768,7 @@ def order(nodes):
     for i in range(n):
         for j in set(list(deps[i]) + nodes[i]["after"]):
             same = nodes[i]["e"] == nodes[j]["e"] and not deps[i].get(j, False)
-            dl = nodes[j]["lat"] + (0.0 if same else HOP)
+            dl = (nodes[j]["lat"] if j in deps[i] or nodes[i]["e"] == "R" else 0.0) + (0.0 if same else HOP)
             pre[i].append((j, dl))
             suc[j].append((i, dl))
     cost = [max(1.0, x["cost"]) for x in nodes]

@@ -5,16 +5,17 @@ V, GH, W, LN, RO = 1024, 896, 2816, 256, 4
 WD = W + LN + 128
 BIG = float(2 ** 26)
 CLAMP = float(4080 * 4096)
-MAGIC = float(3 * 2 ** 22)
-NX = 4
-SUB = [(), (1,), (1,), (1,)]
-RELU = (1,)
-OPT = dict(z="v", kt="a", vf="a")
+NX = (2, 4)
+SUB = [(), (2,), (2,), (2,)]
+RELU = (2,)
+PLAIN = [(), (3,), (3,), (3,)]
+OPT = dict(kt="a", vf="a", rows="vv", bd="a", m="v", mg="aa", wg="a")
 CH0 = [[(4, "v"), (4, "a"), (4, "a"), (4, "a")], [(4, "a")] * 4]
 CH = [[(4, "v"), (4, "a"), (8, "a")], [(8, "a"), (8, "a")]]
+CO0 = [[(4, "v"), (4, "a"), (8, "a")], [(4, "v"), (4, "a"), (8, "a")]]
 CO = [[(8, "a"), (8, "a")], [(8, "a"), (8, "a")]]
-OFF1, OFF2 = (3,), ()
-HOP, PEC, PASSES, AMP, SPAN = 150.0, 0.55, 4000, 1000.0, 9000.0
+OFF1, OFF2 = (), ()
+HOP, PEC, PASSES, AMP, SPAN = 150.0, 0.55, 5000, 2000.0, 3500.0
 PLAN = []
 
 SCRATCH = {}
@@ -25,15 +26,15 @@ def _buf(names, n, dtp, where="sbuf"):
         SCRATCH[x] = (where, [128, n], dtp)
 
 
-_buf("X", WD, "bfloat16")
-_buf("NB", W, "bfloat16")
+_buf("X NB", WD, "bfloat16")
 _buf("MH ZZ XV", V, "bfloat16")
 _buf("L M B", WD, "float32")
 _buf("HI", V, "int32")
 _buf("GA", GH, "bfloat16")
-_buf("GB", GH, "float32")
-_buf("GL", GH, "uint16")
-_buf("LG", 2 * GH, "uint16")
+_buf("GL", GH, "float16")
+_buf("LG", 2 * GH, "float16")
+_buf("IF", 128, "float16")
+_buf("ZS ZT", 256, "float16")
 _buf("LM", 2 * GH, "bfloat16")
 _buf("DC DO D0 D1 D2 E XC", 4096, "bfloat16")
 _buf("ROWS", 2048, "bfloat16")
@@ -47,8 +48,8 @@ _buf("NL MB MZ", 272, "float32")
 _buf("A1 A2 FG", 320, "float32")
 _buf("Z", 576, "float32")
 _buf("MV", 272, "bfloat16")
-_buf("CF KC VT CL ZS ZT RF", 256, "float32")
-_buf("RZ PW2 I256 CR EQ BB BK BY TH MC NN CN SG", 256, "bfloat16")
+_buf("CF KC VT CL RF", 256, "float32")
+_buf("RZ PW2 I256 CR EQ BB BK BY TH MC NN CN", 256, "bfloat16")
 _buf("RI RJ", 256, "int32")
 _buf("RU CU RU2 OU PR", 256, "uint16")
 _buf("FW", 64, "uint16")
@@ -61,17 +62,18 @@ _buf("wi", 48, "int32")
 _buf("wb", 32, "bfloat16")
 _buf("u", 128, "uint16")
 _buf("cu", 32, "uint16")
-_buf("MS", 128, "bfloat16")
-_buf("VR", 32, "float32")
+_buf("MS", 64, "bfloat16")
 _buf("q", 200, "float32")
 _buf("YF", V, "float32")
-_buf("ME0 ME1 ME2 LE0 LE1 LE2", 200, "float32")
+_buf("ME0 ME1 ME2", 164, "float32")
+_buf("LE0 LE1 LE2", 200, "float32")
 _buf("ML0 ML1 ML2", 32, "float32")
 _buf("LL0 LL1 LL2", 64, "float32")
 _buf("PC K0 UE UX KK0 KK1 PA PW", 512, "float32", "psum")
 
-SEMAPHORES = (["sv", "sa", "sp", "sg", "dx", "dn", "dm", "dh", "dl", "dt", "ox", "ol", "of", "tx", "rx", "tl", "rl", "tp", "rp"]
+SEMAPHORES = (["sv", "sa", "sp", "sg", "dx", "dy", "dn", "dm", "dh", "dl", "dt", "ox", "ol", "of", "tx", "rx", "tl", "rl", "tp", "rp"]
               + ["%s%d" % (a, t) for a in ("te", "re", "tm", "rm") for t in range(RO - 1)])
+SHORT = ("bfloat16", "uint16", "float16")
 
 
 def S(name, lo=0, hi=None, st=1, p=None):
@@ -107,7 +109,7 @@ def build(g, core, T, topo):
     def psum(x):
         return x[0] != "*" and SCRATCH[x[0]][0] == "psum"
 
-    def node(e, cost, fn, outs, ins, lat=0, sem=None, inc=1, after=()):
+    def node(e, cost, fn, outs, ins, lat=0, sem=None, inc=1, after=(), free=False):
         rd, wr = [], []
         for x in ins:
             if isinstance(x, tuple):
@@ -118,7 +120,7 @@ def build(g, core, T, topo):
                 rd.append(x[2])
             else:
                 wr.append(x)
-        nodes.append(dict(e=e, cost=cost, fn=fn, rd=rd, wr=wr, lat=lat, sem=sem, inc=inc, after=list(after)))
+        nodes.append(dict(e=e, cost=cost, fn=fn, rd=rd, wr=wr, lat=lat, sem=sem, inc=inc, after=list(after), free=free))
         return len(nodes) - 1
 
     def vcost(out, i0, base):
@@ -130,7 +132,7 @@ def build(g, core, T, topo):
         return max(64, base * n) + 10
 
     def narrow(*xs):
-        return 0.5 if all(dty(x) in ("bfloat16", "uint16") for x in xs) else 1.0
+        return 0.5 if all(dty(x) in SHORT for x in xs) else 1.0
 
     def cp(out, i0):
         return node("v", vcost(out, i0, narrow(out, i0)), lambda: g.vector.tensor_copy(ap(out), ap(i0)), [out], [i0])
@@ -170,17 +172,20 @@ def build(g, core, T, topo):
                     lambda: g.scalar.activation(ap(out), ap(i0), func, **{k: ap(x) for k, x in kw.items()}),
                     [out] + ([] if accum is None else [accum]), [i0, bias, scale])
 
+    def times(e, out, i0, wt):
+        return act(out, i0, scale=wt) if e == "a" else ts(out, i0, wt, A.mult)
+
     def scat(win, off, src):
         return act(IND(win, off), src, func=F.Silu)
 
-    def mm(items, start, stop):
+    def mm(items, start, stop, free=False, after=()):
         def fn():
             r = None
             for j, (o, l, x) in enumerate(items):
                 r = g.tensor.matmul(ap(o), ap(l), ap(x), start and j == 0, stop and j == len(items) - 1)
             return r
         cost = sum(PEC * max(64, cnt(x)) * (4 if dty(x) == "float32" else 1) for o, l, x in items)
-        return node("p", cost, fn, [o for o, l, x in items], [y for o, l, x in items for y in (l, x)])
+        return node("p", cost, fn, [o for o, l, x in items], [y for o, l, x in items for y in (l, x)], after=after, free=free and not (start or stop))
 
     def sel(fam, r):
         return S(fam, 15 - r, 143 - r)
@@ -228,8 +233,11 @@ def build(g, core, T, topo):
 
     def wg(j, n=1):
         return S("WG", 8 * j, 8 * (j + n))
+
+    def fill(out, val):
+        return iota(out, [[0, cnt(out)]], val, after=[sent])
     ROW, GRP, PAR, PID, G15, WN, WS, WM, W014, WH, R4A, R4B, TMP, TMP2, WP, TC2, TC3 = [c(j) for j in range(17)]
-    DUMP, D8, CD8, G8, TH8, T16a, I16 = c(64, 32), c(112, 8), c(120, 8), c(128, 8), c(136, 8), c(144, 16), c(192, 16)
+    DUMP, D8, G8, TH8, T16a, I16 = c(64, 32), c(112, 8), c(128, 8), c(136, 8), c(144, 16), c(192, 16)
     OENT, OBC = S("cu", 0, 8), S("cu", 16, 32)
     first = [iota(ci(0), [[0, 1]], 0, 1), iota(S("IU"), [[1, 144]], 0), iota(S("IG"), [[1, 8], [0, 16]], 0)]
     iota(S("I256"), [[32, 256]], 0)
@@ -256,14 +264,18 @@ def build(g, core, T, topo):
     tt(WH, mk(2), mk(3), A.subtract)
     ts(R4A, mk(4), 32.0 * V / 128, A.mult)
     ts(R4B, mk(4), 32.0 * (V + GH) / 128, A.mult)
-    for fam, wt in (("SN", WN), ("SA", 8192.0), ("SX", -4096.0), ("SM", WM), ("SP", WP), ("S32", 32.0), ("Z0", mk(0))):
-        ts(S(fam), S("IU"), G15, A.is_equal, wt, A.mult)
-    for m, wt in (("RN", WN), ("BDC", -float(2 ** 20)), ("BD1", 1.0)):
-        ts(S(m), S("IG"), GRP, A.is_equal, wt, A.mult)
-    for m, wt in (("IBIG", BIG), ("I1", 1.0), ("I1F", 1.0), ("IM1", -1.0), ("I24", float(2 ** 24)), ("I014", W014), ("IH", WH),
-                  ("I13", 8192.0), ("IM13", -8192.0)):
-        ts(S(m), S("IU", 0, 128), PID, A.is_equal, wt, A.mult)
-    ts(S("RZ", 0, 128), S("RN"), -1.0, A.mult)
+    ts(S("S32"), S("IU"), G15, A.is_equal, 32.0, A.mult)
+    for fam, wt in (("SN", WN), ("SM", WM), ("SP", WP), ("Z0", mk(0))):
+        ts(S(fam), S("S32"), wt, A.mult, 1.0 / 32, A.mult)
+    for fam, wt in (("SA", 256.0), ("SX", -128.0)):
+        times("a", S(fam), S("S32"), wt)
+    ts(S("BD1"), S("IG"), GRP, A.is_equal)
+    ts(S("I1"), S("IU", 0, 128), PID, A.is_equal)
+    for e, m, base, wt in (("v", "RN", "BD1", WN), ("a", "BDC", "BD1", -float(2 ** 20)), ("v", "IBIG", "I1", BIG), ("a", "I1F", "I1", 1.0),
+                           ("a", "IM1", "I1", -1.0), ("a", "I24", "I1", float(2 ** 24)), ("v", "I014", "I1", W014), ("v", "IH", "I1", WH),
+                           ("a", "I13", "I1", 8192.0), ("a", "IM13", "I1", -8192.0), ("v", "IF", "I1", 1.0)):
+        times(e, S(m), S(base), wt)
+    times("a", S("RZ", 0, 128), S("RN"), -1.0)
     mset(S("RZ", 128, 256), 0.0)
     ts(S("IMG"), S("IH"), 1.5 * 2 ** 32, A.mult)
     ts(S("IMH"), S("IH"), -1.5 * 2 ** 32, A.mult)
@@ -273,7 +285,7 @@ def build(g, core, T, topo):
     ts(S("MT"), sel("Z0", 0), 1.0 / 128, A.mult)
     tt(S("WBH"), S("MT"), sel("Z0", 1), A.subtract)
     for r in range(16):
-        ts(S("ROWS", 128 * r, 128 * r + 128), S("BD1"), mk(r), A.mult)
+        times(OPT["rows"][r % 2], S("ROWS", 128 * r, 128 * r + 128), S("BD1"), mk(r))
     mset(c(32, 16), 0.5)
     scan(S("PW2", 0, 16), c(32, 16), c(32, 16), 131072.0, A.mult, A.max)
     for n in (16, 32, 64, 128):
@@ -281,34 +293,29 @@ def build(g, core, T, topo):
     tt(c(48, 16), S("PW2", 0, 16), c(224, 16), A.mult)
     total(c(21), c(48, 16))
     ts(S("BDW"), S("BD1"), c(21), A.mult, 0.5, A.mult)
-    ts(S("BDB"), S("BD1"), 65536.0, A.mult)
-    ts(S("BY", 0, 128), S("BD1"), -1.0, A.mult)
-    cp(S("BY", 128, 256), S("BD1"))
-    ts(S("BJ", 0, 128), S("BD1"), 1.0 / 16, A.mult)
-    ts(S("BJM"), S("BD1"), -1.0 / 16, A.mult)
-    ts(S("BJ", 128, 256), S("BD1"), 1.0 / 8, A.mult)
-    ts(S("BJ", 256, 384), S("BD1"), 1.0 / 8, A.mult)
+    for m, wt in ((S("BDB"), 65536.0), (S("BY", 0, 128), -1.0), (S("BY", 128, 256), 1.0), (S("BJ", 0, 128), 1.0 / 16), (S("BJM"), -1.0 / 16),
+                  (S("BJ", 128, 256), 1.0 / 8), (S("BJ", 256, 384), 1.0 / 8)):
+        times(OPT["bd"], m, S("BD1"), wt)
     ts(G8, S("IU", 0, 8), GRP, A.is_equal)
-    ts(TMP, WS, 1.0 / 4096, A.mult)
-    ts(TMP2, WS, -1.0 / 4096, A.mult)
-    for j, wt in enumerate((WN, WN, TMP, TMP2, -1.0, 1.0, 2.0, -2.0, 8192.0, WM, WP, -4096.0, 4096.0, WN, WN, TMP2, TMP)):
-        ts(wg(j), G8, wt, A.mult)
+    ts(c(30), WS, 1.0 / 4096, A.mult)
+    ts(c(31), WS, -1.0 / 4096, A.mult)
+    for j, wt in enumerate((WN, WN, c(30), c(31), c(30), -1.0, 1.0, 2.0, -2.0, 8192.0, WM, WP, -4096.0, 4096.0)):
+        times(OPT["wg"], wg(j), G8, wt)
     mset(S("ONE"), 1.0)
     for b in ("MV", "MB"):
-        mset(S(b, 256, 272), 128.0)
+        fill(S(b, 256, 272), 128)
     for b in ("MZ", "NL"):
-        mset(S(b, 256, 272), 0.0)
-    for b in ("A1", "A2"):
-        for lo, hi in ((0, 16), (144, 176), (304, 320)):
-            mset(S(b, lo, hi), 0.0)
-    mset(S("M", W, WD), 0.0)
-    mset(S("B", V, V + 8), 128.0)
+        fill(S(b, 256, 272), 0)
+    for lo, hi in ((0, 16), (144, 176), (304, 320)):
+        mset(S("A1", lo, hi), 0.0)
+        fill(S("A2", lo, hi), 0)
+    fill(S("M", W, WD), 0)
+    fill(S("B", V, W), 128)
     ts(T16a, I16, 16.0, A.mult, ROW, A.add)
     ts(c(64, 16), T16a, float(W), A.add)
     ts(c(80, 16), T16a, float(W), A.add)
     ts(D8, c(144, 8), float(W - V + LN), A.add)
-    ts(c(120, 4), c(112, 4), -1.0, A.mult)
-    ts(c(124, 4), c(116, 4), -1.0, A.mult, float(GH), A.add)
+    ts(c(120, 4), c(116, 4), -float(GH), A.add)
     ts(c(18, 2), c(144, 2), 0.5, A.add)
     ts(ci(4), ci(0), 7, A.bitwise_and)
     ts(ci(5), ci(1), 3, A.arith_shift_right)
@@ -333,15 +340,14 @@ def build(g, core, T, topo):
     ts(c(29), mk(2), -16384.0, A.mult)
     tt(TC2, c(29), c(23), A.subtract)
     tt(TC3, c(29), c(23), A.add)
-    ts(S("TH", 0, 128), S("BD1"), TC2, A.mult)
-    ts(S("TH", 128, 256), S("BD1"), TC3, A.mult)
+    times("a", S("TH", 0, 128), S("BD1"), TC2)
+    times("a", S("TH", 128, 256), S("BD1"), TC3)
 
     cp(S("L", 0, V), S("HI"))
     act(S("GA"), S("L", 0, GH), bias=float(GH), scale=-1.0, func=F.Relu)
     for bank, lo, hi in (("KK0", 0, 512), ("KK1", 512, GH)):
         mm([(S(bank, 0, hi - lo), S("RN"), S("NB", lo, hi)), (S(bank, 0, hi - lo), S("IBIG"), S("GA", lo, hi))], True, True)
-        tt(S("GB", lo, hi), S(bank, 0, hi - lo), S("L", lo, hi), A.min)
-    cp(S("GL"), S("GB"))
+        tt(S("GL", lo, hi), S(bank, 0, hi - lo), S("L", lo, hi), A.min)
     exchange([S("GL")] * 2, [S("LG", 0, GH), S("LG", GH, 2 * GH)], "tl", "rl", 6000)
     for lo in (0, 512):
         act(S("HB"), S("L", lo, lo + 512), scale=32.0)
@@ -355,7 +361,7 @@ def build(g, core, T, topo):
 
     for lo in (0, 512):
         pieces(S("MH", lo, lo + 512), S("NB", lo, lo + 512), S("X", lo, lo + 512), S("KK1"))
-    cp(S("M", 0, V), S("MH"))
+    (act if OPT["m"] == "a" else cp)(S("M", 0, V), S("MH"))
     exchange([S("MH", 0, GH)] * 2, [S("LM", 0, GH), S("LM", GH, 2 * GH)], "tp", "rp", 6000)
 
     def w(j, n=1):
@@ -363,8 +369,12 @@ def build(g, core, T, topo):
 
     def u(j, n=16):
         return S("u", j, j + n)
-    VF, VA, AW, VM, BF, JN, G1, J1, OWN, VL, CT = [w(j) for j in range(11)]
-    PU, VU, BU, OL, BBU, BC, SU, GU = u(0), u(16), u(32), u(48), u(64), u(80), u(96, 4), u(104, 8)
+
+    def fw(t, lo, n):
+        return S("fw", 40 * t + lo, 40 * t + lo + n)
+    VF, VA, AW, VM, JN, G1, J1, VL = [w(j) for j in range(8)]
+    BF, CT = w(11), w(12)
+    PU, VU, BU, OL, BBU, SU = u(0), u(16), u(32), u(48), u(64), u(96, 4)
     NJ, TL = S("wb", 0, 16), S("wb", 16, 32)
 
     def pair(b):
@@ -398,13 +408,15 @@ def build(g, core, T, topo):
         mm([(S("PA", 0, LN), S("BJM"), S("PW2"))], True, False)
         for q in range(0, 16, 4):
             mm([(S("PA", 16 * s, 16 * s + 16), S("BDW"), S("E", 272 * s, 272 * s + 16)) for s in range(q, q + 4)]
-               + [(S("PA", 16 * s + 16, LN), S("BDB"), S("E", 272 * s + 16, 256 * s + 256)) for s in range(q, min(q + 4, 15))], False, q == 12)
+               + [(S("PA", 16 * s + 16, LN), S("BDB"), S("E", 272 * s + 16, 256 * s + 256)) for s in range(q, min(q + 4, 15))], False, q == 12, True)
         act(S("CR"), S("PA", 0, LN), bias=1.0, func=F.Relu)
         fold(S("PW", 16, 32), "SA", "CR", 0, 16, True, True)
         tt(VA, S("PW", 16, 32), VF, A.add)
         tt(VM, VA, c(64, 16), A.min)
         cp(OL, VM)
-        ts(AW, VM, float(V), A.is_lt)
+        if t < RO - 1:
+            ts(AW, VM, float(V), A.is_ge, -16384.0, A.mult)
+            ts(AW, AW, -8192.0, A.add)
         act(S("VT"), IND(VF, OBC))
 
     def names(t, h, off, lwin, abuf, raw, outu, outf, dm, pn, chunks, each):
@@ -412,12 +424,9 @@ def build(g, core, T, topo):
         act(S(abuf, a + 16, a + 144), IND(lwin, S(off[0], off[1] + 8 * h, off[1] + 8 * h + 8)))
         tr(S("Z", z, z + 128), S(abuf, a + 16, a + 144))
         tr(S("Z", z + 128, z + 288), S(abuf, a, a + 160))
-        if t == 0:
-            cp(S(outu, o, o + 128), IND(S("Z", z, z + 288), OENT))
-            if outf:
-                act(S(outf, o, o + 128), IND(S("Z", z, z + 288), OENT))
-        else:
-            cp(S(raw, o, o + 128), IND(S("Z", z, z + 288), OENT))
+        cp(S(raw if t else outu, o, o + 128), IND(S("Z", z, z + 288), OENT))
+        if t == 0 and outf:
+            act(S(outf, o, o + 128), IND(S("Z", z, z + 288), OENT))
         k = 16 * h
         for n, e in chunks:
             get = cp if e == "v" else act
@@ -434,9 +443,9 @@ def build(g, core, T, topo):
         for k in range(lo, hi, n):
             tt(S(buf, 128 * k, 128 * (k + n)), IND(S("X", 0, W), S(offs, 8 * k, 8 * (k + n))), rep(y, k // 16, n), A.max)
 
-    def near(buf, src, lo, hi):
+    def near(buf, src, lo, hi, y=None):
         for k in range(lo, hi, 2):
-            tt(S(buf, 128 * k, 128 * k + 256), S(src, 128 * k, 128 * k + 256), S("PC", 256 * (k // 16), 256 * (k // 16) + 256), A.max)
+            tt(S(buf, 128 * k, 128 * k + 256), S(src, 128 * k, 128 * k + 256), y or S("PC", 256 * (k // 16), 256 * (k // 16) + 256), A.max)
 
     def less(lo, hi, n):
         for k in range(lo, hi, n):
@@ -457,36 +466,44 @@ def build(g, core, T, topo):
             mm([(S("K0"), S("I1"), rep("ZZ", j // 2, 4)), (S("K0"), S("IM1"), S(src, x, x + 512))], True, True)
             act(S(buf, x, x + 512), S("K0"), func=F.Relu)
 
-    def lift(bank, lo, src, j, wts, stop=False):
+    def lift(bank, lo, src, j, wts, stop=False, after=()):
         n = cnt(wts)
-        return mm([(S(bank, lo + k % 16, lo + k % 16 + 16 * (n - 1) + 1, 16), S(src, 128 * k, 128 * k + 128), wts) for k in range(8 * j, 8 * j + 8)], False, stop)
+        return mm([(S(bank, lo + k % 16, lo + k % 16 + 16 * (n - 1) + 1, 16), S(src, 128 * k, 128 * k + 128), wts) for k in range(8 * j, 8 * j + 8)],
+                  False, stop, True, after)
 
-    def spread(bank, lo, src, h, wts, start=False, stop=False):
-        return mm([(S(bank, lo, lo + cnt(wts)), S(src[0], src[1] + 128 * h, src[1] + 128 * h + 128), wts)], start, stop)
+    def spread(bank, lo, src, h, wts, start=False, stop=False, free=True, after=()):
+        return mm([(S(bank, lo, lo + cnt(wts)), S(src[0], src[1] + 128 * h, src[1] + 128 * h + 128), wts)], start, stop, free, after)
 
     lanes(0)
     for t in range(RO):
         last = t == RO - 1
-        mcur = S("NB") if t == 0 else S("M", 0, W)
+        mcur = S("NB", 0, W) if t == 0 else S("M", 0, W)
         cnum = "CF" if t == 0 else "PC"
-        OJ, OB = S("fw", 40 * t, 40 * t + 16), S("fw", 40 * t + 20, 40 * t + 36)
+        OJ, OB = fw(t, 0, 16), fw(t, 16, 16)
+        for h in range(2):
+            spread("UX", 256 * h, ("ONE", 0), 0, S("TH"), start=h == 0, free=False)
+            spread("UE", 256 * h, ("MV", 0), h, S("RZ"), start=h == 0, free=False)
         for h in range(2):
             act(rep("XV", h, 1), IND(S("X", 0, V), u(16 + 8 * h, 8)))
-            repeat("XV", h, NX if t else 2)
+            repeat("XV", h, NX[h] if t else 2)
             if t == 0:
                 mm([(S("PC", 256 * h, 256 * h + 256), S("I1"), rep("XV", h, 2))], True, True)
-            spread("UX", 256 * h, ("ONE", 0), 0, S("TH"), start=h == 0)
             spread("UX", 256 * h, pair("XV"), h, S("BY"))
-            spread("UE", 256 * h, ("MV", 0), h, S("RZ"), start=h == 0)
 
             def step1(lo, hi):
                 sub = lo // 8 in SUB[t]
                 if t == 0:
                     near("D0", "DC", lo, hi)
+                elif lo // 8 in PLAIN[t]:
+                    if lo % 8 == 0:
+                        mm([(S("PW", 256, 512), S("I1"), rep("XV", h, 2))], True, True)
+                    for k in range(lo, hi, 4):
+                        act(S("XC", 128 * k, 128 * k + 512), IND(S("X", 0, W), S("CU", 8 * k, 8 * k + 32)))
+                        near("D0", "XC", k, k + 4, S("PW", 256, 512))
                 elif sub:
-                    less(lo, hi, min(NX, hi - lo))
+                    less(lo, hi, min(NX[h], hi - lo))
                 else:
-                    far("D0", "CU", "XV", lo, hi, min(NX, hi - lo))
+                    far("D0", "CU", "XV", lo, hi, min(NX[h], hi - lo))
                 if hi % 8:
                     return
                 j = hi // 8 - 1
@@ -495,7 +512,7 @@ def build(g, core, T, topo):
                 tt(S("EQ", 64 * j, 64 * j + 64), S(cnum, 64 * j, 64 * j + 64), S("VT", 64 * j, 64 * j + 64), A.is_equal)
                 if t:
                     lift("UE", 256 * h, "DC", j, wg(0, 2))
-                lift("UX", 256 * h, "DC", j, wg((15 if sub else 2) if t else 4, 2))
+                lift("UX", 256 * h, "DC", j, wg((3 if sub else 2) if t else 5, 2))
                 put = act if OPT["kt"] == "a" else cp
                 if j == 3:
                     cs = S("K0", 256, 320)
@@ -511,7 +528,7 @@ def build(g, core, T, topo):
                         mm([(k0, S("I1F"), S("CF", 64 * j, 64 * j + 64))], False, True)
                 if j % 2 == 0:
                     put(S("KT", 32 * j, 32 * j + 64), k0)
-                lift("UX", 256 * h, "D0", j, wg(6, 2))
+                lift("UX", 256 * h, "D0", j, wg(7, 2))
             names(t, h, VU, S("L", 0, V), "A1", "RU", "CU", "CF", "DC", 0, CH0[h] if t == 0 else CH[h], step1)
             if t == 0:
                 for lo in (0, 128):
@@ -528,30 +545,25 @@ def build(g, core, T, topo):
             ts(S("wi", 16 + 8 * h, 24 + 8 * h), S("wi", 8 * h, 8 * h + 8), 4095, A.bitwise_and)
             cp(u(32 + 8 * h, 8), S("wi", 16 + 8 * h, 24 + 8 * h))
             if not last:
-                act(S("w", 160 + 8 * h, 168 + 8 * h), S(cnum, 128 * h + 8 * t, 128 * h + 8 * t + 8))
+                act(S("w", 192 + 8 * h, 200 + 8 * h), S(cnum, 128 * h + 8 * t, 128 * h + 8 * t + 8))
         cp(BF, S("wi", 16, 32))
-        ts(BC, S("wi", 16, 32), float(V), A.min)
         if last:
+            dma("s", lambda: T.NB[:, 0:V], lambda: T.X[:, 0:V], "dy", 3000, outs=[S("NB", 0, V)], ins=[S("X", 0, V)])
             act(S("MH"), S("M", 0, V))
             fold(S("PA", 0, 64), "SN", "MH", 0, 64, True, True)
             cp(S("FW"), S("PA", 0, 64))
         if t == 0:
-            for d in range(2):
-                ts(S("L", V + d * GH, V + (d + 1) * GH), S("LG", d * GH, (d + 1) * GH), float(V + d * GH), A.add)
+            for lo in range(0, 2 * GH, GH // 2):
+                mm([(S("PA", 0, GH // 2), S("IF"), S("LG", lo, lo + GH // 2))], True, True)
+                act(S("L", V + lo, V + lo + GH // 2), S("PA", 0, GH // 2), bias=float(V + lo // GH * GH))
         else:
             for d in range(2):
                 ts(IND(S("L", V, WD), u(104 + 4 * d, 2)), S("LL%d" % (t - 1), 32 * d, 32 * d + 32), 1.0, A.mult, float(V + d * GH), A.add)
         for h in range(2):
             o = 128 * h
             tt(S("ZS", o, o + 128), IND(S("X", 0, W), u(32 + 8 * h, 8)), rep("XV", h, 1), A.add)
-            if OPT["z"] == "a":
-                act(S("ZT", o, o + 128), S("ZS", o, o + 128), scale=0.5 - 2.0 ** -11, bias=MAGIC)
-            else:
-                ts(S("ZT", o, o + 128), S("ZS", o, o + 128), 0.5 - 2.0 ** -11, A.mult, MAGIC, A.add)
-            if OPT["z"] != "v":
-                act(rep("ZZ", h, 1), S("ZT", o, o + 128), bias=-MAGIC)
-            else:
-                ts(rep("ZZ", h, 1), S("ZT", o, o + 128), -MAGIC, A.add)
+            ts(S("ZT", o, o + 128), S("ZS", o, o + 128), 0.5 - 2.0 ** -11, A.mult, 1536.0, A.add)
+            ts(rep("ZZ", h, 1), S("ZT", o, o + 128), -1536.0, A.add)
             repeat("ZZ", h, 4)
             if t == 0:
                 mm([(S("PC", 256 * h, 256 * h + 256), S("I1"), rep("ZZ", h, 2))], True, True)
@@ -559,7 +571,7 @@ def build(g, core, T, topo):
         for h in range(2):
             act(S("MB", 128 * h, 128 * h + 128), IND(mcur, u(32 + 8 * h, 8)))
             scat(S("B"), u(48 + 8 * h, 8), S("MB", 128 * h, 128 * h + 128))
-        act(S("BB"), IND(S("B", 0, V + 8), BC))
+        act(S("BB"), IND(S("B", 0, W), BU))
         act(S("MC"), S("MB", 0, LN))
         fold(S("PW", 0, 16), "SN", "BB", 0, 16, True, True)
         if t > 0:
@@ -581,8 +593,8 @@ def build(g, core, T, topo):
         tt(w(16), NJ, VF, A.add)
         tt(w(17), NJ, BF, A.add)
         tt(w(18, 2), w(16, 2), DUMP, A.min)
-        cp(OJ, w(18))
-        cp(OB, w(19))
+        cp(fw(t, 0, 32), w(18, 2))
+        done = []
         mm([(S("KK0", 0, 384), S("BDC"), S("ONE", 0, 384))], True, False)
         for h in range(2):
             for j in (2 * h, 2 * h + 1):
@@ -591,15 +603,18 @@ def build(g, core, T, topo):
                     over("D1", "DC", j) if off else near("D1", "DC", 8 * j, 8 * j + 8)
                 elif off:
                     again(j)
+                elif j in PLAIN[t]:
+                    mm([(S("PW", 256, 512), S("I1"), rep("ZZ", h, 2))], True, True)
+                    near("D1", "XC", 8 * j, 8 * j + 8, S("PW", 256, 512))
                 elif j % 2:
                     far("D1", "CU", "ZZ", 8 * j, 8 * j + 8, 4)
                 else:
                     for lo, n in ((0, 1), (1, 1), (2, 2), (4, 4)):
                         far("D1", "CU", "ZZ", 8 * j + lo, 8 * j + lo + n, n)
-                lift("KK0", 128 * h, "D1", j, wg(8))
-                lift("KK0", 128 * h, "DC", j, wg((10 if off else 9) if t else (12 if off else 11)))
+                k = lift("KK0", 128 * h, "D1", j, wg(9))
+                done.append(lift("KK0", 128 * h, "DC", j, wg((11 if off else 10) if t else (13 if off else 12)), after=[k]))
             if t == 0:
-                spread("KK0", 128 * h, ("A1", 16 + 32 * h), h, S("I1F"))
+                spread("KK0", 128 * h, ("A1", 16 + 32 * h), h, S("I1F"), after=done[-2:])
         for h in range(2):
             spread("UE", 256 * h + 128, ("MC", 0), h, S("RZ", 0, 128))
         for h in range(2):
@@ -616,7 +631,7 @@ def build(g, core, T, topo):
         def masks(h):
             o = 256 * h
             spread("KK1", o, ("MV", 0), h, S("RZ", 0, 128), start=True)
-            spread("KK1", o + 128, ("MC", 0), h, S("RZ", 0, 128))
+            spread("KK1", o + 128, ("MC", 0), h, S("RZ", 0, 128), free=False)
             if t:
                 for j in (2 * h, 2 * h + 1):
                     lift("KK1", o, "DO", j, wg(0, 2))
@@ -636,59 +651,59 @@ def build(g, core, T, topo):
             cp(IND(S("L"), u(48 + 8 * h, 8)), S("NL", o, o + 128))
 
         for h in range(2):
-            names(t, h, BU, S("L", 0, W), "A2", "RU2", "OU", None, "DO", 256, CO[h], lambda lo, hi: None)
+            names(t, h, BU, S("L", 0, W), "A2", "RU2", "OU", None, "DO", 256, (CO if t else CO0)[h], lambda lo, hi: None)
             masks(h)
         if t == 0:
             for d, r4 in enumerate((R4A, R4B)):
-                act(S("M", V + d * GH, V + (d + 1) * GH), S("LM", d * GH, (d + 1) * GH), bias=r4)
+                to, fro = S("M", V + d * GH, V + (d + 1) * GH), S("LM", d * GH, (d + 1) * GH)
+                act(to, fro, bias=r4) if OPT["mg"][d] == "a" else ts(to, fro, r4, A.add)
         if not last:
             pieces(S("MZ", 0, LN), S("MV", 0, LN), zz, S("PW", 256, 512))
             me, le, ml, ll = "ME%d" % t, "LE%d" % t, "ML%d" % t, "LL%d" % t
             for j in range(2):
-                act(S("SG"), S("CN"), bias=c(18 + j), scale=-1.0, func=F.Sign, accum=S("q", 192 + j, 193 + j))
+                act(S("HB", 256 * j, 256 * j + 256), S("CN"), bias=c(18 + j), scale=-1.0, func=F.Sign, accum=S("q", 192 + j, 193 + j))
             ts(u(96, 2), S("q", 192, 194), 0.5, A.mult, 128.0, A.add)
             ts(u(98, 2), S("q", 192, 194), 0.5, A.mult, 128.0, A.add)
             s2 = u(96, 2)
-            for j, src in enumerate(("MV", "MB", "MV", "MB")):
+            for j, src in enumerate(("MV", "MB")):
                 act(S("MS", 32 * j, 32 * j + 32), IND(S(src), s2))
-            act(S(me, 0, 32), IND(S("ZZ", 384, 656), s2))
-            act(S(me, 168, 200), IND(S("ZZ", 384, 656), s2))
-            act(S(me, 32, 96), IND(S("MZ"), SU), bias=R4A)
-            act(S(me, 104, 168), IND(S("MZ"), SU), bias=R4B)
-            fold(S("PW", 0, 8), "SN", "MS", 0, 8, True, True)
-            ts(S("q", 0, 8), S("PW", 0, 8), float(GH), A.is_lt)
-            tt(S("q", 8, 16), S("PW", 0, 8), CD8, A.add)
-            tt(S("q", 16, 24), S("q", 0, 8), S("q", 8, 16), A.mult)
-            tt(S(me, 96, 104), S("q", 16, 24), D8, A.add)
-            exchange([S(me, 0, 100), S(me, 100, 200)], [S(le, 0, 100), S(le, 100, 200)], "te%d" % t, "re%d" % t, 2500)
+            act(S(me, 64, 96), IND(S("ZZ", 384, 656), s2))
+            act(S(me, 0, 64), IND(S("MZ"), SU), bias=R4A)
+            act(S(me, 100, 164), IND(S("MZ"), SU), bias=R4B)
+            fold(S("PW", 0, 4), "SN", "MS", 0, 4, True, True)
+            ts(S("q", 0, 4), S("PW", 0, 4), GH - 0.5, A.subtract, 8192.0, A.mult)
+            tt(S(me, 96, 100), S("q", 0, 4), S("PW", 0, 4), A.max)
+            exchange([S(me, 0, 100), S(me, 64, 164)], [S(le, 0, 100), S(le, 100, 200)], "te%d" % t, "re%d" % t, 2500)
             mm([(S("PW", 0, 32), S("RN"), S("MS", 0, 32))], True, True)
-            act(S("VR"), S("PW", 0, 32))
-            y = [w(j) for j in range(32, 42)]
-            ts(y[0], CT, float(V), A.is_lt)
-            tt(y[1], CT, VF, A.subtract)
-            tt(y[2], y[0], y[1], A.mult)
-            ts(OWN, BF, float(V), A.is_lt)
-            tt(y[3], BF, VF, A.subtract)
-            tt(y[4], y[3], y[2], A.subtract)
-            tt(y[5], y[4], OWN, A.mult)
-            tt(y[6], y[5], y[2], A.add)
-            tt(y[7], AW, JN, A.subtract)
-            tt(y[8], y[6], y[7], A.mult)
-            tt(y[9], y[8], VF, A.add)
-            cp(PU, y[9])
+            act(S("q", 32, 64), S("PW", 0, 32))
+            y = [w(32, 2), w(34, 2), w(36), w(37), w(38), w(39)]
+            ts(y[0], w(11, 2), V - 0.5, A.subtract, 32768.0, A.mult)
+            tt(y[1], y[0], w(11, 2), A.max)
+            ts(y[2], w(35), 4096.0, A.add)
+            tt(y[3], y[2], w(34), A.min)
+            tt(y[4], w(16), NJ, A.add)
+            tt(y[5], y[4], AW, A.add)
+            tt(S("wi", 0, 16), y[5], y[3], A.min)
+            ts(S("wi", 32, 48), S("wi", 0, 16), 4095, A.bitwise_and)
+            cp(PU, S("wi", 32, 48))
             scat(S("M"), OJ, S("MZ", 0, LN))
             scat(S("M"), OB, S("MZ", 0, LN))
             for e in range(t - 1, -1, -1):
-                act(S("FG", 0, LN), IND(S("M"), S("fw", 40 * e, 40 * e + 16)))
-                scat(S("M"), S("fw", 40 * e + 20, 40 * e + 36), S("FG", 0, LN))
-            cp(GU, S(le, 96, 104))
-            for d, lo in ((0, 32), (1, 104)):
+                act(S("FG", 0, LN), IND(S("M"), fw(e, 0, 16)))
+                scat(S("M"), fw(e, 16, 16), S("FG", 0, LN))
+            tt(S("q", 8, 12), S(le, 96, 100), c(112, 4), A.min)
+            tt(S("q", 12, 16), S(le, 132, 136), c(120, 4), A.min)
+            cp(u(104, 4), S("q", 8, 12))
+            ts(u(108, 4), S("q", 12, 16), float(GH), A.add)
+            for d, lo in ((0, 0), (1, 136)):
                 scat(S("M", V, WD), u(104 + 4 * d, 4), S(le, lo, lo + 64))
             if t < RO - 2:
                 for d in range(2):
-                    cp(S("fw", 40 * t + 16 + 2 * d, 40 * t + 18 + 2 * d), S(le, 96 + 4 * d, 98 + 4 * d))
-                    cp(S("fw", 40 * t + 36 + 2 * d, 40 * t + 38 + 2 * d), S(le, 98 + 4 * d, 100 + 4 * d))
+                    cp(fw(t, 32 + 2 * d, 2), u(104 + 4 * d, 2))
+                    cp(fw(t, 36 + 2 * d, 2), u(106 + 4 * d, 2))
         else:
+            cp(IND(S("NB"), OJ), zz)
+            dma("a", lambda: T.yx[:], lambda: T.NB[:, 0:V], "ox", 3000, ins=[S("NB", 0, V)])
             act(S("MZ", 0, LN), S("MV", 0, LN))
             scat(S("M"), OB, S("MZ", 0, LN))
             act(S("MH"), IND(S("M", 0, V), S("FW")))
@@ -701,38 +716,39 @@ def build(g, core, T, topo):
             if j == 2:
                 mm([(S(kk, 0, 128), S("BDC"), S("ONE", 0, 128))], True, False)
             if j == 3:
-                mm(pens(kk, lo, "EO", 1, 1), False, False)
+                mm(pens(kk, lo, "EO", 1, 1), False, False, True)
             if t:
                 far("D2", "OU", "ZZ", 8 * j, 8 * j + 8, 4)
             elif j in OFF2:
                 over("D2", "DO", j)
             else:
                 near("D2", "DO", 8 * j, 8 * j + 8)
-            lift(kk, lo, "D2", j, wg(8))
-            lift(kk, lo, "DO", j, wg(9 if t else 12 if j in OFF2 else 11), stop=t > 0 and j == 3)
+            k = lift(kk, lo, "D2", j, wg(9))
+            done.append(lift(kk, lo, "DO", j, wg(10 if t else 13 if j in OFF2 else 12), stop=t > 0 and j == 3, after=[k]))
             if t == 0 and j % 2:
-                spread(kk, lo, ("A2", 16 + 32 * (j // 2)), j // 2, S("I1F"), stop=j == 3)
+                spread(kk, lo, ("A2", 16 + 32 * (j // 2)), j // 2, S("I1F"), stop=j == 3, after=done[-2:])
             if j == 1:
-                mm(pens(kk, 0, "EU", 0, 0) + pens(kk, 128, "EU", 0, 1) + pens(kk, lo, "EO", 1, 0), False, True)
+                for h in range(2):
+                    mm(pens(kk, 128 * h, "EU", 0, h), False, False, True)
+                mm(pens(kk, lo, "EO", 1, 0), False, True)
                 tt(S("KC"), S(kk, 0, 256), S("CL"), A.min)
                 chosen(0)
         chosen(1)
-        cp(IND(S("X"), OJ), zz)
         if last:
             break
-        for d, lo in ((0, 0), (1, 168)):
+        cp(IND(S("X"), OJ), zz)
+        for d, lo in ((0, 64), (1, 100)):
             cp(IND(S("X", V, WD), u(104 + 4 * d, 2)), S(le, lo, lo + 32))
         ts(S("q", 0, 32), IND(S("NL"), s2), float(GH), A.is_lt)
-        tt(S("q", 64, 96), IND(S("NL"), s2), S("VR"), A.subtract)
+        tt(S("q", 64, 96), IND(S("NL"), s2), S("q", 32, 64), A.subtract)
         tt(S("q", 128, 160), S("q", 0, 32), S("q", 64, 96), A.mult)
-        tt(S(ml), S("q", 128, 160), S("VR"), A.add)
+        tt(S(ml), S("q", 128, 160), S("q", 32, 64), A.add)
         exchange([S(ml)] * 2, [S(ll, 0, 32), S(ll, 32, 64)], "tm%d" % t, "rm%d" % t, 2500)
         lanes(t + 1)
         for e in range(t - 1, -1, -1):
-            act(S("FG", 256, 320), IND(S("M", V, WD), S("fw", 40 * e + 16, 40 * e + 20)))
-            scat(S("M", V, WD), S("fw", 40 * e + 36, 40 * e + 40), S("FG", 256, 320))
+            act(S("FG", 256, 320), IND(S("M", V, WD), fw(e, 32, 4)))
+            scat(S("M", V, WD), fw(e, 36, 4), S("FG", 256, 320))
     dma("s", lambda: T.yl[:], lambda: T.L[:, 0:V], "ol", 4000, ins=[S("L", 0, V)])
-    dma("a", lambda: T.yx[:], lambda: T.X[:, 0:V], "ox", 3000, ins=[S("X", 0, V)])
     return nodes, eng
 
 
@@ -748,8 +764,10 @@ def order(nodes):
             for (j, lo, hi, w2) in hist.get(y[0], ()):
                 meet = lo < y[2] and y[1] < hi
                 if SCRATCH[y[0]][0] == "sbuf" and (nodes[j]["sem"] or x["sem"]) and wr and w2:
-                    q = 8 if SCRATCH[y[0]][2] in ("bfloat16", "uint16") else 4
+                    q = 8 if SCRATCH[y[0]][2] in SHORT else 4
                     meet = lo // q * q < y[2] and y[1] // q * q < hi
+                if bank and wr and w2 and x["free"] and nodes[j]["free"]:
+                    continue
                 if bank and (nodes[j]["e"] != x["e"] or wr or w2):
                     d[j] = d.get(j, False) or (w2 and not wr and meet)
                 elif meet and (wr or w2):
@@ -757,7 +775,8 @@ def order(nodes):
         for y, wr in acc:
             h = hist.setdefault(y[0], [])
             if SCRATCH[y[0]][0] == "psum":
-                h[:] = [z for z in h if z[0] == i or (not wr and (z[3] or nodes[z[0]]["e"] == x["e"]))]
+                if not (wr and x["free"]):
+                    h[:] = [z for z in h if z[0] == i or (not wr and (z[3] or nodes[z[0]]["e"] == x["e"]))]
             elif wr and y[3] == 1 and y[4] is None:
                 h[:] = [z for z in h if z[0] == i or not (y[1] <= z[1] and z[2] <= y[2])]
             h.append((i, y[1], y[2], wr))
@@ -772,57 +791,76 @@ def order(nodes):
             pre[i].append((j, dl))
             suc[j].append((i, dl))
     cost = [max(1.0, x["cost"]) for x in nodes]
+    queue = ["vapgsR".index(x["e"]) for x in nodes]
+    lats = [x["lat"] for x in nodes]
+    fore = [[(j, cost[j] + dl) for j, dl in p] for p in pre]
+    back = [[(j, cost[j] + dl) for j, dl in p] for p in suc]
+    zero = [0.0] * n
+    ends = [i for i in range(n) if not suc[i]]
 
-    def place(lst, before, tail):
+    def place(lst, before, tail, kept=(), old=None):
         at = [0.0] * n
-        busy = {}
+        los, his = [[] for _ in range(6)], [[] for _ in range(6)]
+        for k in kept:
+            at[k] = old[k]
+            los[queue[k]].append(old[k])
+            his[queue[k]].append(old[k] + cost[k])
         for k in lst:
-            st = max([at[j] + cost[j] + dl for j, dl in before[k]] + [tail[k]])
-            b = busy.setdefault(nodes[k]["e"], [])
-            lo, hi = 0, len(b)
-            while lo < hi:
-                mid = (lo + hi) // 2
-                if b[mid][1] <= st:
-                    lo = mid + 1
-                else:
-                    hi = mid
-            while lo < len(b) and b[lo][0] < st + cost[k]:
-                st = max(st, b[lo][1])
-                lo += 1
-            b.insert(lo, (st, st + cost[k]))
+            st = tail[k]
+            for j, dl in before[k]:
+                if at[j] + dl > st:
+                    st = at[j] + dl
+            lo, hi, c = los[queue[k]], his[queue[k]], cost[k]
+            i = m = len(hi)
+            while i and hi[i - 1] > st:
+                i -= 1
+            while i < m and lo[i] < st + c:
+                if hi[i] > st:
+                    st = hi[i]
+                i += 1
+            lo.insert(i, st)
+            hi.insert(i, st + c)
             at[k] = st
         return at
+
+    def finish(at):
+        return max(at[i] + cost[i] + lats[i] for i in ends)
+
+    def turned(at):
+        rev = place(sorted(range(n), key=lambda i: -at[i] - cost[i]), back, lats)
+        return place(sorted(range(n), key=lambda i: -rev[i] - cost[i]), fore, zero)
     prio = [0.0] * n
     for i in range(n - 1, -1, -1):
-        prio[i] = cost[i] + max([prio[k] + dl for k, dl in suc[i]] + [nodes[i]["lat"]])
-    lst = sorted(range(n), key=lambda i: -prio[i])
-    best = None
-    rnd = [12345]
-
-    def shaken(at, amp):
-        key = [0.0] * n
-        rnd[0] = (rnd[0] * 1103515245 + 12345) % 2147483648
-        mid = best[0] * (rnd[0] / 2147483648.0)
-        amp = amp * (1 + rnd[0] // 1024 % 4)
-        for i in range(n):
-            x = at[i]
-            if abs(x - mid) < SPAN:
-                rnd[0] = (rnd[0] * 1103515245 + 12345) % 2147483648
-                x += amp * (rnd[0] / 2147483648.0 - 0.5)
-            key[i] = max([x] + [key[j] + 1.0 for j, dl in pre[i]])
-        return sorted(range(n), key=lambda i: key[i])
+        prio[i] = cost[i] + max([prio[k] + dl for k, dl in suc[i]] + [lats[i]])
+    at = place(sorted(range(n), key=lambda i: -prio[i]), fore, zero)
+    best = (finish(at), at, sorted(range(n), key=lambda i: at[i]))
+    rnd = 12345
     for it in range(PASSES):
-        at = place(lst, pre, [0.0] * n)
-        end = max(at[i] + cost[i] + nodes[i]["lat"] for i in range(n))
-        if best is None or end <= best[0]:
-            best = (end, at)
-        if it % 2 == 1:
-            lst = shaken(best[1], AMP)
-            continue
-        back = place(sorted(range(n), key=lambda i: -at[i] - cost[i]), suc, [x["lat"] for x in nodes])
-        lst = sorted(range(n), key=lambda i: -back[i] - cost[i])
-    times = best[1]
-    return deps, sorted(range(n), key=lambda i: times[i]), times
+        end, old, seq = best
+        rnd = (rnd * 1103515245 + 12345) % 2147483648
+        mid = end * (rnd / 2147483648.0)
+        amp = AMP * (1 + rnd // 1024 % 4)
+        first = 0
+        while first < n - 1 and old[seq[first]] < mid - SPAN:
+            first += 1
+        key = list(old)
+        for i in range(n):
+            x = old[i]
+            if x >= mid - SPAN:
+                if x < mid + SPAN:
+                    rnd = (rnd * 1103515245 + 12345) % 2147483648
+                    x += amp * (rnd / 2147483648.0 - 0.5)
+                for j, dl in pre[i]:
+                    if key[j] >= x:
+                        x = key[j] + 1.0
+                key[i] = x
+        at = place(sorted(seq[first:], key=lambda i: key[i]), fore, zero, seq[:first], old)
+        at2 = turned(at)
+        if finish(at2) <= finish(at):
+            at = at2
+        if finish(at) <= end:
+            best = (finish(at), at, sorted(range(n), key=lambda i: at[i]))
+    return deps, best[2], best[1]
 
 
 def rank_program(g, core, T, topo):

@@ -9,13 +9,16 @@ NX = (2, 4)
 SUB = [(), (2,), (2,), (2,)]
 RELU = (2,)
 PLAIN = [(), (3,), (3,), (3,)]
-OPT = dict(kt="a", vf="a", rows="vv", bd="a", m="v", mg="aa", wg="a")
-CH0 = [[(4, "v"), (4, "a"), (4, "a"), (4, "a")], [(4, "a")] * 4]
-CH = [[(4, "v"), (4, "a"), (8, "a")], [(8, "a"), (8, "a")]]
-CO0 = [[(4, "v"), (4, "a"), (8, "a")], [(4, "v"), (4, "a"), (8, "a")]]
+PLAIN2 = [{}, {}, {}, {0: "near"}]
+OPT = dict(kt="a", vf="a", bd="a", xv="am", zz="mm")
+CH0 = [[(4, "v"), (4, "a"), (4, "a"), (4, "a")]] * 2
+CH = [[(4, "a"), (4, "a"), (8, "a")], [(8, "a"), (8, "a")]]
+CO0 = [[(4, "v"), (4, "a"), (8, "a")], [(8, "a"), (8, "a")]]
 CO = [[(8, "a"), (8, "a")], [(8, "a"), (8, "a")]]
+ND1 = [(1, 1, 2, 2, 2), (2, 2, 4), (4, 4), (4, 4)]
 OFF1, OFF2 = (), ()
-HOP, PEC, PASSES, AMP, SPAN = 150.0, 0.55, 5000, 2000.0, 3500.0
+PEC, DLAT, PASSES, SWAPS, AMP, SPAN = 0.5, 3600, 10500, 12000, 2000.0, 3500.0
+CASES = [(1.56, 3.8, 0.5, 150.0, 1.0), (1.2, 2.5, 0.55, 140.0, 1.0), (1.9, 5.2, 0.5, 105.0, 0.7), (1.4, 4.6, 0.45, 190.0, 1.35)]
 PLAN = []
 
 SCRATCH = {}
@@ -44,13 +47,14 @@ _buf("Z0 IU", 144, "float32")
 _buf("RN BD32 BDC BD1 IBIG I24 I1 IM1 I014 IH WBH I13 IM13 BDW BDB BJM IMG IMH", 128, "bfloat16")
 _buf("WBL IG MT I1F", 128, "float32")
 _buf("BJ", 384, "bfloat16")
-_buf("NL MB MZ", 272, "float32")
+_buf("MB MZ", 272, "float32")
+_buf("NL", 272, "int32")
 _buf("A1 A2 FG", 320, "float32")
 _buf("Z", 576, "float32")
 _buf("MV", 272, "bfloat16")
 _buf("CF KC VT CL RF", 256, "float32")
 _buf("RZ PW2 I256 CR EQ BB BK BY TH MC NN CN", 256, "bfloat16")
-_buf("RI RJ", 256, "int32")
+_buf("RI", 256, "int32")
 _buf("RU CU RU2 OU PR", 256, "uint16")
 _buf("FW", 64, "uint16")
 _buf("fw", 160, "uint16")
@@ -64,7 +68,7 @@ _buf("u", 128, "uint16")
 _buf("cu", 32, "uint16")
 _buf("MS", 64, "bfloat16")
 _buf("q", 200, "float32")
-_buf("YF", V, "float32")
+_buf("YF", 64, "float32")
 _buf("ME0 ME1 ME2", 164, "float32")
 _buf("LE0 LE1 LE2", 200, "float32")
 _buf("ML0 ML1 ML2", 32, "float32")
@@ -72,7 +76,7 @@ _buf("LL0 LL1 LL2", 64, "float32")
 _buf("PC K0 UE UX KK0 KK1 PA PW", 512, "float32", "psum")
 
 SEMAPHORES = (["sv", "sa", "sp", "sg", "dx", "dy", "dn", "dm", "dh", "dl", "dt", "ox", "ol", "of", "tx", "rx", "tl", "rl", "tp", "rp"]
-              + ["%s%d" % (a, t) for a in ("te", "re", "tm", "rm") for t in range(RO - 1)])
+              + ["%s%d" % (a, t) for a in ("te", "re", "tm", "rm") for t in range(RO - 1)] + ["m%d" % j for j in range(1, 40)])
 SHORT = ("bfloat16", "uint16", "float16")
 
 
@@ -88,6 +92,7 @@ def build(g, core, T, topo):
     rank = T.rank_of(core)
     n_ranks = len(T.cores)
     nodes = []
+    moves = []
     eng = {"v": g.vector, "a": g.scalar, "p": g.tensor, "g": g, "s": g.sync}
 
     def ap(x):
@@ -120,7 +125,8 @@ def build(g, core, T, topo):
                 rd.append(x[2])
             else:
                 wr.append(x)
-        nodes.append(dict(e=e, cost=cost, fn=fn, rd=rd, wr=wr, lat=lat, sem=sem, inc=inc, after=list(after), free=free))
+        ind = [cnt(x) if isinstance(x, tuple) and x[0] == "*" else 0 for x in list(ins[:1]) + list(outs[:1])]
+        nodes.append(dict(e=e, ind=ind if len(ind) == 2 else [0, 0], cost=cost, fn=fn, rd=rd, wr=wr, lat=lat, sem=sem, inc=inc, after=list(after), free=free))
         return len(nodes) - 1
 
     def vcost(out, i0, base):
@@ -203,6 +209,10 @@ def build(g, core, T, topo):
     def dma(e, out, in_, sem, lat, outs=(), ins=(), **kw):
         return node(e, 100 if e != "g" else 1200, lambda: eng[e].dma_start(out(), in_(), **kw), list(outs), list(ins), lat=lat, sem=sem, inc=16)
 
+    def move(e, out, in_, rows=slice(None), behind=()):
+        moves.append(1)
+        return dma(e, lambda: T[out[0]][rows, out[1]:out[2]], lambda: T[in_[0]][rows, in_[1]:in_[2]], "m%d" % len(moves), DLAT, outs=[out], ins=[in_] + list(behind))
+
     def exchange(srcs, dsts, tsem, rsem, lat):
         to = [T.cores[(rank - d) % n_ranks] for d in (1, 2)]
         es = [e for e in topo.engines(core, to[0]) if e in topo.engines(core, to[1])]
@@ -240,8 +250,7 @@ def build(g, core, T, topo):
     DUMP, D8, G8, TH8, T16a, I16 = c(64, 32), c(112, 8), c(128, 8), c(136, 8), c(144, 16), c(192, 16)
     OENT, OBC = S("cu", 0, 8), S("cu", 16, 32)
     first = [iota(ci(0), [[0, 1]], 0, 1), iota(S("IU"), [[1, 144]], 0), iota(S("IG"), [[1, 8], [0, 16]], 0)]
-    iota(S("I256"), [[32, 256]], 0)
-    iota(S("NB", 0, V), [[32, V // 256], [0, 256]], 0, after=first)
+    iota(S("NB", 0, V), [[32, V // 256], [0, 256]], 0, after=[iota(S("I256"), [[32, 256]], 0, after=first)])
     iota(S("NB", V, W), [[32, (W - V) // 256], [0, 256]], 32 * V // 256, after=[sent])
     dma("s", lambda: T.NB[1::16, 0:V], lambda: T.I256[0:32, :], "dn", 2500, outs=[S("NB", 0, V)], ins=[S("I256")])
     dma("s", lambda: T.NB[1::16, V:W], lambda: T.I256[0:56, :], "dm", 2500, outs=[S("NB", V, W)], ins=[S("I256")])
@@ -257,11 +266,13 @@ def build(g, core, T, topo):
     ts(TMP, mk(0), 4.0, A.mult)
     ts(TMP2, mk(1), 1.0 / 32, A.mult, TMP, A.add)
     ts(WN, mk(4), 4.0, A.mult, TMP2, A.add)
-    ts(WS, mk(2), mk(3), A.add, -128.0, A.mult)
+    ts(c(19), mk(2), mk(10), A.add, mk(6), A.subtract)
+    ts(WS, c(19), -128.0, A.mult)
+    ts(c(17), mk(10), mk(6), A.add, 256.0, A.mult)
     tt(WM, WN, WS, A.add)
     tt(WP, WN, WS, A.subtract)
     ts(W014, mk(0), mk(1), A.add, mk(4), A.add)
-    tt(WH, mk(2), mk(3), A.subtract)
+    tt(WH, mk(2), mk(10), A.subtract)
     ts(R4A, mk(4), 32.0 * V / 128, A.mult)
     ts(R4B, mk(4), 32.0 * (V + GH) / 128, A.mult)
     ts(S("S32"), S("IU"), G15, A.is_equal, 32.0, A.mult)
@@ -279,13 +290,14 @@ def build(g, core, T, topo):
     mset(S("RZ", 128, 256), 0.0)
     ts(S("IMG"), S("IH"), 1.5 * 2 ** 32, A.mult)
     ts(S("IMH"), S("IH"), -1.5 * 2 ** 32, A.mult)
-    ts(S("IH"), S("IH"), -240.0, A.mult)
-    tt(S("BD32"), sel("S32", 2), sel("S32", 3), A.subtract)
+    tt(S("BD32"), sel("S32", 2), sel("S32", 10), A.subtract)
     ts(S("WBL"), sel("Z0", 1), 32.0, A.mult)
-    ts(S("MT"), sel("Z0", 0), 1.0 / 128, A.mult)
-    tt(S("WBH"), S("MT"), sel("Z0", 1), A.subtract)
-    for r in range(16):
-        times(OPT["rows"][r % 2], S("ROWS", 128 * r, 128 * r + 128), S("BD1"), mk(r))
+    ts(S("MT"), sel("Z0", 0), 1.0 / 4, A.mult)
+    tt(S("WBH"), S("MT"), S("WBL"), A.subtract)
+    mset(S("ONE"), 1.0)
+    for r in range(0, 16, 4):
+        node("g", 200 + 1024, lambda r=r: g.affine_select(T.ROWS[:, 128 * r:128 * r + 512], T.ONE[:], [[1, 4], [16, 8], [0, 16]], A.is_equal, 0.0, r, -1),
+             [S("ROWS", 128 * r, 128 * r + 512)], [S("ONE")], after=[sent])
     mset(c(32, 16), 0.5)
     scan(S("PW2", 0, 16), c(32, 16), c(32, 16), 131072.0, A.mult, A.max)
     for n in (16, 32, 64, 128):
@@ -297,11 +309,13 @@ def build(g, core, T, topo):
                   (S("BJ", 128, 256), 1.0 / 8), (S("BJ", 256, 384), 1.0 / 8)):
         times(OPT["bd"], m, S("BD1"), wt)
     ts(G8, S("IU", 0, 8), GRP, A.is_equal)
-    ts(c(30), WS, 1.0 / 4096, A.mult)
     ts(c(31), WS, -1.0 / 4096, A.mult)
-    for j, wt in enumerate((WN, WN, c(30), c(31), c(30), -1.0, 1.0, 2.0, -2.0, 8192.0, WM, WP, -4096.0, 4096.0)):
-        times(OPT["wg"], wg(j), G8, wt)
-    mset(S("ONE"), 1.0)
+    ts(c(160, 8), G8, -1.0, A.mult)
+    cp(c(168, 8), G8)
+    cp(c(176, 8), c(160, 8))
+    for j, n, base, wt in ((0, 1, G8, WN), (1, 1, G8, WN), (2, 3, c(160, 24), c(31)), (5, 2, c(160, 16), 1.0), (7, 2, c(160, 16), -2.0), (9, 1, G8, 8192.0),
+                           (10, 1, G8, WM), (11, 1, G8, WP), (12, 2, c(160, 16), 4096.0)):
+        times("a", wg(j, n), base, wt)
     for b in ("MV", "MB"):
         fill(S(b, 256, 272), 128)
     for b in ("MZ", "NL"):
@@ -310,7 +324,7 @@ def build(g, core, T, topo):
         mset(S("A1", lo, hi), 0.0)
         fill(S("A2", lo, hi), 0)
     fill(S("M", W, WD), 0)
-    fill(S("B", V, W), 128)
+    fill(S("B", V, V + 8), 128)
     ts(T16a, I16, 16.0, A.mult, ROW, A.add)
     ts(c(64, 16), T16a, float(W), A.add)
     ts(c(80, 16), T16a, float(W), A.add)
@@ -350,18 +364,19 @@ def build(g, core, T, topo):
         tt(S("GL", lo, hi), S(bank, 0, hi - lo), S("L", lo, hi), A.min)
     exchange([S("GL")] * 2, [S("LG", 0, GH), S("LG", GH, 2 * GH)], "tl", "rl", 6000)
     for lo in (0, 512):
-        act(S("HB"), S("L", lo, lo + 512), scale=32.0)
-        mm([(S("KK0"), S("WBH"), S("HB")), (S("KK0"), S("WBL"), S("L", lo, lo + 512))], True, True)
+        act(S("D2", lo, lo + 512), S("L", lo, lo + 512))
+        mm([(S("KK0"), S("WBH"), S("D2", lo, lo + 512)), (S("KK0"), S("WBL"), S("L", lo, lo + 512))], True, True)
         act(S("B", lo, lo + 512), S("KK0"))
 
     def pieces(out, names, x, o):
         one = S("ONE", 0, cnt(out))
-        mm([(o, S("I014"), names), (o, S("IH"), one), (o, S("BD32"), x), (o, S("IMG"), one), (o, S("IMH"), one), (o, sel("S32", 3), x)], True, True)
-        act(out, o)
+        mm([(o, S("IMG"), one), (o, S("BD32"), x), (o, S("IMH"), one), (o, sel("S32", 10), x)] + ([(o, S("I014"), names)] if names else []), True, True)
+        act(out, o, bias=c(17))
 
     for lo in (0, 512):
-        pieces(S("MH", lo, lo + 512), S("NB", lo, lo + 512), S("X", lo, lo + 512), S("KK1"))
-    (act if OPT["m"] == "a" else cp)(S("M", 0, V), S("MH"))
+        pieces(S("MH", lo, lo + 512), None, S("X", lo, lo + 512), S("KK1"))
+    move("g", S("M", 0, W), S("NB", 0, W), behind=[S("LG")])
+    move("g", S("M", 0, V), S("MH"), slice(2, None, 4))
     exchange([S("MH", 0, GH)] * 2, [S("LM", 0, GH), S("LM", GH, 2 * GH)], "tp", "rp", 6000)
 
     def w(j, n=1):
@@ -383,7 +398,16 @@ def build(g, core, T, topo):
     def rep(b, h, n):
         return S(b, 512 - 128 * n, 512) if h == 0 else S(b, 512, 512 + 128 * n)
 
-    def repeat(b, h, n):
+    def repeat(b, h, n, e="a"):
+        if e == "s":
+            for j in range(1, n):
+                lo = 384 - 128 * j if h == 0 else 512 + 128 * j
+                move("s", S(b, lo, lo + 128), rep(b, h, 1))
+            return
+        if e == "m":
+            act(S(b, 256 + 384 * h, 384 + 384 * h), rep(b, h, 1))
+            move("s", S(b, 768 * h, 768 * h + 256), rep(b, h, 2))
+            return
         if n >= 2:
             act(S(b, 256 + 384 * h, 384 + 384 * h), rep(b, h, 1))
         if n >= 4:
@@ -485,7 +509,7 @@ def build(g, core, T, topo):
             spread("UE", 256 * h, ("MV", 0), h, S("RZ"), start=h == 0, free=False)
         for h in range(2):
             act(rep("XV", h, 1), IND(S("X", 0, V), u(16 + 8 * h, 8)))
-            repeat("XV", h, NX[h] if t else 2)
+            repeat("XV", h, NX[h] if t else 2, OPT["xv"][h] if t else "a")
             if t == 0:
                 mm([(S("PC", 256 * h, 256 * h + 256), S("I1"), rep("XV", h, 2))], True, True)
             spread("UX", 256 * h, pair("XV"), h, S("BY"))
@@ -549,7 +573,7 @@ def build(g, core, T, topo):
         cp(BF, S("wi", 16, 32))
         if last:
             dma("s", lambda: T.NB[:, 0:V], lambda: T.X[:, 0:V], "dy", 3000, outs=[S("NB", 0, V)], ins=[S("X", 0, V)])
-            act(S("MH"), S("M", 0, V))
+            move("g", S("MH"), S("M", 0, V))
             fold(S("PA", 0, 64), "SN", "MH", 0, 64, True, True)
             cp(S("FW"), S("PA", 0, 64))
         if t == 0:
@@ -564,14 +588,13 @@ def build(g, core, T, topo):
             tt(S("ZS", o, o + 128), IND(S("X", 0, W), u(32 + 8 * h, 8)), rep("XV", h, 1), A.add)
             ts(S("ZT", o, o + 128), S("ZS", o, o + 128), 0.5 - 2.0 ** -11, A.mult, 1536.0, A.add)
             ts(rep("ZZ", h, 1), S("ZT", o, o + 128), -1536.0, A.add)
-            repeat("ZZ", h, 4)
-            if t == 0:
-                mm([(S("PC", 256 * h, 256 * h + 256), S("I1"), rep("ZZ", h, 2))], True, True)
+            repeat("ZZ", h, 4, OPT["zz"][h]) if t else repeat("ZZ", h, 4 if OFF1 or OFF2 else 2)
         zz = pair("ZZ")
         for h in range(2):
             act(S("MB", 128 * h, 128 * h + 128), IND(mcur, u(32 + 8 * h, 8)))
             scat(S("B"), u(48 + 8 * h, 8), S("MB", 128 * h, 128 * h + 128))
-        act(S("BB"), IND(S("B", 0, W), BU))
+        ts(u(80), S("wi", 16, 32), float(V), A.min)
+        act(S("BB"), IND(S("B", 0, V + 8), u(80)))
         act(S("MC"), S("MB", 0, LN))
         fold(S("PW", 0, 16), "SN", "BB", 0, 16, True, True)
         if t > 0:
@@ -597,6 +620,8 @@ def build(g, core, T, topo):
         done = []
         mm([(S("KK0", 0, 384), S("BDC"), S("ONE", 0, 384))], True, False)
         for h in range(2):
+            if t == 0:
+                mm([(S("PC", 256 * h, 256 * h + 256), S("I1"), rep("ZZ", h, 2))], True, True)
             for j in (2 * h, 2 * h + 1):
                 off = j in (SUB[t] if t else OFF1)
                 if t == 0:
@@ -606,11 +631,11 @@ def build(g, core, T, topo):
                 elif j in PLAIN[t]:
                     mm([(S("PW", 256, 512), S("I1"), rep("ZZ", h, 2))], True, True)
                     near("D1", "XC", 8 * j, 8 * j + 8, S("PW", 256, 512))
-                elif j % 2:
-                    far("D1", "CU", "ZZ", 8 * j, 8 * j + 8, 4)
                 else:
-                    for lo, n in ((0, 1), (1, 1), (2, 2), (4, 4)):
-                        far("D1", "CU", "ZZ", 8 * j + lo, 8 * j + lo + n, n)
+                    lo = 8 * j
+                    for n in ND1[j]:
+                        far("D1", "CU", "ZZ", lo, lo + n, n)
+                        lo += n
                 k = lift("KK0", 128 * h, "D1", j, wg(9))
                 done.append(lift("KK0", 128 * h, "DC", j, wg((11 if off else 10) if t else (13 if off else 12)), after=[k]))
             if t == 0:
@@ -643,20 +668,18 @@ def build(g, core, T, topo):
 
         def chosen(h):
             o = 128 * h
-            tt(S("RI", o, o + 128), S(ko[h][0], ko[h][1], ko[h][1] + 128), S("KC", o, o + 128), A.min)
-            ts(S("RJ", o, o + 128), S("RI", o, o + 128), 4095, A.bitwise_and)
-            cp(S("RF", o, o + 128), S("RJ", o, o + 128))
-            mm([(S("UE", o, o + 128), S("RF", o, o + 128), S("I1F"))], True, True)
-            act(S("NL", o, o + 128), S("UE", o, o + 128))
+            keys, turned = S("RF", o, o + 128), S(("UE", "UX")[h], 0, 128)
+            tt(keys, S(ko[h][0], ko[h][1], ko[h][1] + 128), S("KC", o, o + 128), A.min)
+            node("p", PEC * 512, lambda: g.tensor.transpose(ap(turned), ap(keys), ap(S("I1F"))), [turned], [keys, S("I1F")])
+            cp(S("RI", o, o + 128), turned)
+            ts(S("NL", o, o + 128), S("RI", o, o + 128), 4095, A.bitwise_and)
             cp(IND(S("L"), u(48 + 8 * h, 8)), S("NL", o, o + 128))
 
         for h in range(2):
             names(t, h, BU, S("L", 0, W), "A2", "RU2", "OU", None, "DO", 256, (CO if t else CO0)[h], lambda lo, hi: None)
             masks(h)
         if t == 0:
-            for d, r4 in enumerate((R4A, R4B)):
-                to, fro = S("M", V + d * GH, V + (d + 1) * GH), S("LM", d * GH, (d + 1) * GH)
-                act(to, fro, bias=r4) if OPT["mg"][d] == "a" else ts(to, fro, r4, A.add)
+            move("g", S("M", V, W), S("LM"), slice(2, None, 4))
         if not last:
             pieces(S("MZ", 0, LN), S("MV", 0, LN), zz, S("PW", 256, 512))
             me, le, ml, ll = "ME%d" % t, "LE%d" % t, "ML%d" % t, "LL%d" % t
@@ -688,9 +711,6 @@ def build(g, core, T, topo):
             cp(PU, S("wi", 32, 48))
             scat(S("M"), OJ, S("MZ", 0, LN))
             scat(S("M"), OB, S("MZ", 0, LN))
-            for e in range(t - 1, -1, -1):
-                act(S("FG", 0, LN), IND(S("M"), fw(e, 0, 16)))
-                scat(S("M"), fw(e, 16, 16), S("FG", 0, LN))
             tt(S("q", 8, 12), S(le, 96, 100), c(112, 4), A.min)
             tt(S("q", 12, 16), S(le, 132, 136), c(120, 4), A.min)
             cp(u(104, 4), S("q", 8, 12))
@@ -707,17 +727,21 @@ def build(g, core, T, topo):
             act(S("MZ", 0, LN), S("MV", 0, LN))
             scat(S("M"), OB, S("MZ", 0, LN))
             act(S("MH"), IND(S("M", 0, V), S("FW")))
-            for h, bank in enumerate(("PA", "PW")):
-                mm([(S(bank, 0, 512, 1, (0, 8)), wg(0), S("MH", 512 * h, 512 * h + 512))], True, True)
-                act(S("YF", 512 * h, 512 * h + 512, 1, (0, 8)), S(bank, 0, 512, 1, (0, 8)))
-            dma("s", lambda: T.yf[:], lambda: T.YF[0:8, :], "of", 2500, ins=[S("YF")])
+            mm([(S("PA", 0, 64), sel("SN", r), S("MH", 64 * r, 64 * r + 64)) for r in range(16)], True, True)
+            act(S("YF"), S("PA", 0, 64))
+            dma("s", lambda: T.yf[:], lambda: T.YF[:], "of", 2500, ins=[S("YF")])
         for j in range(4):
             kk, lo = ko[j // 2]
             if j == 2:
                 mm([(S(kk, 0, 128), S("BDC"), S("ONE", 0, 128))], True, False)
             if j == 3:
                 mm(pens(kk, lo, "EO", 1, 1), False, False, True)
-            if t:
+            if j in PLAIN2[t]:
+                for k in range(8 * j, 8 * j + 8, 4):
+                    act(S("XC", 128 * k, 128 * k + 512), IND(S("X", 0, W), S("OU", 8 * k, 8 * k + 32)))
+                mm([(S("PW", 256, 512), S("I1"), rep("ZZ", j // 2, 2))], True, True)
+                near("D2", "XC", 8 * j, 8 * j + 8, S("PW", 256, 512))
+            elif t:
                 far("D2", "OU", "ZZ", 8 * j, 8 * j + 8, 4)
             elif j in OFF2:
                 over("D2", "DO", j)
@@ -746,6 +770,8 @@ def build(g, core, T, topo):
         exchange([S(ml)] * 2, [S(ll, 0, 32), S(ll, 32, 64)], "tm%d" % t, "rm%d" % t, 2500)
         lanes(t + 1)
         for e in range(t - 1, -1, -1):
+            act(S("FG", 0, LN), IND(S("M"), fw(e, 0, 16)))
+            scat(S("M"), fw(e, 16, 16), S("FG", 0, LN))
             act(S("FG", 256, 320), IND(S("M", V, WD), fw(e, 32, 4)))
             scat(S("M", V, WD), fw(e, 36, 4), S("FG", 256, 320))
     dma("s", lambda: T.yl[:], lambda: T.L[:, 0:V], "ol", 4000, ins=[S("L", 0, V)])
@@ -782,29 +808,27 @@ def order(nodes):
             h.append((i, y[1], y[2], wr))
         d.pop(i, None)
         deps.append(d)
-    pre = [[] for _ in range(n)]
-    suc = [[] for _ in range(n)]
-    for i in range(n):
-        for j in set(list(deps[i]) + nodes[i]["after"]):
-            same = nodes[i]["e"] == nodes[j]["e"] and not deps[i].get(j, False)
-            dl = (nodes[j]["lat"] if j in deps[i] or nodes[i]["e"] == "R" else 0.0) + (0.0 if same else HOP)
-            pre[i].append((j, dl))
-            suc[j].append((i, dl))
-    cost = [max(1.0, x["cost"]) for x in nodes]
+    pre = [sorted(set(list(deps[i]) + nodes[i]["after"])) for i in range(n)]
     queue = ["vapgsR".index(x["e"]) for x in nodes]
-    lats = [x["lat"] for x in nodes]
-    fore = [[(j, cost[j] + dl) for j, dl in p] for p in pre]
-    back = [[(j, cost[j] + dl) for j, dl in p] for p in suc]
+    ends = sorted(set(range(n)) - set(j for p in pre for j in p))
     zero = [0.0] * n
-    ends = [i for i in range(n) if not suc[i]]
 
-    def place(lst, before, tail, kept=(), old=None):
+    def case(gather, scatter, pe, hop, far):
+        cost = [max(1.0, x["cost"] * (pe / PEC if x["e"] == "p" else 1.0) + (gather - 1.56) * x["ind"][0] + (scatter - 3.8) * x["ind"][1]) for x in nodes]
+        lats = [far * x["lat"] for x in nodes]
+        fore, back = [[] for _ in range(n)], [[] for _ in range(n)]
+        for i in range(n):
+            for j in pre[i]:
+                same = queue[i] == queue[j] and not deps[i].get(j, False)
+                dl = (lats[j] if j in deps[i] or queue[i] == 5 else 0.0) + (0.0 if same else hop)
+                fore[i].append((j, cost[j] + dl))
+                back[j].append((i, cost[i] + dl))
+        return cost, lats, fore, back
+    cases = [case(*x) for x in CASES]
+
+    def place(lst, cost, before, tail):
         at = [0.0] * n
         los, his = [[] for _ in range(6)], [[] for _ in range(6)]
-        for k in kept:
-            at[k] = old[k]
-            los[queue[k]].append(old[k])
-            his[queue[k]].append(old[k] + cost[k])
         for k in lst:
             st = tail[k]
             for j, dl in before[k]:
@@ -823,26 +847,45 @@ def order(nodes):
             at[k] = st
         return at
 
-    def finish(at):
-        return max(at[i] + cost[i] + lats[i] for i in ends)
+    def replay(seq, cost, lats, fore, back):
+        at = [0.0] * n
+        free = [0.0] * 6
+        for k in seq:
+            st = free[queue[k]]
+            for j, dl in fore[k]:
+                if at[j] + dl > st:
+                    st = at[j] + dl
+            at[k] = st
+            if queue[k] < 5:
+                free[queue[k]] = st + cost[k]
+        return at, max(at[i] + cost[i] + lats[i] for i in ends)
 
-    def turned(at):
-        rev = place(sorted(range(n), key=lambda i: -at[i] - cost[i]), back, lats)
-        return place(sorted(range(n), key=lambda i: -rev[i] - cost[i]), fore, zero)
+    def packed(key, cost, lats, fore, back):
+        at = place(sorted(range(n), key=lambda i: key[i]), cost, fore, zero)
+        rev = place(sorted(range(n), key=lambda i: -at[i] - cost[i]), cost, back, lats)
+        at = place(sorted(range(n), key=lambda i: -rev[i] - cost[i]), cost, fore, zero)
+        return sorted(range(n), key=lambda i: at[i])
+
+    def judged(seq, bound=BIG):
+        runs = [replay(seq, *cases[0])]
+        if runs[0][1] > bound:
+            return BIG, seq, runs
+        runs += [replay(seq, *x) for x in cases[1:]]
+        return sum(r[1] / u for r, u in zip(runs, unit)), seq, runs
+    cost, lats, fore, back = cases[0]
     prio = [0.0] * n
     for i in range(n - 1, -1, -1):
-        prio[i] = cost[i] + max([prio[k] + dl for k, dl in suc[i]] + [lats[i]])
-    at = place(sorted(range(n), key=lambda i: -prio[i]), fore, zero)
-    best = (finish(at), at, sorted(range(n), key=lambda i: at[i]))
+        prio[i] = max([prio[k] - cost[k] + dl for k, dl in back[i]] + [lats[i]]) + cost[i]
+    seq = packed([-x for x in prio], *cases[0])
+    unit = [replay(seq, *x)[1] for x in cases]
+    unit[0] /= 2.5
+    best = judged(seq)
     rnd = 12345
     for it in range(PASSES):
-        end, old, seq = best
+        old, end = best[2][0]
         rnd = (rnd * 1103515245 + 12345) % 2147483648
         mid = end * (rnd / 2147483648.0)
         amp = AMP * (1 + rnd // 1024 % 4)
-        first = 0
-        while first < n - 1 and old[seq[first]] < mid - SPAN:
-            first += 1
         key = list(old)
         for i in range(n):
             x = old[i]
@@ -850,17 +893,56 @@ def order(nodes):
                 if x < mid + SPAN:
                     rnd = (rnd * 1103515245 + 12345) % 2147483648
                     x += amp * (rnd / 2147483648.0 - 0.5)
-                for j, dl in pre[i]:
+                for j in pre[i]:
                     if key[j] >= x:
                         x = key[j] + 1.0
                 key[i] = x
-        at = place(sorted(seq[first:], key=lambda i: key[i]), fore, zero, seq[:first], old)
-        at2 = turned(at)
-        if finish(at2) <= finish(at):
-            at = at2
-        if finish(at) <= end:
-            best = (finish(at), at, sorted(range(n), key=lambda i: at[i]))
-    return deps, best[2], best[1]
+        new = judged(packed(key, *cases[0]), 1.006 * end)
+        if new[0] <= best[0]:
+            best = new
+    chains = {}
+    for it in range(SWAPS):
+        score, seq, runs = best
+        rnd = (rnd * 1103515245 + 12345) % 2147483648
+        c = rnd // 64 % len(cases)
+        if c not in chains:
+            cost, lats, fore, back = cases[c]
+            at = runs[c][0]
+            prev, last = {}, {}
+            for k in seq:
+                prev[k] = last.get(queue[k])
+                last[queue[k]] = k
+            k = max(ends, key=lambda i: at[i] + cost[i] + lats[i])
+            chains[c] = []
+            while k is not None:
+                p = prev[k]
+                if p is not None and queue[k] < 5 and at[p] + cost[p] >= at[k] - 0.5 and p not in pre[k]:
+                    chains[c].append((p, k))
+                    k = p
+                else:
+                    k = max(fore[k], key=lambda z: at[z[0]] + z[1])[0] if fore[k] else None
+        if not chains[c]:
+            continue
+        a, b = chains[c][rnd // 4096 % len(chains[c])]
+        lo, hi = seq.index(a), seq.index(b)
+        for step in range(rnd // 16 % 4 if rnd // 8 % 2 else 0):
+            z = lo - 1
+            while z >= 0 and queue[seq[z]] != queue[b]:
+                z -= 1
+            lo = z if z >= 0 else lo
+        need, part = set(pre[b]), [b]
+        for k in reversed(seq[lo:hi]):
+            if k in need:
+                part.append(k)
+                need.update(pre[k])
+        if seq[lo] in need:
+            continue
+        gone = set(part)
+        new = judged(seq[:lo] + part[::-1] + [k for k in seq[lo:hi] if k not in gone] + seq[hi + 1:], 1.003 * runs[0][1])
+        if new[0] <= score:
+            best = new
+            chains = {}
+    return deps, best[1], best[2][0][0]
 
 
 def rank_program(g, core, T, topo):

@@ -4,19 +4,12 @@ from concourse.mybir import AluOpType as A, AxisListType, ActivationFunctionType
 V, GH, W, LN, RO = 1024, 896, 2816, 256, 4
 WD = W + LN + 128
 BIG = float(2 ** 26)
-CLAMP = float(4080 * 4096)
-NX = (2, 4)
-SUB = [(), (2,), (2,), (2,)]
-RELU = (2,)
-PLAIN = [(), (3,), (3,), (3,)]
-PLAIN2 = [{}, {}, {}, {0: "near"}]
-OPT = dict(kt="a", vf="a", bd="a", xv="am", zz="mm")
-CH0 = [[(4, "v"), (4, "a"), (4, "a"), (4, "a")]] * 2
-CH = [[(4, "a"), (4, "a"), (8, "a")], [(8, "a"), (8, "a")]]
-CO0 = [[(4, "v"), (4, "a"), (8, "a")], [(8, "a"), (8, "a")]]
-CO = [[(8, "a"), (8, "a")], [(8, "a"), (8, "a")]]
-ND1 = [(1, 1, 2, 2, 2), (2, 2, 4), (4, 4), (4, 4)]
-OFF1, OFF2 = (), ()
+R13 = 1.5 * 2 ** 36
+MID = 1408.0
+LO = 64.0
+GE = [[["va", "aa"], ["aa", "aa"]]] * RO
+NC = [[1, 1], [1, 1], [1, 2]]
+OPT = dict(vf="a", bd="a", xf="aavava", lg="vvvv", eq="v", z="vv", fg="a")
 PEC, DLAT, PASSES, SWAPS, AMP, SPAN = 0.5, 3600, 10500, 12000, 2000.0, 3500.0
 CASES = [(1.56, 3.8, 0.5, 150.0, 1.0), (1.2, 2.5, 0.55, 140.0, 1.0), (1.9, 5.2, 0.5, 105.0, 0.7), (1.4, 4.6, 0.45, 190.0, 1.35)]
 PLAN = []
@@ -29,59 +22,62 @@ def _buf(names, n, dtp, where="sbuf"):
         SCRATCH[x] = (where, [128, n], dtp)
 
 
-_buf("X NB", WD, "bfloat16")
-_buf("MH ZZ XV", V, "bfloat16")
-_buf("L M B", WD, "float32")
+_buf("X NB", W, "bfloat16")
+_buf("MH D2", V, "bfloat16")
+_buf("L M B XF XR", WD, "float32")
 _buf("HI", V, "int32")
 _buf("GA", GH, "bfloat16")
 _buf("GL", GH, "float16")
 _buf("LG", 2 * GH, "float16")
 _buf("IF", 128, "float16")
-_buf("ZS ZT", 256, "float16")
-_buf("LM", 2 * GH, "bfloat16")
-_buf("DC DO D0 D1 D2 E XC", 4096, "bfloat16")
+_buf("ZT", 256, "float16")
+_buf("GC GO", 4096, "float32")
+_buf("DA DB DC E", 4096, "bfloat16")
 _buf("ROWS", 2048, "bfloat16")
-_buf("HB EU EO PN ONE", 512, "bfloat16")
-_buf("SA SX SN SM SP S32 WG", 144, "bfloat16")
-_buf("Z0 IU", 144, "float32")
-_buf("RN BD32 BDC BD1 IBIG I24 I1 IM1 I014 IH WBH I13 IM13 BDW BDB BJM IMG IMH", 128, "bfloat16")
-_buf("WBL IG MT I1F", 128, "float32")
-_buf("BJ", 384, "bfloat16")
-_buf("MB MZ", 272, "float32")
-_buf("NL", 272, "int32")
-_buf("A1 A2 FG", 320, "float32")
-_buf("Z", 576, "float32")
+_buf("HB ONE HF", 512, "bfloat16")
+_buf("EU", 1280, "bfloat16")
+_buf("SA SN S32", 144, "bfloat16")
+_buf("Z0 IU SQ", 144, "float32")
+_buf("RN RM BD1 IBIG IMB I1 WBH BDW BDB BJM WPS CB1 CB0 CB2 IH BM8 BM4 MK RS", 128, "bfloat16")
+_buf("WBL IG IR MT I1F IM1F", 128, "float32")
+_buf("BJ BD4", 256, "bfloat16")
+_buf("MB MZ NL", 272, "float32")
+_buf("FG", 320, "float32")
 _buf("MV", 272, "bfloat16")
-_buf("CF KC VT CL RF", 256, "float32")
-_buf("RZ PW2 I256 CR EQ BB BK BY TH MC NN CN", 256, "bfloat16")
-_buf("RI", 256, "int32")
-_buf("RU CU RU2 OU PR", 256, "uint16")
+_buf("KC CL RF KS KM LH QV MF LF ZF", 256, "float32")
+_buf("QS", 512, "float32")
+_buf("PW2 I256 CR EQ BB TH MC NN CN XV XB ZZ", 256, "bfloat16")
+_buf("CU OU PR", 256, "uint16")
 _buf("FW", 64, "uint16")
 _buf("fw", 160, "uint16")
-_buf("KT", 448, "float32")
 _buf("w", 768, "float32")
 _buf("c", 256, "float32")
 _buf("ci", 128, "int32")
-_buf("wi", 48, "int32")
+_buf("wi", 224, "int32")
 _buf("wb", 32, "bfloat16")
+_buf("WG", 8, "bfloat16")
+_buf("WQ", 16, "float32")
 _buf("u", 128, "uint16")
-_buf("cu", 32, "uint16")
+_buf("cu", 8, "uint16")
 _buf("MS", 64, "bfloat16")
 _buf("q", 200, "float32")
 _buf("YF", 64, "float32")
-_buf("ME0 ME1 ME2", 164, "float32")
-_buf("LE0 LE1 LE2", 200, "float32")
-_buf("ML0 ML1 ML2", 32, "float32")
-_buf("LL0 LL1 LL2", 64, "float32")
-_buf("PC K0 UE UX KK0 KK1 PA PW", 512, "float32", "psum")
+_buf("ME0 ME1 ME2", 132, "float32")
+_buf("LE0 LE1 LE2", 136, "float32")
+_buf("ML0 ML1 ML2 LL0 LL1 LL2", 64, "float32")
+_buf("Q0 Q1 K0 K1 Y0 Y1 PA PW", 512, "float32", "psum")
 
-SEMAPHORES = (["sv", "sa", "sp", "sg", "dx", "dy", "dn", "dm", "dh", "dl", "dt", "ox", "ol", "of", "tx", "rx", "tl", "rl", "tp", "rp"]
+SEMAPHORES = (["sv", "sa", "sp", "sg", "dx", "dn", "dm", "dh", "dl", "dt", "ox", "ol", "of", "tx", "rx", "tl", "rl"]
               + ["%s%d" % (a, t) for a in ("te", "re", "tm", "rm") for t in range(RO - 1)] + ["m%d" % j for j in range(1, 40)])
 SHORT = ("bfloat16", "uint16", "float16")
 
 
 def S(name, lo=0, hi=None, st=1, p=None):
     return (name, lo, SCRATCH[name][1][1] if hi is None else hi, st, p)
+
+
+def step(name, lo, n, st):
+    return S(name, lo, lo + st * (n - 1) + 1, st)
 
 
 def IND(win, off):
@@ -163,9 +159,6 @@ def build(g, core, T, topo):
     def mset(out, val):
         return node("v", max(64, cnt(out) * narrow(out)), lambda: g.vector.memset(ap(out), val), [out], [])
 
-    def tr(out, i0):
-        return node("v", cnt(out) + 10, lambda: g.vector.transpose(ap(out), ap(i0)), [out], [i0])
-
     def act(out, i0, bias=None, scale=None, func=F.Identity, accum=None):
         kw = {}
         if bias is not None:
@@ -180,6 +173,9 @@ def build(g, core, T, topo):
 
     def times(e, out, i0, wt):
         return act(out, i0, scale=wt) if e == "a" else ts(out, i0, wt, A.mult)
+
+    def plus(e, out, i0, b):
+        return act(out, i0, bias=b) if e == "a" else ts(out, i0, b, A.add)
 
     def scat(win, off, src):
         return act(IND(win, off), src, func=F.Silu)
@@ -197,7 +193,7 @@ def build(g, core, T, topo):
         return S(fam, 15 - r, 143 - r)
 
     def fold(out, fam, src, lo, n, start, stop):
-        return mm([(out, sel(fam, r), S(src, lo + r, lo + r + 16 * (n - 1) + 1, 16)) for r in range(16)], start, stop)
+        return mm([(out, sel(fam, r), step(src, lo + r, n, 16)) for r in range(16)], start, stop)
 
     def iota(out, pat, base, cm=0, after=()):
         if dty(out) == "int32":
@@ -232,7 +228,7 @@ def build(g, core, T, topo):
 
     dma("s", lambda: T.X[:, 0:V], lambda: T.feat[:], "dx", 3500, outs=[S("X", 0, V)])
     dma("a", lambda: T.HI[:], lambda: T.hits[:], "dh", 4500, outs=[S("HI")])
-    dma("s", lambda: T.wi[:, 32:48], lambda: T.lane0[:], "dl", 2500, outs=[S("wi", 32, 48)])
+    dma("s", lambda: T.wi[:, 48:64], lambda: T.lane0[:], "dl", 2500, outs=[S("wi", 48, 64)])
     sent = exchange([S("X", 0, GH)] * 2, [S("X", V, V + GH), S("X", V + GH, W)], "tx", "rx", 6000)
 
     def c(j, n=1):
@@ -241,23 +237,20 @@ def build(g, core, T, topo):
     def ci(j, n=1):
         return S("ci", j, j + n)
 
-    def wg(j, n=1):
-        return S("WG", 8 * j, 8 * (j + n))
-
     def fill(out, val):
         return iota(out, [[0, cnt(out)]], val, after=[sent])
-    ROW, GRP, PAR, PID, G15, WN, WS, WM, W014, WH, R4A, R4B, TMP, TMP2, WP, TC2, TC3 = [c(j) for j in range(17)]
+    ROW, GRP, HW, PID, G15, WN, PSI, R4A, R4B, MCB, BB1, TMP, TMP2, TC = [c(j) for j in range(14)]
     DUMP, D8, G8, TH8, T16a, I16 = c(64, 32), c(112, 8), c(128, 8), c(136, 8), c(144, 16), c(192, 16)
-    OENT, OBC = S("cu", 0, 8), S("cu", 16, 32)
+    OMIN = S("cu")
     first = [iota(ci(0), [[0, 1]], 0, 1), iota(S("IU"), [[1, 144]], 0), iota(S("IG"), [[1, 8], [0, 16]], 0)]
     iota(S("NB", 0, V), [[32, V // 256], [0, 256]], 0, after=[iota(S("I256"), [[32, 256]], 0, after=first)])
     iota(S("NB", V, W), [[32, (W - V) // 256], [0, 256]], 32 * V // 256, after=[sent])
+    iota(S("IR"), [[0, 8], [1, 16]], 0, after=[sent])
     dma("s", lambda: T.NB[1::16, 0:V], lambda: T.I256[0:32, :], "dn", 2500, outs=[S("NB", 0, V)], ins=[S("I256")])
     dma("s", lambda: T.NB[1::16, V:W], lambda: T.I256[0:56, :], "dm", 2500, outs=[S("NB", V, W)], ins=[S("I256")])
     ts(ci(1), ci(0), 15, A.bitwise_and)
     ts(ci(2), ci(0), 4, A.arith_shift_right)
-    ts(ci(3), ci(2), 1, A.bitwise_and)
-    cp(c(0, 3), ci(1, 3))
+    cp(c(0, 2), ci(1, 2))
     cp(PID, ci(0))
     ts(G15, GRP, 16.0, A.mult, 15.0, A.add)
     cp(I16, S("IU", 0, 16))
@@ -266,35 +259,32 @@ def build(g, core, T, topo):
     ts(TMP, mk(0), 4.0, A.mult)
     ts(TMP2, mk(1), 1.0 / 32, A.mult, TMP, A.add)
     ts(WN, mk(4), 4.0, A.mult, TMP2, A.add)
-    ts(c(19), mk(2), mk(10), A.add, mk(6), A.subtract)
-    ts(WS, c(19), -128.0, A.mult)
-    ts(c(17), mk(10), mk(6), A.add, 256.0, A.mult)
-    tt(WM, WN, WS, A.add)
-    tt(WP, WN, WS, A.subtract)
-    ts(W014, mk(0), mk(1), A.add, mk(4), A.add)
-    tt(WH, mk(2), mk(10), A.subtract)
-    ts(R4A, mk(4), 32.0 * V / 128, A.mult)
-    ts(R4B, mk(4), 32.0 * (V + GH) / 128, A.mult)
+    ts(c(14), mk(12), mk(13), A.add, 85.0 / 4096, A.mult)
+    ts(HW, mk(14), 86.0 / 4096, A.mult, c(14), A.add)
+    ts(c(15), mk(15), 128.0 / 4096, A.mult)
+    ts(PSI, HW, 5.0, A.mult, c(15), A.add)
+    ts(R4A, HW, -float(V // 256), A.mult)
+    ts(R4B, HW, -float((V + GH) // 256), A.mult, c(15), A.subtract)
+    ts(MCB, mk(0), -MID / 4, A.mult)
+    ts(BB1, mk(1), -32 * LO, A.mult)
     ts(S("S32"), S("IU"), G15, A.is_equal, 32.0, A.mult)
-    for fam, wt in (("SN", WN), ("SM", WM), ("SP", WP), ("Z0", mk(0))):
+    for fam, wt in (("SN", WN), ("Z0", mk(0))):
         ts(S(fam), S("S32"), wt, A.mult, 1.0 / 32, A.mult)
-    for fam, wt in (("SA", 256.0), ("SX", -128.0)):
+    for fam, wt in (("SA", 256.0), ("SQ", -128.0)):
         times("a", S(fam), S("S32"), wt)
     ts(S("BD1"), S("IG"), GRP, A.is_equal)
     ts(S("I1"), S("IU", 0, 128), PID, A.is_equal)
-    for e, m, base, wt in (("v", "RN", "BD1", WN), ("a", "BDC", "BD1", -float(2 ** 20)), ("v", "IBIG", "I1", BIG), ("a", "I1F", "I1", 1.0),
-                           ("a", "IM1", "I1", -1.0), ("a", "I24", "I1", float(2 ** 24)), ("v", "I014", "I1", W014), ("v", "IH", "I1", WH),
-                           ("a", "I13", "I1", 8192.0), ("a", "IM13", "I1", -8192.0), ("v", "IF", "I1", 1.0)):
+    for e, m, base, wt in (("v", "RN", "BD1", WN), ("v", "IBIG", "I1", BIG), ("a", "I1F", "I1", 1.0), ("a", "IM1F", "I1", -1.0),
+                           ("v", "RM", "RN", -1.0), ("a", "IMB", "I1", -BIG), ("v", "IF", "I1", 1.0), ("v", "IH", "I1", 0.5)):
         times(e, S(m), S(base), wt)
-    times("a", S("RZ", 0, 128), S("RN"), -1.0)
-    mset(S("RZ", 128, 256), 0.0)
-    ts(S("IMG"), S("IH"), 1.5 * 2 ** 32, A.mult)
-    ts(S("IMH"), S("IH"), -1.5 * 2 ** 32, A.mult)
-    tt(S("BD32"), sel("S32", 2), sel("S32", 10), A.subtract)
     ts(S("WBL"), sel("Z0", 1), 32.0, A.mult)
     ts(S("MT"), sel("Z0", 0), 1.0 / 4, A.mult)
     tt(S("WBH"), S("MT"), S("WBL"), A.subtract)
     mset(S("ONE"), 1.0)
+    ts(G8, S("IU", 0, 8), GRP, A.is_equal)
+    mset(S("WPS"), 0.0)
+    for r, j, wt in ((12, 0, 85.0), (13, 0, 85.0), (14, 0, 86.0), (15, 1, 1.0)):
+        ts(step("WPS", r, 8, 16), G8, mk(j), A.mult, -wt / 2 ** 17, A.mult)
     for r in range(0, 16, 4):
         node("g", 200 + 1024, lambda r=r: g.affine_select(T.ROWS[:, 128 * r:128 * r + 512], T.ONE[:], [[1, 4], [16, 8], [0, 16]], A.is_equal, 0.0, r, -1),
              [S("ROWS", 128 * r, 128 * r + 512)], [S("ONE")], after=[sent])
@@ -305,25 +295,28 @@ def build(g, core, T, topo):
     tt(c(48, 16), S("PW2", 0, 16), c(224, 16), A.mult)
     total(c(21), c(48, 16))
     ts(S("BDW"), S("BD1"), c(21), A.mult, 0.5, A.mult)
-    for m, wt in ((S("BDB"), 65536.0), (S("BY", 0, 128), -1.0), (S("BY", 128, 256), 1.0), (S("BJ", 0, 128), 1.0 / 16), (S("BJM"), -1.0 / 16),
-                  (S("BJ", 128, 256), 1.0 / 8), (S("BJ", 256, 384), 1.0 / 8)):
+    for m, wt in ((S("BDB"), 65536.0), (S("BJM"), -1.0 / 16), (S("BJ", 0, 128), -512.0), (S("BJ", 128, 256), 512.0),
+                  (S("BD4", 0, 128), 4096.0), (S("BD4", 128, 256), 4096.0), (S("BM8"), -8192.0), (S("BM4"), -4096.0)):
         times(OPT["bd"], m, S("BD1"), wt)
-    ts(G8, S("IU", 0, 8), GRP, A.is_equal)
-    ts(c(31), WS, -1.0 / 4096, A.mult)
-    ts(c(160, 8), G8, -1.0, A.mult)
-    cp(c(168, 8), G8)
-    cp(c(176, 8), c(160, 8))
-    for j, n, base, wt in ((0, 1, G8, WN), (1, 1, G8, WN), (2, 3, c(160, 24), c(31)), (5, 2, c(160, 16), 1.0), (7, 2, c(160, 16), -2.0), (9, 1, G8, 8192.0),
-                           (10, 1, G8, WM), (11, 1, G8, WP), (12, 2, c(160, 16), 4096.0)):
-        times("a", wg(j, n), base, wt)
+    times("a", S("WG"), G8, 8192.0)
+    for lo in (0, 8):
+        times("a", S("WQ", lo, lo + 8), G8, -4096.0)
+    fill(S("CB1"), 0)
+    for lo, hi, val in ((0, 64, R13 / 64), (64, 96, -float(2 ** 19)), (96, 97, 32768.0)):
+        mset(S("CB1", p=(lo, hi)), val)
+    mset(S("CB0"), -R13 / 128)
+    mset(S("CB2"), R13 / 256)
+    for j, val in enumerate((0.5, -1.0 / 512, -2.0 ** -13, 2.0 ** -13)):
+        mset(S("HF", 128 * j, 128 * j + 128), val)
+    ts(S("MK"), S("IR"), ROW, A.is_equal)
+    ts(S("RS"), S("IR"), 0.0, A.is_equal, BIG, A.mult)
+    ts(OMIN, c(192, 8), 16.0, A.mult, 15.0, A.add)
     for b in ("MV", "MB"):
         fill(S(b, 256, 272), 128)
-    for b in ("MZ", "NL"):
-        fill(S(b, 256, 272), 0)
-    for lo, hi in ((0, 16), (144, 176), (304, 320)):
-        mset(S("A1", lo, hi), 0.0)
-        fill(S("A2", lo, hi), 0)
-    fill(S("M", W, WD), 0)
+    fill(S("MZ", 256, 272), 0)
+    fill(S("NL", 256, 272), int(LO))
+    fill(S("XF", W, WD), 0)
+    fill(S("TH", 128, 256), 0)
     fill(S("B", V, V + 8), 128)
     ts(T16a, I16, 16.0, A.mult, ROW, A.add)
     ts(c(64, 16), T16a, float(W), A.add)
@@ -331,17 +324,6 @@ def build(g, core, T, topo):
     ts(D8, c(144, 8), float(W - V + LN), A.add)
     ts(c(120, 4), c(116, 4), -float(GH), A.add)
     ts(c(18, 2), c(144, 2), 0.5, A.add)
-    ts(ci(4), ci(0), 7, A.bitwise_and)
-    ts(ci(5), ci(1), 3, A.arith_shift_right)
-    tt(ci(6), ci(1), ci(3), A.add)
-    ts(ci(7), ci(6), 1, A.bitwise_and)
-    cp(c(24, 4), ci(4, 4))
-    ts(TMP, c(24), 16.0, A.mult, c(25), A.add)
-    ts(TMP2, c(27), 144.0, A.mult, TMP, A.add)
-    ts(OENT, c(192, 8), 2.0, A.mult, TMP2, A.add)
-    ts(S("cu", 16, 24), c(192, 8), 0.0, A.mult, c(24), A.add)
-    ts(c(28), c(24), 8.0, A.add)
-    ts(S("cu", 24, 32), c(192, 8), 0.0, A.mult, c(28), A.add)
     dma("g", lambda: T.ci[0:1, 96:104], lambda: T.th[:], "dt", 3000, outs=[ci(96, 8)], allow_slow_non_contiguous=True)
     node("g", 200, lambda: g.partition_broadcast(T.ci[:, 104:112], T.ci[0:1, 96:104], 128), [ci(104, 8)], [ci(96, 8)])
     tt(TH8, ci(104, 8), G8, A.mult)
@@ -349,35 +331,37 @@ def build(g, core, T, topo):
     cp(ci(8), c(20))
     ts(ci(9), ci(8), 15, A.bitwise_and)
     ts(ci(10), ci(8), 4080, A.bitwise_and)
-    ts(c(22), ci(9), 0.5, A.add, mk(1), A.mult)
+    ts(c(22), ci(9), 8.5, A.add, mk(1), A.mult)
     ts(c(23), ci(10), mk(0), A.mult, c(22), A.add)
-    ts(c(29), mk(2), -16384.0, A.mult)
-    tt(TC2, c(29), c(23), A.subtract)
-    tt(TC3, c(29), c(23), A.add)
-    times("a", S("TH", 0, 128), S("BD1"), TC2)
-    times("a", S("TH", 128, 256), S("BD1"), TC3)
+    ts(c(24), mk(2), -4096.0, A.mult, c(23), A.add)
+    ts(TC, mk(3), BIG / 4096, A.mult, c(24), A.add)
+    ts(S("TH", 0, 128), S("BD1"), TC, A.mult, 4096.0, A.mult)
 
-    cp(S("L", 0, V), S("HI"))
-    act(S("GA"), S("L", 0, GH), bias=float(GH), scale=-1.0, func=F.Relu)
-    for bank, lo, hi in (("KK0", 0, 512), ("KK1", 512, GH)):
+    ts(S("L", 0, V), S("HI"), LO, A.add)
+    act(S("GA"), S("L", 0, GH), bias=GH + LO, scale=-1.0, func=F.Relu)
+    for bank, lo, hi in (("K0", 0, 512), ("K1", 512, GH)):
         mm([(S(bank, 0, hi - lo), S("RN"), S("NB", lo, hi)), (S(bank, 0, hi - lo), S("IBIG"), S("GA", lo, hi))], True, True)
-        tt(S("GL", lo, hi), S(bank, 0, hi - lo), S("L", lo, hi), A.min)
+        tt(S("GL", lo, hi), S(bank, 0, hi - lo), S("HI", lo, hi), A.min)
     exchange([S("GL")] * 2, [S("LG", 0, GH), S("LG", GH, 2 * GH)], "tl", "rl", 6000)
-    for lo in (0, 512):
-        act(S("D2", lo, lo + 512), S("L", lo, lo + 512))
-        mm([(S("KK0"), S("WBH"), S("D2", lo, lo + 512)), (S("KK0"), S("WBL"), S("L", lo, lo + 512))], True, True)
-        act(S("B", lo, lo + 512), S("KK0"))
 
-    def pieces(out, names, x, o):
-        one = S("ONE", 0, cnt(out))
-        mm([(o, S("IMG"), one), (o, S("BD32"), x), (o, S("IMH"), one), (o, sel("S32", 10), x)] + ([(o, S("I014"), names)] if names else []), True, True)
-        act(out, o, bias=c(17))
+    def entry(e, out, names, x, o):
+        mm([(o, S("I1"), x), (o, S("WPS"), names)], True, True)
+        plus(e, out, o, PSI)
 
+    for j, lo in enumerate((0, 512)):
+        entry(OPT["xf"][j], S("XF", lo, lo + 512), S("NB", lo, lo + 512), S("X", lo, lo + 512), S("Q%d" % j))
+    act(S("XR", 0, V), S("X", 0, V), scale=32.0)
+    fill(S("XR", V, V + 8), 0)
+    for j, bank in enumerate(("Q0", "Q1", "Y1", "K0")):
+        lo, hi, o = V + GH // 2 * j, V + GH // 2 * (j + 1), S(bank, 0, GH // 2)
+        mm([(o, S("WPS"), S("NB", lo, hi))], True, False)
+        mm([(o, S("I1"), S("X", lo, hi))], False, True)
+        plus(OPT["xf"][2 + j], S("XF", lo, hi), o, PSI)
     for lo in (0, 512):
-        pieces(S("MH", lo, lo + 512), None, S("X", lo, lo + 512), S("KK1"))
-    move("g", S("M", 0, W), S("NB", 0, W), behind=[S("LG")])
-    move("g", S("M", 0, V), S("MH"), slice(2, None, 4))
-    exchange([S("MH", 0, GH)] * 2, [S("LM", 0, GH), S("LM", GH, 2 * GH)], "tp", "rp", 6000)
+        act(S("D2", lo, lo + 512), S("L", lo, lo + 512), bias=-LO)
+        mm([(S("K1"), S("WBH"), S("D2", lo, lo + 512)), (S("K1"), S("WBL"), S("L", lo, lo + 512))], True, True)
+        act(S("B", lo, lo + 512), S("K1"), bias=BB1)
+    move("g", S("M", 0, V), S("NB", 0, V), behind=[S("LG")])
 
     def w(j, n=1):
         return S("w", 16 * j, 16 * (j + n))
@@ -385,303 +369,204 @@ def build(g, core, T, topo):
     def u(j, n=16):
         return S("u", j, j + n)
 
+    def wi(j, n=16):
+        return S("wi", j, j + n)
+
     def fw(t, lo, n):
         return S("fw", 40 * t + lo, 40 * t + lo + n)
     VF, VA, AW, VM, JN, G1, J1, VL = [w(j) for j in range(8)]
-    BF, CT = w(11), w(12)
+    BI, CI = wi(16), wi(32)
     PU, VU, BU, OL, BBU, SU = u(0), u(16), u(32), u(48), u(64), u(96, 4)
     NJ, TL = S("wb", 0, 16), S("wb", 16, 32)
 
-    def pair(b):
-        return S(b, 384, 640)
+    def half(b, h, lo=0):
+        return S(b, lo + 128 * h, lo + 128 * h + 128)
 
-    def rep(b, h, n):
-        return S(b, 512 - 128 * n, 512) if h == 0 else S(b, 512, 512 + 128 * n)
-
-    def repeat(b, h, n, e="a"):
-        if e == "s":
-            for j in range(1, n):
-                lo = 384 - 128 * j if h == 0 else 512 + 128 * j
-                move("s", S(b, lo, lo + 128), rep(b, h, 1))
-            return
-        if e == "m":
-            act(S(b, 256 + 384 * h, 384 + 384 * h), rep(b, h, 1))
-            move("s", S(b, 768 * h, 768 * h + 256), rep(b, h, 2))
-            return
-        if n >= 2:
-            act(S(b, 256 + 384 * h, 384 + 384 * h), rep(b, h, 1))
-        if n >= 4:
-            act(S(b, 768 * h, 768 * h + 256), rep(b, h, 2))
+    def one(n):
+        return S("ONE", 0, n)
 
     def lanes(t):
         if t == 0:
-            cp(VU, S("wi", 32, 48))
-            cp(VF, S("wi", 32, 48))
+            cp(VU, wi(48))
+            cp(VF, wi(48))
             act(S("MV", 0, LN), IND(S("NB", 0, V), VU))
         else:
             act(S("MV", 0, LN), IND(S("M", 0, V), PU))
             fold(S("PW", 0, 16), "SN", "MV", 0, 16, True, True)
             cp(VU, S("PW", 0, 16))
             (act if OPT["vf"] == "a" else cp)(VF, S("PW", 0, 16))
-        mm([(S("PA", 0, LN), S("RN"), S("MV", 0, LN))], True, True)
-        cp(S("PR"), S("PA", 0, LN))
-        mm([(S("PA", 128 * h, 128 * h + 128), S("MV", 128 * h, 128 * h + 128), S("RN")) for h in range(2)], True, True)
-        act(S("CL"), S("PA", 0, LN), bias=CLAMP)
+        mm([(S("PW", 256, 512), S("RN"), S("MV", 0, LN))], True, True)
+        cp(S("PR"), S("PW", 256, 512))
         for s in range(16):
             ts(S("E", 272 * s, 256 * s + 256), S("PR", 16 * s, 256), S("w", s, s + 1), A.is_equal)
+
+    def awake(t):
+        mm([(half("PA", h), half("MV", h), S("RN")) for h in range(2)], True, True)
+        act(S("CL"), S("PA", 0, LN), bias=-MID)
         mm([(S("PA", 0, LN), S("BJM"), S("PW2"))], True, False)
         for q in range(0, 16, 4):
             mm([(S("PA", 16 * s, 16 * s + 16), S("BDW"), S("E", 272 * s, 272 * s + 16)) for s in range(q, q + 4)]
                + [(S("PA", 16 * s + 16, LN), S("BDB"), S("E", 272 * s + 16, 256 * s + 256)) for s in range(q, min(q + 4, 15))], False, q == 12, True)
         act(S("CR"), S("PA", 0, LN), bias=1.0, func=F.Relu)
-        fold(S("PW", 16, 32), "SA", "CR", 0, 16, True, True)
-        tt(VA, S("PW", 16, 32), VF, A.add)
+        fold(S("PA", 256, 272), "SA", "CR", 0, 16, True, True)
+        tt(VA, S("PA", 256, 272), VF, A.add)
         tt(VM, VA, c(64, 16), A.min)
         cp(OL, VM)
         if t < RO - 1:
             ts(AW, VM, float(V), A.is_ge, -16384.0, A.mult)
             ts(AW, AW, -8192.0, A.add)
-        act(S("VT"), IND(VF, OBC))
+            move("g", S("MF"), S("MV", 0, LN))
 
-    def names(t, h, off, lwin, abuf, raw, outu, outf, dm, pn, chunks, each):
-        a, z, o = 160 * h, 288 * h, 128 * h
-        act(S(abuf, a + 16, a + 144), IND(lwin, S(off[0], off[1] + 8 * h, off[1] + 8 * h + 8)))
-        tr(S("Z", z, z + 128), S(abuf, a + 16, a + 144))
-        tr(S("Z", z + 128, z + 288), S(abuf, a, a + 160))
-        cp(S(raw if t else outu, o, o + 128), IND(S("Z", z, z + 288), OENT))
-        if t == 0 and outf:
-            act(S(outf, o, o + 128), IND(S("Z", z, z + 288), OENT))
-        k = 16 * h
-        for n, e in chunks:
-            get = cp if e == "v" else act
-            if t == 0:
-                get(S(dm, 128 * k, 128 * (k + n)), IND(S("X", 0, W), S(outu, 8 * k, 8 * (k + n))))
-            else:
-                get(S(dm, 128 * k, 128 * (k + n)), IND(S("M", 0, W), S(raw, 8 * k, 8 * (k + n))))
-                fold(S("PC", pn + 8 * k, pn + 8 * (k + n)), "SN", dm, 128 * k, 8 * n, True, True)
-                cp(S(outu, 8 * k, 8 * (k + n)), S("PC", pn + 8 * k, pn + 8 * (k + n)))
-            each(k, k + n)
-            k += n
+    def spread(out, src, h, wts):
+        return (out, half(src, h), wts)
 
-    def far(buf, offs, y, lo, hi, n):
-        for k in range(lo, hi, n):
-            tt(S(buf, 128 * k, 128 * (k + n)), IND(S("X", 0, W), S(offs, 8 * k, 8 * (k + n))), rep(y, k // 16, n), A.max)
+    def four(src, h):
+        mm([(step("Y%d" % h, j, 128, 4), S("I1"), half(src, h)) for j in range(4)], True, True)
 
-    def near(buf, src, lo, hi, y=None):
-        for k in range(lo, hi, 2):
-            tt(S(buf, 128 * k, 128 * k + 256), S(src, 128 * k, 128 * k + 256), y or S("PC", 256 * (k // 16), 256 * (k // 16) + 256), A.max)
+    def entries(t, i, h, off, lwin, ub, gb):
+        q = S("Q%d" % h, 0, 128)
+        rows = IND(lwin, S(off[0], off[1] + 8 * h, off[1] + 8 * h + 8))
+        if OPT["lg"][2 * i + h] == "a":
+            act(half("LF", h), rows)
+            rows = half("LF", h)
+        ts(half(ub, h), rows, 0.25 - LO, A.add)
+        n = 128 // len(GE[t][i][h])
+        for j, e in enumerate(GE[t][i][h]):
+            lo = 128 * h + n * j
+            (cp if e == "v" else act)(S(gb, 16 * lo, 16 * (lo + n)), IND(S("XF", 0, W), S(ub, lo, lo + n)))
+        mm([spread(S(q[0], 0, 256), "XV", h, S("BD4")), spread(S(q[0], 128, 256), "MV", h, S("RM"))], True, False)
+        for k0 in range(0, 16, 2):
+            mm([(step(q[0], k, 16, 16), step(gb, 2048 * h + k, 128, 16), S("WQ")) for k in (k0, k0 + 1)], False, k0 == 14, True)
+        ts(eu(h, 2 * i), S(q[0], 128, 256), -MID, A.is_equal, float(2 ** 24), A.mult)
+        tt(S("QS", 256 * h + 128 * i, 256 * h + 128 * i + 128), q, eu(h, 2 * i), A.add)
 
-    def less(lo, hi, n):
-        for k in range(lo, hi, n):
-            d, r = S("XC", 128 * k, 128 * (k + n)), S("D0", 128 * k, 128 * (k + n))
-            tt(d, IND(S("X", 0, W), S("CU", 8 * k, 8 * (k + n))), rep("XV", k // 16, n), A.subtract)
-            if k // 8 in RELU:
-                act(r, d, scale=-1.0, func=F.Relu)
-            else:
-                ts(r, d, -1.0, A.mult, 0.0, A.max)
+    def eu(h, j):
+        return S("EU", 640 * h + 128 * j, 640 * h + 128 * j + 128)
 
-    def again(j):
-        for x in (1024 * j, 1024 * j + 512):
-            mm([(S("K0"), S("I1"), rep("ZZ", j // 2, 4)), (S("K0"), S("IM1"), rep("XV", j // 2, 4)), (S("K0"), S("IM1"), S("XC", x, x + 512))], True, True)
-            act(S("D1", x, x + 512), S("K0"), func=F.Relu)
-
-    def over(buf, src, j):
-        for x in (1024 * j, 1024 * j + 512):
-            mm([(S("K0"), S("I1"), rep("ZZ", j // 2, 4)), (S("K0"), S("IM1"), S(src, x, x + 512))], True, True)
-            act(S(buf, x, x + 512), S("K0"), func=F.Relu)
-
-    def lift(bank, lo, src, j, wts, stop=False, after=()):
-        n = cnt(wts)
-        return mm([(S(bank, lo + k % 16, lo + k % 16 + 16 * (n - 1) + 1, 16), S(src, 128 * k, 128 * k + 128), wts) for k in range(8 * j, 8 * j + 8)],
-                  False, stop, True, after)
-
-    def spread(bank, lo, src, h, wts, start=False, stop=False, free=True, after=()):
-        return mm([(S(bank, lo, lo + cnt(wts)), S(src[0], src[1] + 128 * h, src[1] + 128 * h + 128), wts)], start, stop, free, after)
+    def near(d, gb, h, n, bank, lo):
+        m = 512 // n
+        for k0 in range(4):
+            o = 2048 * h + 512 * k0
+            for j in range(n):
+                tt(S(d, o + m * j, o + m * j + m), step(gb, 2048 * h + 4 * m * j + k0, m, 4), S("Y%d" % h, m * j, m * j + m), A.max)
+            mm([(step(bank, lo + k0 + 4 * x, 8, 16), step(d, o + x, 128, 4), S("WG")) for x in range(4)], False, False, True)
 
     lanes(0)
+    awake(0)
     for t in range(RO):
         last = t == RO - 1
-        mcur = S("NB", 0, W) if t == 0 else S("M", 0, W)
-        cnum = "CF" if t == 0 else "PC"
         OJ, OB = fw(t, 0, 16), fw(t, 16, 16)
         for h in range(2):
-            spread("UX", 256 * h, ("ONE", 0), 0, S("TH"), start=h == 0, free=False)
-            spread("UE", 256 * h, ("MV", 0), h, S("RZ"), start=h == 0, free=False)
-        for h in range(2):
-            act(rep("XV", h, 1), IND(S("X", 0, V), u(16 + 8 * h, 8)))
-            repeat("XV", h, NX[h] if t else 2, OPT["xv"][h] if t else "a")
-            if t == 0:
-                mm([(S("PC", 256 * h, 256 * h + 256), S("I1"), rep("XV", h, 2))], True, True)
-            spread("UX", 256 * h, pair("XV"), h, S("BY"))
-
-            def step1(lo, hi):
-                sub = lo // 8 in SUB[t]
-                if t == 0:
-                    near("D0", "DC", lo, hi)
-                elif lo // 8 in PLAIN[t]:
-                    if lo % 8 == 0:
-                        mm([(S("PW", 256, 512), S("I1"), rep("XV", h, 2))], True, True)
-                    for k in range(lo, hi, 4):
-                        act(S("XC", 128 * k, 128 * k + 512), IND(S("X", 0, W), S("CU", 8 * k, 8 * k + 32)))
-                        near("D0", "XC", k, k + 4, S("PW", 256, 512))
-                elif sub:
-                    less(lo, hi, min(NX[h], hi - lo))
-                else:
-                    far("D0", "CU", "XV", lo, hi, min(NX[h], hi - lo))
-                if hi % 8:
-                    return
-                j = hi // 8 - 1
-                k0 = S("KK%d" % h if j % 2 else "K0", 0, 64)
-                fam = ("SP" if sub else "SM") if t else "SX"
-                tt(S("EQ", 64 * j, 64 * j + 64), S(cnum, 64 * j, 64 * j + 64), S("VT", 64 * j, 64 * j + 64), A.is_equal)
-                if t:
-                    lift("UE", 256 * h, "DC", j, wg(0, 2))
-                lift("UX", 256 * h, "DC", j, wg((3 if sub else 2) if t else 5, 2))
-                put = act if OPT["kt"] == "a" else cp
-                if j == 3:
-                    cs = S("K0", 256, 320)
-                    fold(cs, fam, "DC", 3072, 64, True, t > 0)
-                    if t == 0:
-                        mm([(cs, S("I1F"), S("CF", 192, 256))], False, True)
-                    put(S("KT", 128, 192), cs)
-                mm([(k0, S("BDC"), S("ONE", 0, 64)), (k0, S("I24"), S("EQ", 64 * j, 64 * j + 64))], True, False)
-                fold(k0, "SA", "D0", 1024 * j, 64, False, j == 3)
-                if j < 3:
-                    fold(k0, fam, "DC", 1024 * j, 64, False, t > 0)
-                    if t == 0:
-                        mm([(k0, S("I1F"), S("CF", 64 * j, 64 * j + 64))], False, True)
-                if j % 2 == 0:
-                    put(S("KT", 32 * j, 32 * j + 64), k0)
-                lift("UX", 256 * h, "D0", j, wg(7, 2))
-            names(t, h, VU, S("L", 0, V), "A1", "RU", "CU", "CF", "DC", 0, CH0[h] if t == 0 else CH[h], step1)
-            if t == 0:
-                for lo in (0, 128):
-                    spread("UE", 256 * h + lo, ("A1", 16 + 32 * h), h, S("I1F"))
-            kt = lambda lo, n: S("KT", 192 + 128 * h + lo, 192 + 128 * h + lo + n)
-            if h == 0:
-                tt(kt(0, 64), S("KK0", 0, 64), S("KT", 0, 64), A.min)
-            else:
-                tt(S("KT", 0, 64), S("KK1", 0, 64), S("KT", 128, 192), A.add)
-                tt(kt(0, 64), S("KT", 0, 64), S("KT", 64, 128), A.min)
-            tt(kt(64, 32), kt(0, 32), kt(32, 32), A.min)
-            tt(kt(96, 16), kt(64, 16), kt(80, 16), A.min)
-            tt(S("wi", 8 * h, 8 * h + 8), kt(96, 8), kt(104, 8), A.min)
-            ts(S("wi", 16 + 8 * h, 24 + 8 * h), S("wi", 8 * h, 8 * h + 8), 4095, A.bitwise_and)
-            cp(u(32 + 8 * h, 8), S("wi", 16 + 8 * h, 24 + 8 * h))
-            if not last:
-                act(S("w", 192 + 8 * h, 200 + 8 * h), S(cnum, 128 * h + 8 * t, 128 * h + 8 * t + 8))
-        cp(BF, S("wi", 16, 32))
+            kb = "K%d" % h
+            k = S(kb, 0, 128)
+            act(half("XV", h), IND(S("XR", 0, V), u(16 + 8 * h, 8)), scale=1.0 / 32)
+            four("XV", h)
+            entries(t, 0, h, VU, S("L", 0, V), "CU", "GC")
+            mm([(k, S("CB1"), one(128)), spread(k, "XV", h, S("BM8"))], True, False)
+            near("DA", "GC", h, NC[0][h], kb, 0)
+            mm([(k, S("CB0"), one(128))], False, True)
+            tt(half("KS", h), k, S("QS", 256 * h, 256 * h + 128), A.add)
+            scan(half("KM", h), S("RS"), half("KS", h), 0.0, A.add, A.min)
+            tt(half("LH", h), IND(half("KM", h), OMIN), S("MK"), A.mult)
+            mm([(S("PW", 8 * h, 8 * h + 8), half("LH", h), G8)], True, True)
+            ts(wi(8 * h, 8), S("PW", 8 * h, 8 * h + 8), MID, A.add)
+            ts(wi(16 + 8 * h, 8), wi(8 * h, 8), 4095, A.bitwise_and)
+            cp(u(32 + 8 * h, 8), wi(16 + 8 * h, 8))
         if last:
-            dma("s", lambda: T.NB[:, 0:V], lambda: T.X[:, 0:V], "dy", 3000, outs=[S("NB", 0, V)], ins=[S("X", 0, V)])
-            move("g", S("MH"), S("M", 0, V))
-            fold(S("PA", 0, 64), "SN", "MH", 0, 64, True, True)
-            cp(S("FW"), S("PA", 0, 64))
+            for r0 in range(0, 16, 4):
+                mm([(S("PA", 0, 64), sel("SQ", r), step("XF", r, 64, 16)) for r in range(r0, r0 + 4)], r0 == 0, r0 == 12)
+            ts(wi(96, 64), S("PA", 0, 64), MID, A.add)
+            ts(wi(160, 64), wi(96, 64), 4095, A.bitwise_and)
+            cp(S("FW"), wi(160, 64))
+        else:
+            for r0 in range(0, 16, 4):
+                mm([(S("PA", 0, 16), sel("SQ", r), step("GC", 16 * r + t, 16, 256)) for r in range(r0, r0 + 4)], r0 == 0, r0 == 12)
+            ts(wi(64), S("PA", 0, 16), MID, A.add)
+            ts(CI, wi(64), 4095, A.bitwise_and)
         if t == 0:
             for lo in range(0, 2 * GH, GH // 2):
                 mm([(S("PA", 0, GH // 2), S("IF"), S("LG", lo, lo + GH // 2))], True, True)
-                act(S("L", V + lo, V + lo + GH // 2), S("PA", 0, GH // 2), bias=float(V + lo // GH * GH))
+                act(S("L", V + lo, V + lo + GH // 2), S("PA", 0, GH // 2), bias=V + lo // GH * GH + LO)
         else:
             for d in range(2):
-                ts(IND(S("L", V, WD), u(104 + 4 * d, 2)), S("LL%d" % (t - 1), 32 * d, 32 * d + 32), 1.0, A.mult, float(V + d * GH), A.add)
+                scat(S("L", V, WD), u(104 + 4 * d, 2), S("LL%d" % (t - 1), 32 * d, 32 * d + 32))
+            if OPT["eq"] == "v":
+                entry("a", S("QV"), S("MV", 0, LN), S("XV"), S("PW", 256, 512))
         for h in range(2):
-            o = 128 * h
-            tt(S("ZS", o, o + 128), IND(S("X", 0, W), u(32 + 8 * h, 8)), rep("XV", h, 1), A.add)
-            ts(S("ZT", o, o + 128), S("ZS", o, o + 128), 0.5 - 2.0 ** -11, A.mult, 1536.0, A.add)
-            ts(rep("ZZ", h, 1), S("ZT", o, o + 128), -1536.0, A.add)
-            repeat("ZZ", h, 4, OPT["zz"][h]) if t else repeat("ZZ", h, 4 if OFF1 or OFF2 else 2)
-        zz = pair("ZZ")
+            y = S("Y%d" % h, 0, 128)
+            ts(u(80 + 8 * h, 8), wi(16 + 8 * h, 8), float(V), A.min)
+            act(half("XB", h), IND(S("XR", 0, V + 8), u(80 + 8 * h, 8)), scale=1.0 / 32)
+            if OPT["z"][h] == "a":
+                mm([(y, S("IH"), half("XV", h)), (y, S("IH"), half("XB", h)), (y, one(128), S("HF", 128, 256)),
+                    (y, S("CB0"), S("HF", 256, 384)), (y, S("CB0"), S("HF", 384, 512))], True, True)
+                act(half("ZZ", h), y)
+                act(half("ZF", h), y, scale=32.0)
+            else:
+                mm([(y, S("I1"), half("XV", h)), (y, S("I1"), half("XB", h))], True, True)
+                ts(half("ZT", h), y, 0.5 - 2.0 ** -11, A.mult, 1536.0, A.add)
+                ts(half("ZZ", h), half("ZT", h), -1536.0, A.add)
+                act(half("ZF", h), half("ZZ", h), scale=32.0)
+            four("ZZ", h)
         for h in range(2):
-            act(S("MB", 128 * h, 128 * h + 128), IND(mcur, u(32 + 8 * h, 8)))
-            scat(S("B"), u(48 + 8 * h, 8), S("MB", 128 * h, 128 * h + 128))
-        ts(u(80), S("wi", 16, 32), float(V), A.min)
+            act(half("MB", h), IND(S("NB", 0, W), u(32 + 8 * h, 8)))
+            scat(S("B"), u(48 + 8 * h, 8), half("MB", h))
         act(S("BB"), IND(S("B", 0, V + 8), u(80)))
-        act(S("MC"), S("MB", 0, LN))
+        act(S("MC"), S("MB", 0, LN), bias=MCB)
         fold(S("PW", 0, 16), "SN", "BB", 0, 16, True, True)
+        tt(G1, BI, VM, A.is_gt)
         if t > 0:
             cp(BBU, S("PW", 0, 16))
-            act(S("BK"), IND(mcur, BBU))
-            fold(S("PW", 0, 16), "SN", "BK", 0, 16, True, True)
-        tt(G1, BF, VM, A.is_gt)
-        tt(J1, S("PW", 0, 16), VF, A.is_equal)
+            if OPT["eq"] == "v":
+                tt(S("EQ"), IND(S("XF", 0, W), BBU), S("QV"), A.is_equal)
+            else:
+                o = S("PW", 256, 512)
+                act(S("QV"), IND(S("XF", 0, W), BBU))
+                mm([(o, S("I1"), S("XV")), (o, S("WPS"), S("MV", 0, LN)), (o, S("IM1F"), S("QV"))], True, True)
+                act(S("EQ"), o, bias=PSI, func=F.Abs)
+            fold(S("PW", 0, 16), "SA", "EQ", 0, 16, True, True)
+            ts(J1, S("PW", 0, 16), 16 * 8192.0 if OPT["eq"] == "v" else 0.0, A.is_equal)
+        else:
+            tt(J1, S("PW", 0, 16), VF, A.is_equal)
         tt(JN, J1, G1, A.mult)
         ts(NJ, JN, -8192.0, A.mult, 8192.0, A.add)
         if not last:
             ts(VL, VF, float(GH), A.is_lt)
             tt(TL, JN, VL, A.mult)
         nb = 1 if last else 2
-        mm([(S("PA", r, r + 16 * (16 * nb - 1) + 1, 16), S("ROWS", 128 * r, 128 * r + 128), S("wb", 0, 16 * nb)) for r in range(16)], True, True)
+        mm([(step("PA", r, 16 * nb, 16), S("ROWS", 128 * r, 128 * r + 128), S("wb", 0, 16 * nb)) for r in range(16)], True, True)
         if not last:
-            scan(S("CN"), S("ONE", 0, LN), S("PA", LN, 2 * LN), 0.0, A.mult, A.add)
+            scan(S("CN"), one(LN), S("PA", LN, 2 * LN), 0.0, A.mult, A.add)
         act(S("NN"), S("PA", 0, LN))
         tt(w(16), NJ, VF, A.add)
-        tt(w(17), NJ, BF, A.add)
+        tt(w(17), NJ, BI, A.add)
         tt(w(18, 2), w(16, 2), DUMP, A.min)
         cp(fw(t, 0, 32), w(18, 2))
-        done = []
-        mm([(S("KK0", 0, 384), S("BDC"), S("ONE", 0, 384))], True, False)
         for h in range(2):
-            if t == 0:
-                mm([(S("PC", 256 * h, 256 * h + 256), S("I1"), rep("ZZ", h, 2))], True, True)
-            for j in (2 * h, 2 * h + 1):
-                off = j in (SUB[t] if t else OFF1)
-                if t == 0:
-                    over("D1", "DC", j) if off else near("D1", "DC", 8 * j, 8 * j + 8)
-                elif off:
-                    again(j)
-                elif j in PLAIN[t]:
-                    mm([(S("PW", 256, 512), S("I1"), rep("ZZ", h, 2))], True, True)
-                    near("D1", "XC", 8 * j, 8 * j + 8, S("PW", 256, 512))
-                else:
-                    lo = 8 * j
-                    for n in ND1[j]:
-                        far("D1", "CU", "ZZ", lo, lo + n, n)
-                        lo += n
-                k = lift("KK0", 128 * h, "D1", j, wg(9))
-                done.append(lift("KK0", 128 * h, "DC", j, wg((11 if off else 10) if t else (13 if off else 12)), after=[k]))
-            if t == 0:
-                spread("KK0", 128 * h, ("A1", 16 + 32 * h), h, S("I1F"), after=done[-2:])
+            th, eb = S("PA", 256 * h, 256 * h + 256), S("PA", 256 * h + 128, 256 * h + 256)
+            mm([(th, one(128), S("TH")), spread(eb, "XV", h, S("BD4", 0, 128)), spread(eb, "XB", h, S("BM4")), spread(eb, "MC", h, S("RN")),
+                spread(th, "NN", h, S("BJ"))], h == 0, h == 1)
         for h in range(2):
-            spread("UE", 256 * h + 128, ("MC", 0), h, S("RZ", 0, 128))
-        for h in range(2):
-            spread("UE", 256 * h + 128, ("NN", 0), h, S("BJ", 0, 128), stop=h == 1)
-            spread("UX", 256 * h, ("NN", 0), h, S("BJ", 128, 384))
-        ts(S("EU"), S("UE"), 0.0, A.is_equal)
-        mm([(S("UX", o + lo, o + lo + 128), S(m), S("EU", o, o + 128)) for o in (0, 256) for lo, m in ((0, "I13"), (128, "IM13"))], False, True)
-        act(S("PN"), S("UX"), scale=2 * BIG, func=F.Relu)
-        ko = (("KK0", 256), ("K0", 0))
+            tt(eu(h, 4), half("KS", h), S("PA", 256 * h, 256 * h + 128), A.is_ge)
+            tt(eu(h, 1), S("QS", 256 * h, 256 * h + 128), S("PA", 256 * h + 128, 256 * h + 256), A.is_equal)
 
-        def pens(bank, lo, e, i, h):
-            return [(S(bank, lo, lo + 128), S(m), S(x, 256 * h + o, 256 * h + o + 128)) for m, x, o in (("IBIG", e, 0), ("IBIG", e, 128), ("I1", "PN", 128 * i))]
-
-        def masks(h):
-            o = 256 * h
-            spread("KK1", o, ("MV", 0), h, S("RZ", 0, 128), start=True)
-            spread("KK1", o + 128, ("MC", 0), h, S("RZ", 0, 128), free=False)
-            if t:
-                for j in (2 * h, 2 * h + 1):
-                    lift("KK1", o, "DO", j, wg(0, 2))
-            else:
-                for lo in (0, 128):
-                    spread("KK1", o + lo, ("A2", 16 + 32 * h), h, S("I1F"))
-            spread("KK1", o + 128, ("NN", 0), h, S("BJ", 0, 128), stop=True)
-            ts(S("EO", o, o + 256), S("KK1", o, o + 256), 0.0, A.is_equal)
-
-        def chosen(h):
-            o = 128 * h
-            keys, turned = S("RF", o, o + 128), S(("UE", "UX")[h], 0, 128)
-            tt(keys, S(ko[h][0], ko[h][1], ko[h][1] + 128), S("KC", o, o + 128), A.min)
-            node("p", PEC * 512, lambda: g.tensor.transpose(ap(turned), ap(keys), ap(S("I1F"))), [turned], [keys, S("I1F")])
-            cp(S("RI", o, o + 128), turned)
-            ts(S("NL", o, o + 128), S("RI", o, o + 128), 4095, A.bitwise_and)
-            cp(IND(S("L"), u(48 + 8 * h, 8)), S("NL", o, o + 128))
+        def close(k, h, i):
+            mm([(k, S("CB0"), one(128)), spread(k, "XV", h, S("BM4")), spread(k, "ZZ", h, S("BM4")),
+                (k, S("I1F"), S("QS", 256 * h + 128 * i, 256 * h + 128 * i + 128))], False, True)
 
         for h in range(2):
-            names(t, h, BU, S("L", 0, W), "A2", "RU2", "OU", None, "DO", 256, (CO if t else CO0)[h], lambda lo, hi: None)
-            masks(h)
-        if t == 0:
-            move("g", S("M", V, W), S("LM"), slice(2, None, 4))
+            entries(t, 1, h, BU, S("L", 0, W), "OU", "GO")
+        if last:
+            ts(S("L", 0, V), S("L", 0, V), 1.5 * 2 ** 23 - LO, A.add, 1.5 * 2 ** 23, A.subtract)
+        for h in range(2):
+            kb = "K%d" % h
+            k = S(kb, 0, 128)
+            mm([(k, S("CB1"), one(128))], True, False)
+            near("DB", "GC", h, NC[1][h], kb, 0)
+            mm([(k, S("IBIG"), eu(h, j)) for j in (1, 4)], False, False, True)
+            close(k, h, 0)
+            tt(half("KC", h), k, half("CL", h), A.min)
         if not last:
-            pieces(S("MZ", 0, LN), S("MV", 0, LN), zz, S("PW", 256, 512))
+            entry("a", S("MZ", 0, LN), S("MV", 0, LN), S("ZZ"), S("PW", 256, 512))
             me, le, ml, ll = "ME%d" % t, "LE%d" % t, "ML%d" % t, "LL%d" % t
             for j in range(2):
                 act(S("HB", 256 * j, 256 * j + 256), S("CN"), bias=c(18 + j), scale=-1.0, func=F.Sign, accum=S("q", 192 + j, 193 + j))
@@ -690,90 +575,81 @@ def build(g, core, T, topo):
             s2 = u(96, 2)
             for j, src in enumerate(("MV", "MB")):
                 act(S("MS", 32 * j, 32 * j + 32), IND(S(src), s2))
-            act(S(me, 64, 96), IND(S("ZZ", 384, 656), s2))
             act(S(me, 0, 64), IND(S("MZ"), SU), bias=R4A)
-            act(S(me, 100, 164), IND(S("MZ"), SU), bias=R4B)
+            act(S(me, 68, 132), IND(S("MZ"), SU), bias=R4B)
             fold(S("PW", 0, 4), "SN", "MS", 0, 4, True, True)
             ts(S("q", 0, 4), S("PW", 0, 4), GH - 0.5, A.subtract, 8192.0, A.mult)
-            tt(S(me, 96, 100), S("q", 0, 4), S("PW", 0, 4), A.max)
-            exchange([S(me, 0, 100), S(me, 64, 164)], [S(le, 0, 100), S(le, 100, 200)], "te%d" % t, "re%d" % t, 2500)
+            tt(S(me, 64, 68), S("q", 0, 4), S("PW", 0, 4), A.max)
+            exchange([S(me, 0, 68), S(me, 64, 132)], [S(le, 0, 68), S(le, 68, 136)], "te%d" % t, "re%d" % t, 2500)
             mm([(S("PW", 0, 32), S("RN"), S("MS", 0, 32))], True, True)
-            act(S("q", 32, 64), S("PW", 0, 32))
+            act(S("q", 32, 64), S("PW", 0, 32), bias=LO)
             y = [w(32, 2), w(34, 2), w(36), w(37), w(38), w(39)]
-            ts(y[0], w(11, 2), V - 0.5, A.subtract, 32768.0, A.mult)
-            tt(y[1], y[0], w(11, 2), A.max)
+            ts(y[0], wi(16, 32), V - 0.5, A.subtract, 32768.0, A.mult)
+            tt(y[1], y[0], wi(16, 32), A.max)
             ts(y[2], w(35), 4096.0, A.add)
             tt(y[3], y[2], w(34), A.min)
             tt(y[4], w(16), NJ, A.add)
             tt(y[5], y[4], AW, A.add)
-            tt(S("wi", 0, 16), y[5], y[3], A.min)
-            ts(S("wi", 32, 48), S("wi", 0, 16), 4095, A.bitwise_and)
-            cp(PU, S("wi", 32, 48))
-            scat(S("M"), OJ, S("MZ", 0, LN))
-            scat(S("M"), OB, S("MZ", 0, LN))
-            tt(S("q", 8, 12), S(le, 96, 100), c(112, 4), A.min)
-            tt(S("q", 12, 16), S(le, 132, 136), c(120, 4), A.min)
+            tt(wi(64), y[5], y[3], A.min)
+            ts(wi(80), wi(64), 4095, A.bitwise_and)
+            cp(PU, wi(80))
+            scat(S("M"), OB, S("MF"))
+            scat(S("XR"), OJ, S("ZF"))
+            cp(IND(S("XF"), OJ), S("MZ", 0, LN))
+            cp(IND(S("XF"), OB), S("MZ", 0, LN))
+            for e in range(t - 1, -1, -1):
+                act(S("FG", 0, LN), IND(S("XF"), fw(e, 0, 16)))
+                cp(IND(S("XF"), fw(e, 16, 16)), S("FG", 0, LN))
+            tt(S("q", 8, 12), S(le, 64, 68), c(112, 4), A.min)
+            tt(S("q", 12, 16), S(le, 68, 72), c(120, 4), A.min)
             cp(u(104, 4), S("q", 8, 12))
             ts(u(108, 4), S("q", 12, 16), float(GH), A.add)
-            for d, lo in ((0, 0), (1, 136)):
-                scat(S("M", V, WD), u(104 + 4 * d, 4), S(le, lo, lo + 64))
+            for d, lo in ((0, 0), (1, 72)):
+                cp(IND(S("XF", V, WD), u(104 + 4 * d, 4)), S(le, lo, lo + 64))
             if t < RO - 2:
                 for d in range(2):
                     cp(fw(t, 32 + 2 * d, 2), u(104 + 4 * d, 2))
                     cp(fw(t, 36 + 2 * d, 2), u(106 + 4 * d, 2))
+            for e in range(t - 1, -1, -1):
+                (cp if OPT["fg"] == "v" else act)(S("FG", 256, 320), IND(S("XF", V, WD), fw(e, 32, 4)))
+                cp(IND(S("XF", V, WD), fw(e, 36, 4)), S("FG", 256, 320))
+            lanes(t + 1)
         else:
-            cp(IND(S("NB"), OJ), zz)
-            dma("a", lambda: T.yx[:], lambda: T.NB[:, 0:V], "ox", 3000, ins=[S("NB", 0, V)])
-            act(S("MZ", 0, LN), S("MV", 0, LN))
-            scat(S("M"), OB, S("MZ", 0, LN))
+            scat(S("XR"), OJ, S("ZF"))
+            act(S("X", 0, V), S("XR", 0, V), scale=1.0 / 32)
+            dma("a", lambda: T.yx[:], lambda: T.X[:, 0:V], "ox", 3000, ins=[S("X", 0, V)])
+            act(S("MF"), S("MV", 0, LN))
+            scat(S("M"), OB, S("MF"))
             act(S("MH"), IND(S("M", 0, V), S("FW")))
-            mm([(S("PA", 0, 64), sel("SN", r), S("MH", 64 * r, 64 * r + 64)) for r in range(16)], True, True)
-            act(S("YF"), S("PA", 0, 64))
+            mm([(S("PW", 0, 64), sel("SN", r), S("MH", 64 * r, 64 * r + 64)) for r in range(16)], True, True)
+            act(S("YF"), S("PW", 0, 64))
             dma("s", lambda: T.yf[:], lambda: T.YF[:], "of", 2500, ins=[S("YF")])
-        for j in range(4):
-            kk, lo = ko[j // 2]
-            if j == 2:
-                mm([(S(kk, 0, 128), S("BDC"), S("ONE", 0, 128))], True, False)
-            if j == 3:
-                mm(pens(kk, lo, "EO", 1, 1), False, False, True)
-            if j in PLAIN2[t]:
-                for k in range(8 * j, 8 * j + 8, 4):
-                    act(S("XC", 128 * k, 128 * k + 512), IND(S("X", 0, W), S("OU", 8 * k, 8 * k + 32)))
-                mm([(S("PW", 256, 512), S("I1"), rep("ZZ", j // 2, 2))], True, True)
-                near("D2", "XC", 8 * j, 8 * j + 8, S("PW", 256, 512))
-            elif t:
-                far("D2", "OU", "ZZ", 8 * j, 8 * j + 8, 4)
-            elif j in OFF2:
-                over("D2", "DO", j)
+        for h in range(2):
+            kb = "K%d" % h
+            k = S(kb, 128, 256)
+            mm([(k, S("CB1"), one(128)), spread(k, "NN", h, S("BJ", 128, 256))], True, False)
+            tt(eu(h, 3), S("QS", 256 * h + 128, 256 * h + 256), S("PA", 256 * h + 128, 256 * h + 256), A.is_equal)
+            near("DC", "GO", h, NC[2][h], kb, 128)
+            mm([(k, S("IMB"), eu(h, 4)), (k, S("IBIG"), eu(h, 3))], False, False, True)
+            close(k, h, 1)
+            tt(half("RF", h), k, half("KC", h), A.min)
+            y = S("Y%d" % h, 0, 128)
+            mm([(y, half("RF", h), S("IM1F")), (y, S("CB2"), one(128)), (y, S("CB0"), S("HF", 0, 128)), (y, half("RF", h), S("I1F"))], True, True)
+            act(half("NL", h), y, bias=MID + (0.0 if last else LO))
+            if last:
+                cp(IND(S("L"), u(48 + 8 * h, 8)), half("NL", h))
             else:
-                near("D2", "DO", 8 * j, 8 * j + 8)
-            k = lift(kk, lo, "D2", j, wg(9))
-            done.append(lift(kk, lo, "DO", j, wg(10 if t else 13 if j in OFF2 else 12), stop=t > 0 and j == 3, after=[k]))
-            if t == 0 and j % 2:
-                spread(kk, lo, ("A2", 16 + 32 * (j // 2)), j // 2, S("I1F"), stop=j == 3, after=done[-2:])
-            if j == 1:
-                for h in range(2):
-                    mm(pens(kk, 128 * h, "EU", 0, h), False, False, True)
-                mm(pens(kk, lo, "EO", 1, 0), False, True)
-                tt(S("KC"), S(kk, 0, 256), S("CL"), A.min)
-                chosen(0)
-        chosen(1)
+                scat(S("L"), u(48 + 8 * h, 8), half("NL", h))
         if last:
             break
-        cp(IND(S("X"), OJ), zz)
-        for d, lo in ((0, 64), (1, 100)):
-            cp(IND(S("X", V, WD), u(104 + 4 * d, 2)), S(le, lo, lo + 32))
-        ts(S("q", 0, 32), IND(S("NL"), s2), float(GH), A.is_lt)
+        ts(S("q", 0, 32), IND(S("NL"), s2), GH + LO, A.is_lt)
         tt(S("q", 64, 96), IND(S("NL"), s2), S("q", 32, 64), A.subtract)
         tt(S("q", 128, 160), S("q", 0, 32), S("q", 64, 96), A.mult)
-        tt(S(ml), S("q", 128, 160), S("q", 32, 64), A.add)
-        exchange([S(ml)] * 2, [S(ll, 0, 32), S(ll, 32, 64)], "tm%d" % t, "rm%d" % t, 2500)
-        lanes(t + 1)
-        for e in range(t - 1, -1, -1):
-            act(S("FG", 0, LN), IND(S("M"), fw(e, 0, 16)))
-            scat(S("M"), fw(e, 16, 16), S("FG", 0, LN))
-            act(S("FG", 256, 320), IND(S("M", V, WD), fw(e, 32, 4)))
-            scat(S("M", V, WD), fw(e, 36, 4), S("FG", 256, 320))
+        tt(S("q", 160, 192), S("q", 128, 160), S("q", 32, 64), A.add)
+        for d in range(2):
+            act(S(ml, 32 * d, 32 * d + 32), S("q", 160, 192), bias=float(V + d * GH))
+        exchange([S(ml, 0, 32), S(ml, 32, 64)], [S(ll, 0, 32), S(ll, 32, 64)], "tm%d" % t, "rm%d" % t, 2500)
+        awake(t + 1)
     dma("s", lambda: T.yl[:], lambda: T.L[:, 0:V], "ol", 4000, ins=[S("L", 0, V)])
     return nodes, eng
 
@@ -925,7 +801,7 @@ def order(nodes):
             continue
         a, b = chains[c][rnd // 4096 % len(chains[c])]
         lo, hi = seq.index(a), seq.index(b)
-        for step in range(rnd // 16 % 4 if rnd // 8 % 2 else 0):
+        for hop in range(rnd // 16 % 4 if rnd // 8 % 2 else 0):
             z = lo - 1
             while z >= 0 and queue[seq[z]] != queue[b]:
                 z -= 1

@@ -9,8 +9,9 @@ MID = 1408.0
 LO = 64.0
 GE = [[["va", "aa"], ["aa", "aa"]]] * RO
 NC = [[1, 1], [1, 1], [1, 2]]
-OPT = dict(vf="a", bd="a", xf="aavava", lg="vvvv", eq="v", z="vv", fg="a")
-PEC, DLAT, PASSES, SWAPS, AMP, SPAN = 0.5, 3600, 10500, 12000, 2000.0, 3500.0
+OPT = dict(vf="a", bd="a", xf="aaaaaa", lg="vava", eq="vvvv", z="vv", fg="a", bf="a", ct="PA", gl="vvvv")
+PEC, DLAT, PASSES, SWAPS, AMP, SPAN = 0.5, 3600, 5000, 8000, 2000.0, 3500.0
+LOCAL, WIDE, WARM = 16000, 400, 0.002
 CASES = [(1.56, 3.8, 0.5, 150.0, 1.0), (1.2, 2.5, 0.55, 140.0, 1.0), (1.9, 5.2, 0.5, 105.0, 0.7), (1.4, 4.6, 0.45, 190.0, 1.35)]
 PLAN = []
 
@@ -23,7 +24,7 @@ def _buf(names, n, dtp, where="sbuf"):
 
 
 _buf("X NB", W, "bfloat16")
-_buf("MH D2", V, "bfloat16")
+_buf("MH", V, "bfloat16")
 _buf("L M B XF XR", WD, "float32")
 _buf("HI", V, "int32")
 _buf("GA", GH, "bfloat16")
@@ -37,16 +38,16 @@ _buf("ROWS", 2048, "bfloat16")
 _buf("HB ONE HF", 512, "bfloat16")
 _buf("EU", 1280, "bfloat16")
 _buf("SA SN S32", 144, "bfloat16")
-_buf("Z0 IU SQ", 144, "float32")
-_buf("RN RM BD1 IBIG IMB I1 WBH BDW BDB BJM WPS CB1 CB0 CB2 IH BM8 BM4 MK RS", 128, "bfloat16")
-_buf("WBL IG IR MT I1F IM1F", 128, "float32")
-_buf("BJ BD4", 256, "bfloat16")
+_buf("UP IU SQ", 144, "float32")
+_buf("RN RM BD1 IBIG IMB I1 BDW BDB BJM WPS CB1 CB0 CB2 IH BM8 BM4 MK RS", 128, "bfloat16")
+_buf("IG IR I1F IM1F", 128, "float32")
+_buf("BD4", 256, "bfloat16")
 _buf("MB MZ NL", 272, "float32")
 _buf("FG", 320, "float32")
 _buf("MV", 272, "bfloat16")
 _buf("KC CL RF KS KM LH QV MF LF ZF", 256, "float32")
 _buf("QS", 512, "float32")
-_buf("PW2 I256 CR EQ BB TH MC NN CN XV XB ZZ", 256, "bfloat16")
+_buf("PW2 I256 CR EQ BB TH MC JJ TL CN XV XB ZZ", 256, "bfloat16")
 _buf("CU OU PR", 256, "uint16")
 _buf("FW", 64, "uint16")
 _buf("fw", 160, "uint16")
@@ -57,6 +58,7 @@ _buf("wi", 224, "int32")
 _buf("wb", 32, "bfloat16")
 _buf("WG", 8, "bfloat16")
 _buf("WQ", 16, "float32")
+_buf("WP", 16, "bfloat16")
 _buf("u", 128, "uint16")
 _buf("cu", 8, "uint16")
 _buf("MS", 64, "bfloat16")
@@ -67,7 +69,7 @@ _buf("LE0 LE1 LE2", 136, "float32")
 _buf("ML0 ML1 ML2 LL0 LL1 LL2", 64, "float32")
 _buf("Q0 Q1 K0 K1 Y0 Y1 PA PW", 512, "float32", "psum")
 
-SEMAPHORES = (["sv", "sa", "sp", "sg", "dx", "dn", "dm", "dh", "dl", "dt", "ox", "ol", "of", "tx", "rx", "tl", "rl"]
+SEMAPHORES = (["sv", "sa", "sp", "sg", "dx", "dn", "dm", "dh", "dl", "dt", "db", "b0", "b1", "b4", "f0", "f1", "f2", "f3", "ox", "ol", "of", "tx", "rx", "tl", "rl"]
               + ["%s%d" % (a, t) for a in ("te", "re", "tm", "rm") for t in range(RO - 1)] + ["m%d" % j for j in range(1, 40)])
 SHORT = ("bfloat16", "uint16", "float16")
 
@@ -151,7 +153,7 @@ def build(g, core, T, topo):
         return node("v", vcost(out, i0, narrow(out, i0)), fn, [out], [i0, s1, s2])
 
     def scan(out, d0, d1, first, op0, op1):
-        return node("v", vcost(out, d1, 1.0), lambda: g.vector.tensor_tensor_scan(ap(out), ap(d0), ap(d1), first, op0, op1), [out], [d0, d1])
+        return node("v", vcost(out, d1, narrow(out, d0, d1)), lambda: g.vector.tensor_tensor_scan(ap(out), ap(d0), ap(d1), first, op0, op1), [out], [d0, d1])
 
     def total(out, i0):
         return node("v", 74, lambda: g.vector.tensor_reduce(ap(out), ap(i0), AxisListType.X, A.add), [out], [i0])
@@ -239,9 +241,9 @@ def build(g, core, T, topo):
 
     def fill(out, val):
         return iota(out, [[0, cnt(out)]], val, after=[sent])
-    ROW, GRP, HW, PID, G15, WN, PSI, R4A, R4B, MCB, BB1, TMP, TMP2, TC = [c(j) for j in range(14)]
+    ROW, GRP, HW, PID, G15, WN, PSI, R4A, R4B, MCB, LOW, TMP, TMP2, TC = [c(j) for j in range(14)]
     DUMP, D8, G8, TH8, T16a, I16 = c(64, 32), c(112, 8), c(128, 8), c(136, 8), c(144, 16), c(192, 16)
-    OMIN = S("cu")
+    OMIN, G8N = S("cu"), c(160, 8)
     first = [iota(ci(0), [[0, 1]], 0, 1), iota(S("IU"), [[1, 144]], 0), iota(S("IG"), [[1, 8], [0, 16]], 0)]
     iota(S("NB", 0, V), [[32, V // 256], [0, 256]], 0, after=[iota(S("I256"), [[32, 256]], 0, after=first)])
     iota(S("NB", V, W), [[32, (W - V) // 256], [0, 256]], 32 * V // 256, after=[sent])
@@ -266,20 +268,22 @@ def build(g, core, T, topo):
     ts(R4A, HW, -float(V // 256), A.mult)
     ts(R4B, HW, -float((V + GH) // 256), A.mult, c(15), A.subtract)
     ts(MCB, mk(0), -MID / 4, A.mult)
-    ts(BB1, mk(1), -32 * LO, A.mult)
+    ts(LOW, ROW, 8.0, A.is_lt)
+    ts(c(26), LOW, -17.0, A.mult, 1.0, A.add)
+    ts(c(27), LOW, -1.0, A.mult, 1.0, A.add)
+    ts(c(28), LOW, -BIG / 4, A.mult, BIG / 8, A.add)
     ts(S("S32"), S("IU"), G15, A.is_equal, 32.0, A.mult)
-    for fam, wt in (("SN", WN), ("Z0", mk(0))):
-        ts(S(fam), S("S32"), wt, A.mult, 1.0 / 32, A.mult)
+    ts(S("SN"), S("S32"), WN, A.mult, 1.0 / 32, A.mult)
     for fam, wt in (("SA", 256.0), ("SQ", -128.0)):
         times("a", S(fam), S("S32"), wt)
     ts(S("BD1"), S("IG"), GRP, A.is_equal)
     ts(S("I1"), S("IU", 0, 128), PID, A.is_equal)
     for e, m, base, wt in (("v", "RN", "BD1", WN), ("v", "IBIG", "I1", BIG), ("a", "I1F", "I1", 1.0), ("a", "IM1F", "I1", -1.0),
-                           ("v", "RM", "RN", -1.0), ("a", "IMB", "I1", -BIG), ("v", "IF", "I1", 1.0), ("v", "IH", "I1", 0.5)):
+                           ("v", "RM", "RN", -1.0), ("a", "IMB", "I1", -BIG), ("v", "IH", "I1", 0.5), ("v", "IF", "I1", 1.0)):
         times(e, S(m), S(base), wt)
-    ts(S("WBL"), sel("Z0", 1), 32.0, A.mult)
-    ts(S("MT"), sel("Z0", 0), 1.0 / 4, A.mult)
-    tt(S("WBH"), S("MT"), S("WBL"), A.subtract)
+    ts(c(16), ROW, 4.0, A.is_lt)
+    ts(c(17), PID, 16.0, A.add)
+    ts(S("UP"), S("IU"), c(17), A.is_equal, c(16), A.mult)
     mset(S("ONE"), 1.0)
     ts(G8, S("IU", 0, 8), GRP, A.is_equal)
     mset(S("WPS"), 0.0)
@@ -295,12 +299,14 @@ def build(g, core, T, topo):
     tt(c(48, 16), S("PW2", 0, 16), c(224, 16), A.mult)
     total(c(21), c(48, 16))
     ts(S("BDW"), S("BD1"), c(21), A.mult, 0.5, A.mult)
-    for m, wt in ((S("BDB"), 65536.0), (S("BJM"), -1.0 / 16), (S("BJ", 0, 128), -512.0), (S("BJ", 128, 256), 512.0),
+    for m, wt in ((S("BDB"), 65536.0), (S("BJM"), -1.0 / 16), (S("TH", 128, 256), c(28)),
                   (S("BD4", 0, 128), 4096.0), (S("BD4", 128, 256), 4096.0), (S("BM8"), -8192.0), (S("BM4"), -4096.0)):
         times(OPT["bd"], m, S("BD1"), wt)
     times("a", S("WG"), G8, 8192.0)
+    times("a", G8N, G8, -1.0)
     for lo in (0, 8):
         times("a", S("WQ", lo, lo + 8), G8, -4096.0)
+    act(S("WP"), S("WQ"))
     fill(S("CB1"), 0)
     for lo, hi, val in ((0, 64, R13 / 64), (64, 96, -float(2 ** 19)), (96, 97, 32768.0)):
         mset(S("CB1", p=(lo, hi)), val)
@@ -316,7 +322,6 @@ def build(g, core, T, topo):
     fill(S("MZ", 256, 272), 0)
     fill(S("NL", 256, 272), int(LO))
     fill(S("XF", W, WD), 0)
-    fill(S("TH", 128, 256), 0)
     fill(S("B", V, V + 8), 128)
     ts(T16a, I16, 16.0, A.mult, ROW, A.add)
     ts(c(64, 16), T16a, float(W), A.add)
@@ -331,10 +336,10 @@ def build(g, core, T, topo):
     cp(ci(8), c(20))
     ts(ci(9), ci(8), 15, A.bitwise_and)
     ts(ci(10), ci(8), 4080, A.bitwise_and)
-    ts(c(22), ci(9), 8.5, A.add, mk(1), A.mult)
-    ts(c(23), ci(10), mk(0), A.mult, c(22), A.add)
-    ts(c(24), mk(2), -4096.0, A.mult, c(23), A.add)
-    ts(TC, mk(3), BIG / 4096, A.mult, c(24), A.add)
+    ts(c(22), ci(9), 8.5, A.add, mk(9), A.mult)
+    ts(c(23), ci(10), mk(8), A.mult, c(22), A.add)
+    ts(c(24), mk(10), -4096.0, A.mult, c(23), A.add)
+    ts(TC, LOW, BIG / 8 / 4096, A.mult, c(24), A.add)
     ts(S("TH", 0, 128), S("BD1"), TC, A.mult, 4096.0, A.mult)
 
     ts(S("L", 0, V), S("HI"), LO, A.add)
@@ -352,16 +357,16 @@ def build(g, core, T, topo):
         entry(OPT["xf"][j], S("XF", lo, lo + 512), S("NB", lo, lo + 512), S("X", lo, lo + 512), S("Q%d" % j))
     act(S("XR", 0, V), S("X", 0, V), scale=32.0)
     fill(S("XR", V, V + 8), 0)
-    for j, bank in enumerate(("Q0", "Q1", "Y1", "K0")):
-        lo, hi, o = V + GH // 2 * j, V + GH // 2 * (j + 1), S(bank, 0, GH // 2)
-        mm([(o, S("WPS"), S("NB", lo, hi))], True, False)
-        mm([(o, S("I1"), S("X", lo, hi))], False, True)
-        plus(OPT["xf"][2 + j], S("XF", lo, hi), o, PSI)
-    for lo in (0, 512):
-        act(S("D2", lo, lo + 512), S("L", lo, lo + 512), bias=-LO)
-        mm([(S("K1"), S("WBH"), S("D2", lo, lo + 512)), (S("K1"), S("WBL"), S("L", lo, lo + 512))], True, True)
-        act(S("B", lo, lo + 512), S("K1"), bias=BB1)
-    move("g", S("M", 0, V), S("NB", 0, V), behind=[S("LG")])
+    move("g", S("M", 0, V), S("NB", 0, V), behind=[S("X", V, W)])
+    mset(S("B", 0, V), 0.0)
+    dma("s", lambda: T.wi[:, 96:160], lambda: T.hits[0::16, :], "db", 2500, outs=[S("wi", 96, 160)])
+    ts(S("wi", 160, 224), S("wi", 96, 160), 8, A.arith_shift_right)
+    ts(S("wi", 96, 160), S("wi", 96, 160), 255, A.bitwise_and)
+    for r, lo in ((0, 160), (1, 96)):
+        ts(S("RF", 64 * r, 64 * r + 64), S("wi", lo, lo + 64), 32.0, A.mult)
+    for r, lo in ((0, 0), (4, 0), (1, 64)):
+        dma("s", lambda r=r: T.B[r::16, 0:V], lambda lo=lo: T.RF[:, lo:lo + 64], "b%d" % r, 2500,
+            outs=[S("B", 64 * r, 64 * r + 64)], ins=[S("RF", lo, lo + 64)])
 
     def w(j, n=1):
         return S("w", 16 * j, 16 * (j + n))
@@ -374,10 +379,10 @@ def build(g, core, T, topo):
 
     def fw(t, lo, n):
         return S("fw", 40 * t + lo, 40 * t + lo + n)
-    VF, VA, AW, VM, JN, G1, J1, VL = [w(j) for j in range(8)]
-    BI, CI = wi(16), wi(32)
+    VF, VA, AW, VM, NJ, VL = [w(j) for j in range(6)]
+    BF = w(11)
     PU, VU, BU, OL, BBU, SU = u(0), u(16), u(32), u(48), u(64), u(96, 4)
-    NJ, TL = S("wb", 0, 16), S("wb", 16, 32)
+    G1, G2 = S("wb", 0, 16), S("wb", 16, 32)
 
     def half(b, h, lo=0):
         return S(b, lo + 128 * h, lo + 128 * h + 128)
@@ -414,7 +419,7 @@ def build(g, core, T, topo):
         cp(OL, VM)
         if t < RO - 1:
             ts(AW, VM, float(V), A.is_ge, -16384.0, A.mult)
-            ts(AW, AW, -8192.0, A.add)
+            tt(AW, AW, VF, A.add)
             move("g", S("MF"), S("MV", 0, LN))
 
     def spread(out, src, h, wts):
@@ -426,17 +431,20 @@ def build(g, core, T, topo):
     def entries(t, i, h, off, lwin, ub, gb):
         q = S("Q%d" % h, 0, 128)
         rows = IND(lwin, S(off[0], off[1] + 8 * h, off[1] + 8 * h + 8))
-        if OPT["lg"][2 * i + h] == "a":
-            act(half("LF", h), rows)
+        plain = gb == "E"
+        if OPT["lg"][2 * i + h] == "a" or plain:
+            act(half("LF", h), rows, bias=-LO - MID if plain else 0.0)
             rows = half("LF", h)
-        ts(half(ub, h), rows, 0.25 - LO, A.add)
+        ts(half(ub, h), rows, MID if plain else 0.25 - LO, A.add)
         n = 128 // len(GE[t][i][h])
         for j, e in enumerate(GE[t][i][h]):
             lo = 128 * h + n * j
-            (cp if e == "v" else act)(S(gb, 16 * lo, 16 * (lo + n)), IND(S("XF", 0, W), S(ub, lo, lo + n)))
-        mm([spread(S(q[0], 0, 256), "XV", h, S("BD4")), spread(S(q[0], 128, 256), "MV", h, S("RM"))], True, False)
-        for k0 in range(0, 16, 2):
-            mm([(step(q[0], k, 16, 16), step(gb, 2048 * h + k, 128, 16), S("WQ")) for k in (k0, k0 + 1)], False, k0 == 14, True)
+            (cp if e == "v" else act)(S(gb, 16 * lo, 16 * (lo + n)), IND(S("X" if plain else "XF", 0, W), S(ub, lo, lo + n)))
+        mm([spread(S(q[0], 0, 256), "XV", h, S("BD4")), spread(S(q[0], 128, 256), "MV", h, S("RM"))]
+           + [spread(S(q[0], lo, lo + 128), "LF", h, S("I1F")) for lo in (0, 128) if plain], True, False)
+        n = 8 if plain else 2
+        for k0 in range(0, 16, n):
+            mm([(step(q[0], k, 16, 16), step(gb, 2048 * h + k, 128, 16), S("WP" if plain else "WQ")) for k in range(k0, k0 + n)], False, k0 + n == 16, True)
         ts(eu(h, 2 * i), S(q[0], 128, 256), -MID, A.is_equal, float(2 ** 24), A.mult)
         tt(S("QS", 256 * h + 128 * i, 256 * h + 128 * i + 128), q, eu(h, 2 * i), A.add)
 
@@ -451,50 +459,70 @@ def build(g, core, T, topo):
                 tt(S(d, o + m * j, o + m * j + m), step(gb, 2048 * h + 4 * m * j + k0, m, 4), S("Y%d" % h, m * j, m * j + m), A.max)
             mm([(step(bank, lo + k0 + 4 * x, 8, 16), step(d, o + x, 128, 4), S("WG")) for x in range(4)], False, False, True)
 
+    def row_t(t, bank):
+        if t == 0:
+            act(S("BB"), IND(S("B", 0, V), VU))
+            ct = S(bank, 0, 16)
+            fold(ct, "SN", "BB", 0, 16, True, True)
+        else:
+            for r0 in (0, 2):
+                mm([(S(bank, 0, 64), sel("SQ", r), step("GC", 16 * r + t, 64, 64)) for r in (r0, r0 + 1)], r0 == 0, r0 == 2)
+            act(S("YF"), S(bank, 0, 64), bias=MID)
+            for x0 in (0, 2):
+                mm([(S(bank, 64, 80), S("UP", 16 - 4 * x, 144 - 4 * x), step("YF", x, 16, 4)) for x in (x0, x0 + 1)], x0 == 0, x0 == 2)
+            cp(wi(0), S(bank, 64, 80))
+            ct = wi(32)
+            ts(ct, wi(0), 4095, A.bitwise_and)
+        ts(w(33), ct, V - 0.5, A.subtract, 32768.0, A.mult)
+        tt(w(35), w(33), ct, A.max)
+        plus(OPT["bf"], w(36), w(35), 4096.0)
+
     lanes(0)
     awake(0)
+    for j in range(4):
+        lo, hi = V + GH // 2 * j, V + GH // 2 * (j + 1)
+        entry(OPT["xf"][2 + j], S("XF", lo, hi), S("NB", lo, hi), S("X", lo, hi), S(("PA", "PW")[j % 2], 0, GH // 2))
     for t in range(RO):
         last = t == RO - 1
         OJ, OB = fw(t, 0, 16), fw(t, 16, 16)
+        gc = "GC" if t else "E"
         for h in range(2):
             kb = "K%d" % h
             k = S(kb, 0, 128)
             act(half("XV", h), IND(S("XR", 0, V), u(16 + 8 * h, 8)), scale=1.0 / 32)
             four("XV", h)
-            entries(t, 0, h, VU, S("L", 0, V), "CU", "GC")
+            entries(t, 0, h, VU, S("L", 0, V), "CU", gc)
             mm([(k, S("CB1"), one(128)), spread(k, "XV", h, S("BM8"))], True, False)
-            near("DA", "GC", h, NC[0][h], kb, 0)
+            near("DA", gc, h, NC[0][h], kb, 0)
             mm([(k, S("CB0"), one(128))], False, True)
             tt(half("KS", h), k, S("QS", 256 * h, 256 * h + 128), A.add)
             scan(half("KM", h), S("RS"), half("KS", h), 0.0, A.add, A.min)
             tt(half("LH", h), IND(half("KM", h), OMIN), S("MK"), A.mult)
-            mm([(S("PW", 8 * h, 8 * h + 8), half("LH", h), G8)], True, True)
-            ts(wi(8 * h, 8), S("PW", 8 * h, 8 * h + 8), MID, A.add)
-            ts(wi(16 + 8 * h, 8), wi(8 * h, 8), 4095, A.bitwise_and)
-            cp(u(32 + 8 * h, 8), wi(16 + 8 * h, 8))
+            o = S("PW", 8 * h, 8 * h + 8)
+            mm([(o, half("LH", h), G8N), (o, S("CB2"), one(8)), (o, S("CB0"), S("HF", 0, 8)), (o, half("LH", h), G8)], True, True)
+            ts(u(32 + 8 * h, 8), o, MID, A.add)
+            ts(u(80 + 8 * h, 8), o, MID, A.add, float(V), A.min)
+            plus(OPT["bf"], S("w", 176 + 8 * h, 184 + 8 * h), o, MID)
         if last:
-            for r0 in range(0, 16, 4):
-                mm([(S("PA", 0, 64), sel("SQ", r), step("XF", r, 64, 16)) for r in range(r0, r0 + 4)], r0 == 0, r0 == 12)
-            ts(wi(96, 64), S("PA", 0, 64), MID, A.add)
-            ts(wi(160, 64), wi(96, 64), 4095, A.bitwise_and)
-            cp(S("FW"), wi(160, 64))
-        else:
-            for r0 in range(0, 16, 4):
-                mm([(S("PA", 0, 16), sel("SQ", r), step("GC", 16 * r + t, 16, 256)) for r in range(r0, r0 + 4)], r0 == 0, r0 == 12)
-            ts(wi(64), S("PA", 0, 16), MID, A.add)
-            ts(CI, wi(64), 4095, A.bitwise_and)
+            for r in range(4):
+                dma("s", lambda r=r: T.FG[:, 64 * r:64 * r + 64], lambda r=r: T.XF[12 + r::16, 0:V], "f%d" % r, 2500,
+                    outs=[S("FG", 64 * r, 64 * r + 64)], ins=[S("XF", 0, V)])
+        elif OPT["ct"] == "PA":
+            row_t(t, "PA")
         if t == 0:
-            for lo in range(0, 2 * GH, GH // 2):
-                mm([(S("PA", 0, GH // 2), S("IF"), S("LG", lo, lo + GH // 2))], True, True)
-                act(S("L", V + lo, V + lo + GH // 2), S("PA", 0, GH // 2), bias=V + lo // GH * GH + LO)
+            for j, lo in enumerate(range(0, 2 * GH, GH // 2)):
+                src = S("LG", lo, lo + GH // 2)
+                if OPT["gl"][j] == "a":
+                    mm([(S("PA", 0, GH // 2), S("IF"), src)], True, True)
+                    src = S("PA", 0, GH // 2)
+                plus(OPT["gl"][j], S("L", V + lo, V + lo + GH // 2), src, V + lo // GH * GH + LO)
         else:
             for d in range(2):
-                scat(S("L", V, WD), u(104 + 4 * d, 2), S("LL%d" % (t - 1), 32 * d, 32 * d + 32))
-            if OPT["eq"] == "v":
-                entry("a", S("QV"), S("MV", 0, LN), S("XV"), S("PW", 256, 512))
+                scat(S("L", V, WD), u(108 - 4 * d, 2), S("LL%d" % (t - 1), 32 * d, 32 * d + 32))
+        if OPT["eq"][t] == "v":
+            entry("a", S("QV"), S("MV", 0, LN), S("XV"), S("PW", 256, 512))
         for h in range(2):
             y = S("Y%d" % h, 0, 128)
-            ts(u(80 + 8 * h, 8), wi(16 + 8 * h, 8), float(V), A.min)
             act(half("XB", h), IND(S("XR", 0, V + 8), u(80 + 8 * h, 8)), scale=1.0 / 32)
             if OPT["z"][h] == "a":
                 mm([(y, S("IH"), half("XV", h)), (y, S("IH"), half("XB", h)), (y, one(128), S("HF", 128, 256)),
@@ -513,38 +541,37 @@ def build(g, core, T, topo):
         act(S("BB"), IND(S("B", 0, V + 8), u(80)))
         act(S("MC"), S("MB", 0, LN), bias=MCB)
         fold(S("PW", 0, 16), "SN", "BB", 0, 16, True, True)
-        tt(G1, BI, VM, A.is_gt)
-        if t > 0:
-            cp(BBU, S("PW", 0, 16))
-            if OPT["eq"] == "v":
-                tt(S("EQ"), IND(S("XF", 0, W), BBU), S("QV"), A.is_equal)
-            else:
-                o = S("PW", 256, 512)
-                act(S("QV"), IND(S("XF", 0, W), BBU))
-                mm([(o, S("I1"), S("XV")), (o, S("WPS"), S("MV", 0, LN)), (o, S("IM1F"), S("QV"))], True, True)
-                act(S("EQ"), o, bias=PSI, func=F.Abs)
-            fold(S("PW", 0, 16), "SA", "EQ", 0, 16, True, True)
-            ts(J1, S("PW", 0, 16), 16 * 8192.0 if OPT["eq"] == "v" else 0.0, A.is_equal)
-        else:
-            tt(J1, S("PW", 0, 16), VF, A.is_equal)
-        tt(JN, J1, G1, A.mult)
-        ts(NJ, JN, -8192.0, A.mult, 8192.0, A.add)
+        cp(BBU, S("PW", 0, 16))
+        tt(G1, BF, VM, A.is_gt)
         if not last:
             ts(VL, VF, float(GH), A.is_lt)
-            tt(TL, JN, VL, A.mult)
+            tt(G2, G1, VL, A.mult)
         nb = 1 if last else 2
-        mm([(step("PA", r, 16 * nb, 16), S("ROWS", 128 * r, 128 * r + 128), S("wb", 0, 16 * nb)) for r in range(16)], True, True)
+        mm([(step("PA", r, 16 * nb, 16), S("ROWS", 128 * r, 128 * r + 128), S("wb", 0, 16 * nb)) for r in range(16)], True, False)
+        if OPT["eq"][t] == "v":
+            tt(S("EQ"), IND(S("XF", 0, W), BBU), S("QV"), A.is_equal)
+        else:
+            o = S("PW", 256, 512)
+            act(S("QV"), IND(S("XF", 0, W), BBU))
+            mm([(o, S("I1"), S("XV")), (o, S("WPS"), S("MV", 0, LN)), (o, S("IM1F"), S("QV"))], True, True)
+            act(S("EQ"), o, bias=PSI, func=F.Abs)
+        mm([(S("PA", LN * j, LN * j + LN), S("BD1" if OPT["eq"][t] == "v" else "BM4"), S("EQ")) for j in range(nb)], False, True)
+        lift = -16.0 if OPT["eq"][t] == "v" else 0.0
         if not last:
-            scan(S("CN"), one(LN), S("PA", LN, 2 * LN), 0.0, A.mult, A.add)
-        act(S("NN"), S("PA", 0, LN))
+            act(S("TL"), S("PA", LN, 2 * LN), bias=lift, func=F.Relu)
+            scan(S("CN"), one(LN), S("TL"), 0.0, A.mult, A.add)
+        act(S("JJ"), S("PA", 0, LN), scale=LOW, bias=c(26 if OPT["eq"][t] == "v" else 27), func=F.Relu)
+        fold(S("PW", 0, 16), "SA", "JJ", 0, 16, True, True)
+        ts(NJ, S("PW", 0, 16), -1.0 / 8, A.mult, 16384.0, A.add)
+        if not last:
+            act(w(38), S("PW", 0, 16), scale=-1.0 / 4, bias=24576.0)
         tt(w(16), NJ, VF, A.add)
-        tt(w(17), NJ, BI, A.add)
+        tt(w(17), NJ, BF, A.add)
         tt(w(18, 2), w(16, 2), DUMP, A.min)
         cp(fw(t, 0, 32), w(18, 2))
         for h in range(2):
             th, eb = S("PA", 256 * h, 256 * h + 256), S("PA", 256 * h + 128, 256 * h + 256)
-            mm([(th, one(128), S("TH")), spread(eb, "XV", h, S("BD4", 0, 128)), spread(eb, "XB", h, S("BM4")), spread(eb, "MC", h, S("RN")),
-                spread(th, "NN", h, S("BJ"))], h == 0, h == 1)
+            mm([spread(th, "JJ", h, S("TH")), spread(eb, "XV", h, S("BD4", 0, 128)), spread(eb, "XB", h, S("BM4")), spread(eb, "MC", h, S("RN"))], h == 0, h == 1)
         for h in range(2):
             tt(eu(h, 4), half("KS", h), S("PA", 256 * h, 256 * h + 128), A.is_ge)
             tt(eu(h, 1), S("QS", 256 * h, 256 * h + 128), S("PA", 256 * h + 128, 256 * h + 256), A.is_equal)
@@ -561,7 +588,7 @@ def build(g, core, T, topo):
             kb = "K%d" % h
             k = S(kb, 0, 128)
             mm([(k, S("CB1"), one(128))], True, False)
-            near("DB", "GC", h, NC[1][h], kb, 0)
+            near("DB", gc, h, NC[1][h], kb, 0)
             mm([(k, S("IBIG"), eu(h, j)) for j in (1, 4)], False, False, True)
             close(k, h, 0)
             tt(half("KC", h), k, half("CL", h), A.min)
@@ -580,17 +607,16 @@ def build(g, core, T, topo):
             fold(S("PW", 0, 4), "SN", "MS", 0, 4, True, True)
             ts(S("q", 0, 4), S("PW", 0, 4), GH - 0.5, A.subtract, 8192.0, A.mult)
             tt(S(me, 64, 68), S("q", 0, 4), S("PW", 0, 4), A.max)
-            exchange([S(me, 0, 68), S(me, 64, 132)], [S(le, 0, 68), S(le, 68, 136)], "te%d" % t, "re%d" % t, 2500)
+            exchange([S(me, 0, 68), S(me, 64, 132)], [S(le, 68, 136), S(le, 0, 68)], "te%d" % t, "re%d" % t, 2500)
             mm([(S("PW", 0, 32), S("RN"), S("MS", 0, 32))], True, True)
             act(S("q", 32, 64), S("PW", 0, 32), bias=LO)
-            y = [w(32, 2), w(34, 2), w(36), w(37), w(38), w(39)]
-            ts(y[0], wi(16, 32), V - 0.5, A.subtract, 32768.0, A.mult)
-            tt(y[1], y[0], wi(16, 32), A.max)
-            ts(y[2], w(35), 4096.0, A.add)
-            tt(y[3], y[2], w(34), A.min)
-            tt(y[4], w(16), NJ, A.add)
-            tt(y[5], y[4], AW, A.add)
-            tt(wi(64), y[5], y[3], A.min)
+            if OPT["ct"] != "PA":
+                row_t(t, OPT["ct"])
+            ts(w(32), BF, V - 0.5, A.subtract, 32768.0, A.mult)
+            tt(w(34), w(32), BF, A.max)
+            tt(w(37), w(36), w(34), A.min)
+            tt(w(39), w(38), AW, A.add)
+            tt(wi(64), w(39), w(37), A.min)
             ts(wi(80), wi(64), 4095, A.bitwise_and)
             cp(PU, wi(80))
             scat(S("M"), OB, S("MF"))
@@ -600,12 +626,11 @@ def build(g, core, T, topo):
             for e in range(t - 1, -1, -1):
                 act(S("FG", 0, LN), IND(S("XF"), fw(e, 0, 16)))
                 cp(IND(S("XF"), fw(e, 16, 16)), S("FG", 0, LN))
-            tt(S("q", 8, 12), S(le, 64, 68), c(112, 4), A.min)
-            tt(S("q", 12, 16), S(le, 68, 72), c(120, 4), A.min)
-            cp(u(104, 4), S("q", 8, 12))
-            ts(u(108, 4), S("q", 12, 16), float(GH), A.add)
-            for d, lo in ((0, 0), (1, 72)):
-                cp(IND(S("XF", V, WD), u(104 + 4 * d, 4)), S(le, lo, lo + 64))
+            tt(S("q", 8, 12), S(le, 132, 136), c(112, 4), A.min)
+            tt(S("q", 12, 16), S(le, 0, 4), c(120, 4), A.min)
+            cp(u(108, 4), S("q", 8, 12))
+            ts(u(104, 4), S("q", 12, 16), float(GH), A.add)
+            cp(IND(S("XF", V, WD), u(104, 8)), S(le, 4, 132))
             if t < RO - 2:
                 for d in range(2):
                     cp(fw(t, 32 + 2 * d, 2), u(104 + 4 * d, 2))
@@ -620,14 +645,18 @@ def build(g, core, T, topo):
             dma("a", lambda: T.yx[:], lambda: T.X[:, 0:V], "ox", 3000, ins=[S("X", 0, V)])
             act(S("MF"), S("MV", 0, LN))
             scat(S("M"), OB, S("MF"))
+            mm([(S("PW", 0, 64), S("IM1F"), S("FG", 64 * r, 64 * r + 64)) for r in range(4)], True, True)
+            ts(wi(96, 64), S("PW", 0, 64), 4096.0, A.mult, MID, A.add)
+            ts(wi(160, 64), wi(96, 64), 4095, A.bitwise_and)
+            cp(S("FW"), wi(160, 64))
             act(S("MH"), IND(S("M", 0, V), S("FW")))
-            mm([(S("PW", 0, 64), sel("SN", r), S("MH", 64 * r, 64 * r + 64)) for r in range(16)], True, True)
+            fold(S("PW", 0, 64), "SN", "MH", 0, 64, True, True)
             act(S("YF"), S("PW", 0, 64))
             dma("s", lambda: T.yf[:], lambda: T.YF[:], "of", 2500, ins=[S("YF")])
         for h in range(2):
             kb = "K%d" % h
             k = S(kb, 128, 256)
-            mm([(k, S("CB1"), one(128)), spread(k, "NN", h, S("BJ", 128, 256))], True, False)
+            mm([(k, S("CB1"), one(128)), spread(k, "JJ", h, S("TH", 128, 256))], True, False)
             tt(eu(h, 3), S("QS", 256 * h + 128, 256 * h + 256), S("PA", 256 * h + 128, 256 * h + 256), A.is_equal)
             near("DC", "GO", h, NC[2][h], kb, 128)
             mm([(k, S("IMB"), eu(h, 4)), (k, S("IBIG"), eu(h, 3))], False, False, True)
@@ -642,10 +671,9 @@ def build(g, core, T, topo):
                 scat(S("L"), u(48 + 8 * h, 8), half("NL", h))
         if last:
             break
-        ts(S("q", 0, 32), IND(S("NL"), s2), GH + LO, A.is_lt)
-        tt(S("q", 64, 96), IND(S("NL"), s2), S("q", 32, 64), A.subtract)
-        tt(S("q", 128, 160), S("q", 0, 32), S("q", 64, 96), A.mult)
-        tt(S("q", 160, 192), S("q", 128, 160), S("q", 32, 64), A.add)
+        ts(S("q", 0, 32), IND(S("NL"), s2), GH + LO, A.is_lt, 8192.0, A.mult)
+        tt(S("q", 64, 96), S("q", 0, 32), S("q", 32, 64), A.add)
+        tt(S("q", 160, 192), IND(S("NL"), s2), S("q", 64, 96), A.min)
         for d in range(2):
             act(S(ml, 32 * d, 32 * d + 32), S("q", 160, 192), bias=float(V + d * GH))
         exchange([S(ml, 0, 32), S(ml, 32, 64)], [S(ll, 0, 32), S(ll, 32, 64)], "tm%d" % t, "rm%d" % t, 2500)
@@ -702,8 +730,8 @@ def order(nodes):
         return cost, lats, fore, back
     cases = [case(*x) for x in CASES]
 
-    def place(lst, cost, before, tail):
-        at = [0.0] * n
+    def place(lst, cost, before, tail, at=None):
+        at = at or [0.0] * n
         los, his = [[] for _ in range(6)], [[] for _ in range(6)]
         for k in lst:
             st = tail[k]
@@ -776,6 +804,50 @@ def order(nodes):
         new = judged(packed(key, *cases[0]), 1.006 * end)
         if new[0] <= best[0]:
             best = new
+    cur, late = best, None
+    for it in range(LOCAL):
+        score, seq, runs = cur
+        old = runs[0][0]
+        rnd = (rnd * 1103515245 + 12345) % 2147483648
+        m = 20 + rnd // 64 % WIDE
+        a = rnd // 16384 % (n - 10)
+        amp = AMP * (0.25, 0.5, 1.0, 2.0)[rnd // 16 % 4]
+        part = seq[a:a + m]
+        key = {}
+        for i in part:
+            rnd = (rnd * 1103515245 + 12345) % 2147483648
+            x = old[i] + amp * (rnd / 2147483648.0 - 0.5)
+            for j in pre[i]:
+                if key.get(j, -BIG) >= x:
+                    x = key[j] + 1.0
+            key[i] = x
+        free = [0.0] * 6
+        for k in seq[max(0, a - 200):a]:
+            free[queue[k]] = old[k] + cost[k]
+        free[5] = 0.0
+        head = [free[q] for q in queue]
+        at = place(sorted(part, key=key.get), cost, fore, head, list(old))
+        if late is None:
+            late, free = [0.0] * n, [0.0] * 6
+            for k in reversed(seq):
+                st = max(free[queue[k]], lats[k])
+                for j, dl in back[k]:
+                    if late[j] + dl > st:
+                        st = late[j] + dl
+                late[k] = st
+                if queue[k] < 5:
+                    free[queue[k]] = st + cost[k]
+        free = [0.0] * 6
+        for k in reversed(seq[a + m:a + m + 200]):
+            free[queue[k]] = late[k] + cost[k]
+        free[5] = 0.0
+        rev = place(sorted(part, key=lambda i: -at[i] - cost[i]), cost, back, [max(free[queue[i]], lats[i]) for i in range(n)], list(late))
+        at = place(sorted(part, key=lambda i: -rev[i] - cost[i]), cost, fore, head, at)
+        new = judged(seq[:a] + sorted(part, key=lambda i: at[i]) + seq[a + m:], 1.004 * runs[0][1])
+        if new[0] <= score + WARM * (1.0 - it / LOCAL) * (rnd // 256 % 1024) / 1024.0:
+            cur, late = new, None
+            if new[0] <= best[0]:
+                best = new
     chains = {}
     for it in range(SWAPS):
         score, seq, runs = best

from concourse.bass import DstId, RemoteDMATransfer
from concourse.mybir import AluOpType as A, AxisListType, ActivationFunctionType as F

V, GH, W, LN, RO = 1024, 896, 2816, 256, 4
WD = W + LN + 128
BIG = float(2 ** 26)
R13 = 1.5 * 2 ** 36
MID = 1408.0
LO = 64.0
GE = [[["va", "aa"], ["aa", "aa"]]] * RO
NC = [[1, 1], [1, 1], [1, 2]]
OPT = dict(vf="a", bd="a", xf="aaaaaa", lg="vava", eq="vvvv", z="vv", fg="a", bf="a", ct="PA", gl="vvvv")
PEC, DLAT, PASSES, SWAPS, AMP, SPAN = 0.5, 3600, 5000, 8000, 2000.0, 3500.0
LOCAL, WIDE, WARM = 16000, 400, 0.002
CASES = [(1.56, 3.8, 0.5, 150.0, 1.0), (1.2, 2.5, 0.55, 140.0, 1.0), (1.9, 5.2, 0.5, 105.0, 0.7), (1.4, 4.6, 0.45, 190.0, 1.35)]
PLAN = []

SCRATCH = {}


def _buf(names, n, dtp, where="sbuf"):
    for x in names.split():
        SCRATCH[x] = (where, [128, n], dtp)


_buf("X NB", W, "bfloat16")
_buf("MH", V, "bfloat16")
_buf("L M B XF XR", WD, "float32")
_buf("HI", V, "int32")
_buf("GA", GH, "bfloat16")
_buf("GL", GH, "float16")
_buf("LG", 2 * GH, "float16")
_buf("IF", 128, "float16")
_buf("ZT", 256, "float16")
_buf("GC GO", 4096, "float32")
_buf("DA DB DC E", 4096, "bfloat16")
_buf("ROWS", 2048, "bfloat16")
_buf("HB ONE HF", 512, "bfloat16")
_buf("EU", 1280, "bfloat16")
_buf("SA SN S32", 144, "bfloat16")
_buf("UP IU SQ", 144, "float32")
_buf("RN RM BD1 IBIG IMB I1 BDW BDB BJM WPS CB1 CB0 CB2 IH BM8 BM4 MK RS", 128, "bfloat16")
_buf("IG IR I1F IM1F", 128, "float32")
_buf("BD4", 256, "bfloat16")
_buf("MB MZ NL", 272, "float32")
_buf("FG", 320, "float32")
_buf("MV", 272, "bfloat16")
_buf("KC CL RF KS KM LH QV MF LF ZF", 256, "float32")
_buf("QS", 512, "float32")
_buf("PW2 I256 CR EQ BB TH MC JJ TL CN XV XB ZZ", 256, "bfloat16")
_buf("CU OU PR", 256, "uint16")
_buf("FW", 64, "uint16")
_buf("fw", 160, "uint16")
_buf("w", 768, "float32")
_buf("c", 256, "float32")
_buf("ci", 128, "int32")
_buf("wi", 224, "int32")
_buf("wb", 32, "bfloat16")
_buf("WG", 8, "bfloat16")
_buf("WQ", 16, "float32")
_buf("WP", 16, "bfloat16")
_buf("u", 128, "uint16")
_buf("cu", 8, "uint16")
_buf("MS", 64, "bfloat16")
_buf("q", 200, "float32")
_buf("YF", 64, "float32")
_buf("ME0 ME1 ME2", 132, "float32")
_buf("LE0 LE1 LE2", 136, "float32")
_buf("ML0 ML1 ML2 LL0 LL1 LL2", 64, "float32")
_buf("Q0 Q1 K0 K1 Y0 Y1 PA PW", 512, "float32", "psum")

SEMAPHORES = (["sv", "sa", "sp", "sg", "dx", "dn", "dm", "dh", "dl", "dt", "db", "b0", "b1", "b4", "f0", "f1", "f2", "f3", "ox", "ol", "of", "tx", "rx", "tl", "rl"]
              + ["%s%d" % (a, t) for a in ("te", "re", "tm", "rm") for t in range(RO - 1)] + ["m%d" % j for j in range(1, 40)])
SHORT = ("bfloat16", "uint16", "float16")


def S(name, lo=0, hi=None, st=1, p=None):
    return (name, lo, SCRATCH[name][1][1] if hi is None else hi, st, p)


def step(name, lo, n, st):
    return S(name, lo, lo + st * (n - 1) + 1, st)


def IND(win, off):
    return ("*", win, off)


def build(g, core, T, topo):
    rank = T.rank_of(core)
    n_ranks = len(T.cores)
    nodes = []
    moves = []
    eng = {"v": g.vector, "a": g.scalar, "p": g.tensor, "g": g, "s": g.sync}

    def ap(x):
        if not isinstance(x, tuple):
            return x
        if x[0] == "*":
            return ap(x[1]).indirect(ap(x[2]))
        ps = slice(None) if x[4] is None else slice(x[4][0], x[4][1])
        return T[x[0]][ps, x[1]:x[2]:x[3]] if x[3] != 1 else T[x[0]][ps, x[1]:x[2]]

    def cnt(x):
        if x[0] == "*":
            return 16 * (x[2][2] - x[2][1])
        return (x[2] - x[1] + x[3] - 1) // x[3]

    def dty(x):
        return SCRATCH[x[1][0] if x[0] == "*" else x[0]][2]

    def psum(x):
        return x[0] != "*" and SCRATCH[x[0]][0] == "psum"

    def node(e, cost, fn, outs, ins, lat=0, sem=None, inc=1, after=(), free=False):
        rd, wr = [], []
        for x in ins:
            if isinstance(x, tuple):
                rd += [x[1], x[2]] if x[0] == "*" else [x]
        for x in outs:
            if x[0] == "*":
                wr.append(x[1])
                rd.append(x[2])
            else:
                wr.append(x)
        ind = [cnt(x) if isinstance(x, tuple) and x[0] == "*" else 0 for x in list(ins[:1]) + list(outs[:1])]
        nodes.append(dict(e=e, ind=ind if len(ind) == 2 else [0, 0], cost=cost, fn=fn, rd=rd, wr=wr, lat=lat, sem=sem, inc=inc, after=list(after), free=free))
        return len(nodes) - 1

    def vcost(out, i0, base):
        n = cnt(out)
        if out[0] == "*":
            return 60 + 3.8 * n
        if i0[0] == "*":
            return 60 + 1.56 * n
        return max(64, base * n) + 10

    def narrow(*xs):
        return 0.5 if all(dty(x) in SHORT for x in xs) else 1.0

    def cp(out, i0):
        return node("v", vcost(out, i0, narrow(out, i0)), lambda: g.vector.tensor_copy(ap(out), ap(i0)), [out], [i0])

    def tt(out, i0, i1, op):
        return node("v", vcost(out, i0, 1.0 if psum(i0) or psum(i1) else 2.0),
                    lambda: g.vector.tensor_tensor(ap(out), ap(i0), ap(i1), op), [out], [i0, i1])

    def ts(out, i0, s1, op0, s2=None, op1=None):
        if op1 is None:
            fn = lambda: g.vector.tensor_scalar(ap(out), ap(i0), ap(s1), None, op0)
        else:
            fn = lambda: g.vector.tensor_scalar(ap(out), ap(i0), ap(s1), ap(s2), op0, op1)
        return node("v", vcost(out, i0, narrow(out, i0)), fn, [out], [i0, s1, s2])

    def scan(out, d0, d1, first, op0, op1):
        return node("v", vcost(out, d1, narrow(out, d0, d1)), lambda: g.vector.tensor_tensor_scan(ap(out), ap(d0), ap(d1), first, op0, op1), [out], [d0, d1])

    def total(out, i0):
        return node("v", 74, lambda: g.vector.tensor_reduce(ap(out), ap(i0), AxisListType.X, A.add), [out], [i0])

    def mset(out, val):
        return node("v", max(64, cnt(out) * narrow(out)), lambda: g.vector.memset(ap(out), val), [out], [])

    def act(out, i0, bias=None, scale=None, func=F.Identity, accum=None):
        kw = {}
        if bias is not None:
            kw["bias"] = bias
        if scale is not None:
            kw["scale"] = scale
        if accum is not None:
            kw["accum_out"] = accum
        return node("a", vcost(out, i0, 1.0) + (20 if accum is None else 45),
                    lambda: g.scalar.activation(ap(out), ap(i0), func, **{k: ap(x) for k, x in kw.items()}),
                    [out] + ([] if accum is None else [accum]), [i0, bias, scale])

    def times(e, out, i0, wt):
        return act(out, i0, scale=wt) if e == "a" else ts(out, i0, wt, A.mult)

    def plus(e, out, i0, b):
        return act(out, i0, bias=b) if e == "a" else ts(out, i0, b, A.add)

    def scat(win, off, src):
        return act(IND(win, off), src, func=F.Silu)

    def mm(items, start, stop, free=False, after=()):
        def fn():
            r = None
            for j, (o, l, x) in enumerate(items):
                r = g.tensor.matmul(ap(o), ap(l), ap(x), start and j == 0, stop and j == len(items) - 1)
            return r
        cost = sum(PEC * max(64, cnt(x)) * (4 if dty(x) == "float32" else 1) for o, l, x in items)
        return node("p", cost, fn, [o for o, l, x in items], [y for o, l, x in items for y in (l, x)], after=after, free=free and not (start or stop))

    def sel(fam, r):
        return S(fam, 15 - r, 143 - r)

    def fold(out, fam, src, lo, n, start, stop):
        return mm([(out, sel(fam, r), step(src, lo + r, n, 16)) for r in range(16)], start, stop)

    def iota(out, pat, base, cm=0, after=()):
        if dty(out) == "int32":
            fn = lambda: g.iota(ap(out), pat, base, cm)
        else:
            fn = lambda: g.iota(ap(out), pat, base, cm, allow_small_or_imprecise_dtypes=True)
        return node("g", 160 + 2 * cnt(out), fn, [out], [], after=after)

    def dma(e, out, in_, sem, lat, outs=(), ins=(), **kw):
        return node(e, 100 if e != "g" else 1200, lambda: eng[e].dma_start(out(), in_(), **kw), list(outs), list(ins), lat=lat, sem=sem, inc=16)

    def move(e, out, in_, rows=slice(None), behind=()):
        moves.append(1)
        return dma(e, lambda: T[out[0]][rows, out[1]:out[2]], lambda: T[in_[0]][rows, in_[1]:in_[2]], "m%d" % len(moves), DLAT, outs=[out], ins=[in_] + list(behind))

    def exchange(srcs, dsts, tsem, rsem, lat):
        to = [T.cores[(rank - d) % n_ranks] for d in (1, 2)]
        es = [e for e in topo.engines(core, to[0]) if e in topo.engines(core, to[1])]
        h = len(es) // 2

        def fn():
            trs = []
            for d in range(2):
                rid, pid = topo.addr(to[d], core)
                trs.append(RemoteDMATransfer(dst_ids=[DstId(rid=rid, pnc=pid)], dma_engine_mask=sum(1 << e for e in es[d * h:(d + 1) * h]),
                                             remote_sem=T.sem[rsem], src=ap(srcs[d]), dst=ap(dsts[d])))
            g.remote_dma_fused(trs, local_sem=T.sem[tsem])
            return None
        k = node("g", 600, fn, [], srcs, lat=lat, sem=tsem, inc=2 * h)
        node("R", 0, None, dsts, [], lat=1500, sem=rsem, inc=2 * h, after=[k])
        return k

    dma("s", lambda: T.X[:, 0:V], lambda: T.feat[:], "dx", 3500, outs=[S("X", 0, V)])
    dma("a", lambda: T.HI[:], lambda: T.hits[:], "dh", 4500, outs=[S("HI")])
    dma("s", lambda: T.wi[:, 48:64], lambda: T.lane0[:], "dl", 2500, outs=[S("wi", 48, 64)])
    sent = exchange([S("X", 0, GH)] * 2, [S("X", V, V + GH), S("X", V + GH, W)], "tx", "rx", 6000)

    def c(j, n=1):
        return S("c", j, j + n)

    def ci(j, n=1):
        return S("ci", j, j + n)

    def fill(out, val):
        return iota(out, [[0, cnt(out)]], val, after=[sent])
    ROW, GRP, HW, PID, G15, WN, PSI, R4A, R4B, MCB, LOW, TMP, TMP2, TC = [c(j) for j in range(14)]
    DUMP, D8, G8, TH8, T16a, I16 = c(64, 32), c(112, 8), c(128, 8), c(136, 8), c(144, 16), c(192, 16)
    OMIN, G8N = S("cu"), c(160, 8)
    first = [iota(ci(0), [[0, 1]], 0, 1), iota(S("IU"), [[1, 144]], 0), iota(S("IG"), [[1, 8], [0, 16]], 0)]
    iota(S("NB", 0, V), [[32, V // 256], [0, 256]], 0, after=[iota(S("I256"), [[32, 256]], 0, after=first)])
    iota(S("NB", V, W), [[32, (W - V) // 256], [0, 256]], 32 * V // 256, after=[sent])
    iota(S("IR"), [[0, 8], [1, 16]], 0, after=[sent])
    dma("s", lambda: T.NB[1::16, 0:V], lambda: T.I256[0:32, :], "dn", 2500, outs=[S("NB", 0, V)], ins=[S("I256")])
    dma("s", lambda: T.NB[1::16, V:W], lambda: T.I256[0:56, :], "dm", 2500, outs=[S("NB", V, W)], ins=[S("I256")])
    ts(ci(1), ci(0), 15, A.bitwise_and)
    ts(ci(2), ci(0), 4, A.arith_shift_right)
    cp(c(0, 2), ci(1, 2))
    cp(PID, ci(0))
    ts(G15, GRP, 16.0, A.mult, 15.0, A.add)
    cp(I16, S("IU", 0, 16))
    ts(c(224, 16), S("IU", 0, 16), ROW, A.is_equal)
    mk = lambda j: c(224 + j)
    ts(TMP, mk(0), 4.0, A.mult)
    ts(TMP2, mk(1), 1.0 / 32, A.mult, TMP, A.add)
    ts(WN, mk(4), 4.0, A.mult, TMP2, A.add)
    ts(c(14), mk(12), mk(13), A.add, 85.0 / 4096, A.mult)
    ts(HW, mk(14), 86.0 / 4096, A.mult, c(14), A.add)
    ts(c(15), mk(15), 128.0 / 4096, A.mult)
    ts(PSI, HW, 5.0, A.mult, c(15), A.add)
    ts(R4A, HW, -float(V // 256), A.mult)
    ts(R4B, HW, -float((V + GH) // 256), A.mult, c(15), A.subtract)
    ts(MCB, mk(0), -MID / 4, A.mult)
    ts(LOW, ROW, 8.0, A.is_lt)
    ts(c(26), LOW, -17.0, A.mult, 1.0, A.add)
    ts(c(27), LOW, -1.0, A.mult, 1.0, A.add)
    ts(c(28), LOW, -BIG / 4, A.mult, BIG / 8, A.add)
    ts(S("S32"), S("IU"), G15, A.is_equal, 32.0, A.mult)
    ts(S("SN"), S("S32"), WN, A.mult, 1.0 / 32, A.mult)
    for fam, wt in (("SA", 256.0), ("SQ", -128.0)):
        times("a", S(fam), S("S32"), wt)
    ts(S("BD1"), S("IG"), GRP, A.is_equal)
    ts(S("I1"), S("IU", 0, 128), PID, A.is_equal)
    for e, m, base, wt in (("v", "RN", "BD1", WN), ("v", "IBIG", "I1", BIG), ("a", "I1F", "I1", 1.0), ("a", "IM1F", "I1", -1.0),
                           ("v", "RM", "RN", -1.0), ("a", "IMB", "I1", -BIG), ("v", "IH", "I1", 0.5), ("v", "IF", "I1", 1.0)):
        times(e, S(m), S(base), wt)
    ts(c(16), ROW, 4.0, A.is_lt)
    ts(c(17), PID, 16.0, A.add)
    ts(S("UP"), S("IU"), c(17), A.is_equal, c(16), A.mult)
    mset(S("ONE"), 1.0)
    ts(G8, S("IU", 0, 8), GRP, A.is_equal)
    mset(S("WPS"), 0.0)
    for r, j, wt in ((12, 0, 85.0), (13, 0, 85.0), (14, 0, 86.0), (15, 1, 1.0)):
        ts(step("WPS", r, 8, 16), G8, mk(j), A.mult, -wt / 2 ** 17, A.mult)
    for r in range(0, 16, 4):
        node("g", 200 + 1024, lambda r=r: g.affine_select(T.ROWS[:, 128 * r:128 * r + 512], T.ONE[:], [[1, 4], [16, 8], [0, 16]], A.is_equal, 0.0, r, -1),
             [S("ROWS", 128 * r, 128 * r + 512)], [S("ONE")], after=[sent])
    mset(c(32, 16), 0.5)
    scan(S("PW2", 0, 16), c(32, 16), c(32, 16), 131072.0, A.mult, A.max)
    for n in (16, 32, 64, 128):
        cp(S("PW2", n, 2 * n), S("PW2", 0, n))
    tt(c(48, 16), S("PW2", 0, 16), c(224, 16), A.mult)
    total(c(21), c(48, 16))
    ts(S("BDW"), S("BD1"), c(21), A.mult, 0.5, A.mult)
    for m, wt in ((S("BDB"), 65536.0), (S("BJM"), -1.0 / 16), (S("TH", 128, 256), c(28)),
                  (S("BD4", 0, 128), 4096.0), (S("BD4", 128, 256), 4096.0), (S("BM8"), -8192.0), (S("BM4"), -4096.0)):
        times(OPT["bd"], m, S("BD1"), wt)
    times("a", S("WG"), G8, 8192.0)
    times("a", G8N, G8, -1.0)
    for lo in (0, 8):
        times("a", S("WQ", lo, lo + 8), G8, -4096.0)
    act(S("WP"), S("WQ"))
    fill(S("CB1"), 0)
    for lo, hi, val in ((0, 64, R13 / 64), (64, 96, -float(2 ** 19)), (96, 97, 32768.0)):
        mset(S("CB1", p=(lo, hi)), val)
    mset(S("CB0"), -R13 / 128)
    mset(S("CB2"), R13 / 256)
    for j, val in enumerate((0.5, -1.0 / 512, -2.0 ** -13, 2.0 ** -13)):
        mset(S("HF", 128 * j, 128 * j + 128), val)
    ts(S("MK"), S("IR"), ROW, A.is_equal)
    ts(S("RS"), S("IR"), 0.0, A.is_equal, BIG, A.mult)
    ts(OMIN, c(192, 8), 16.0, A.mult, 15.0, A.add)
    for b in ("MV", "MB"):
        fill(S(b, 256, 272), 128)
    fill(S("MZ", 256, 272), 0)
    fill(S("NL", 256, 272), int(LO))
    fill(S("XF", W, WD), 0)
    fill(S("B", V, V + 8), 128)
    ts(T16a, I16, 16.0, A.mult, ROW, A.add)
    ts(c(64, 16), T16a, float(W), A.add)
    ts(c(80, 16), T16a, float(W), A.add)
    ts(D8, c(144, 8), float(W - V + LN), A.add)
    ts(c(120, 4), c(116, 4), -float(GH), A.add)
    ts(c(18, 2), c(144, 2), 0.5, A.add)
    dma("g", lambda: T.ci[0:1, 96:104], lambda: T.th[:], "dt", 3000, outs=[ci(96, 8)], allow_slow_non_contiguous=True)
    node("g", 200, lambda: g.partition_broadcast(T.ci[:, 104:112], T.ci[0:1, 96:104], 128), [ci(104, 8)], [ci(96, 8)])
    tt(TH8, ci(104, 8), G8, A.mult)
    total(c(20), TH8)
    cp(ci(8), c(20))
    ts(ci(9), ci(8), 15, A.bitwise_and)
    ts(ci(10), ci(8), 4080, A.bitwise_and)
    ts(c(22), ci(9), 8.5, A.add, mk(9), A.mult)
    ts(c(23), ci(10), mk(8), A.mult, c(22), A.add)
    ts(c(24), mk(10), -4096.0, A.mult, c(23), A.add)
    ts(TC, LOW, BIG / 8 / 4096, A.mult, c(24), A.add)
    ts(S("TH", 0, 128), S("BD1"), TC, A.mult, 4096.0, A.mult)

    ts(S("L", 0, V), S("HI"), LO, A.add)
    act(S("GA"), S("L", 0, GH), bias=GH + LO, scale=-1.0, func=F.Relu)
    for bank, lo, hi in (("K0", 0, 512), ("K1", 512, GH)):
        mm([(S(bank, 0, hi - lo), S("RN"), S("NB", lo, hi)), (S(bank, 0, hi - lo), S("IBIG"), S("GA", lo, hi))], True, True)
        tt(S("GL", lo, hi), S(bank, 0, hi - lo), S("HI", lo, hi), A.min)
    exchange([S("GL")] * 2, [S("LG", 0, GH), S("LG", GH, 2 * GH)], "tl", "rl", 6000)

    def entry(e, out, names, x, o):
        mm([(o, S("I1"), x), (o, S("WPS"), names)], True, True)
        plus(e, out, o, PSI)

    for j, lo in enumerate((0, 512)):
        entry(OPT["xf"][j], S("XF", lo, lo + 512), S("NB", lo, lo + 512), S("X", lo, lo + 512), S("Q%d" % j))
    act(S("XR", 0, V), S("X", 0, V), scale=32.0)
    fill(S("XR", V, V + 8), 0)
    move("g", S("M", 0, V), S("NB", 0, V), behind=[S("X", V, W)])
    mset(S("B", 0, V), 0.0)
    dma("s", lambda: T.wi[:, 96:160], lambda: T.hits[0::16, :], "db", 2500, outs=[S("wi", 96, 160)])
    ts(S("wi", 160, 224), S("wi", 96, 160), 8, A.arith_shift_right)
    ts(S("wi", 96, 160), S("wi", 96, 160), 255, A.bitwise_and)
    for r, lo in ((0, 160), (1, 96)):
        ts(S("RF", 64 * r, 64 * r + 64), S("wi", lo, lo + 64), 32.0, A.mult)
    for r, lo in ((0, 0), (4, 0), (1, 64)):
        dma("s", lambda r=r: T.B[r::16, 0:V], lambda lo=lo: T.RF[:, lo:lo + 64], "b%d" % r, 2500,
            outs=[S("B", 64 * r, 64 * r + 64)], ins=[S("RF", lo, lo + 64)])

    def w(j, n=1):
        return S("w", 16 * j, 16 * (j + n))

    def u(j, n=16):
        return S("u", j, j + n)

    def wi(j, n=16):
        return S("wi", j, j + n)

    def fw(t, lo, n):
        return S("fw", 40 * t + lo, 40 * t + lo + n)
    VF, VA, AW, VM, NJ, VL = [w(j) for j in range(6)]
    BF = w(11)
    PU, VU, BU, OL, BBU, SU = u(0), u(16), u(32), u(48), u(64), u(96, 4)
    G1, G2 = S("wb", 0, 16), S("wb", 16, 32)

    def half(b, h, lo=0):
        return S(b, lo + 128 * h, lo + 128 * h + 128)

    def one(n):
        return S("ONE", 0, n)

    def lanes(t):
        if t == 0:
            cp(VU, wi(48))
            cp(VF, wi(48))
            act(S("MV", 0, LN), IND(S("NB", 0, V), VU))
        else:
            act(S("MV", 0, LN), IND(S("M", 0, V), PU))
            fold(S("PW", 0, 16), "SN", "MV", 0, 16, True, True)
            cp(VU, S("PW", 0, 16))
            (act if OPT["vf"] == "a" else cp)(VF, S("PW", 0, 16))
        mm([(S("PW", 256, 512), S("RN"), S("MV", 0, LN))], True, True)
        cp(S("PR"), S("PW", 256, 512))
        for s in range(16):
            ts(S("E", 272 * s, 256 * s + 256), S("PR", 16 * s, 256), S("w", s, s + 1), A.is_equal)

    def awake(t):
        mm([(half("PA", h), half("MV", h), S("RN")) for h in range(2)], True, True)
        act(S("CL"), S("PA", 0, LN), bias=-MID)
        mm([(S("PA", 0, LN), S("BJM"), S("PW2"))], True, False)
        for q in range(0, 16, 4):
            mm([(S("PA", 16 * s, 16 * s + 16), S("BDW"), S("E", 272 * s, 272 * s + 16)) for s in range(q, q + 4)]
               + [(S("PA", 16 * s + 16, LN), S("BDB"), S("E", 272 * s + 16, 256 * s + 256)) for s in range(q, min(q + 4, 15))], False, q == 12, True)
        act(S("CR"), S("PA", 0, LN), bias=1.0, func=F.Relu)
        fold(S("PA", 256, 272), "SA", "CR", 0, 16, True, True)
        tt(VA, S("PA", 256, 272), VF, A.add)
        tt(VM, VA, c(64, 16), A.min)
        cp(OL, VM)
        if t < RO - 1:
            ts(AW, VM, float(V), A.is_ge, -16384.0, A.mult)
            tt(AW, AW, VF, A.add)
            move("g", S("MF"), S("MV", 0, LN))

    def spread(out, src, h, wts):
        return (out, half(src, h), wts)

    def four(src, h):
        mm([(step("Y%d" % h, j, 128, 4), S("I1"), half(src, h)) for j in range(4)], True, True)

    def entries(t, i, h, off, lwin, ub, gb):
        q = S("Q%d" % h, 0, 128)
        rows = IND(lwin, S(off[0], off[1] + 8 * h, off[1] + 8 * h + 8))
        plain = gb == "E"
        if OPT["lg"][2 * i + h] == "a" or plain:
            act(half("LF", h), rows, bias=-LO - MID if plain else 0.0)
            rows = half("LF", h)
        ts(half(ub, h), rows, MID if plain else 0.25 - LO, A.add)
        n = 128 // len(GE[t][i][h])
        for j, e in enumerate(GE[t][i][h]):
            lo = 128 * h + n * j
            (cp if e == "v" else act)(S(gb, 16 * lo, 16 * (lo + n)), IND(S("X" if plain else "XF", 0, W), S(ub, lo, lo + n)))
        mm([spread(S(q[0], 0, 256), "XV", h, S("BD4")), spread(S(q[0], 128, 256), "MV", h, S("RM"))]
           + [spread(S(q[0], lo, lo + 128), "LF", h, S("I1F")) for lo in (0, 128) if plain], True, False)
        n = 8 if plain else 2
        for k0 in range(0, 16, n):
            mm([(step(q[0], k, 16, 16), step(gb, 2048 * h + k, 128, 16), S("WP" if plain else "WQ")) for k in range(k0, k0 + n)], False, k0 + n == 16, True)
        ts(eu(h, 2 * i), S(q[0], 128, 256), -MID, A.is_equal, float(2 ** 24), A.mult)
        tt(S("QS", 256 * h + 128 * i, 256 * h + 128 * i + 128), q, eu(h, 2 * i), A.add)

    def eu(h, j):
        return S("EU", 640 * h + 128 * j, 640 * h + 128 * j + 128)

    def near(d, gb, h, n, bank, lo):
        m = 512 // n
        for k0 in range(4):
            o = 2048 * h + 512 * k0
            for j in range(n):
                tt(S(d, o + m * j, o + m * j + m), step(gb, 2048 * h + 4 * m * j + k0, m, 4), S("Y%d" % h, m * j, m * j + m), A.max)
            mm([(step(bank, lo + k0 + 4 * x, 8, 16), step(d, o + x, 128, 4), S("WG")) for x in range(4)], False, False, True)

    def row_t(t, bank):
        if t == 0:
            act(S("BB"), IND(S("B", 0, V), VU))
            ct = S(bank, 0, 16)
            fold(ct, "SN", "BB", 0, 16, True, True)
        else:
            for r0 in (0, 2):
                mm([(S(bank, 0, 64), sel("SQ", r), step("GC", 16 * r + t, 64, 64)) for r in (r0, r0 + 1)], r0 == 0, r0 == 2)
            act(S("YF"), S(bank, 0, 64), bias=MID)
            for x0 in (0, 2):
                mm([(S(bank, 64, 80), S("UP", 16 - 4 * x, 144 - 4 * x), step("YF", x, 16, 4)) for x in (x0, x0 + 1)], x0 == 0, x0 == 2)
            cp(wi(0), S(bank, 64, 80))
            ct = wi(32)
            ts(ct, wi(0), 4095, A.bitwise_and)
        ts(w(33), ct, V - 0.5, A.subtract, 32768.0, A.mult)
        tt(w(35), w(33), ct, A.max)
        plus(OPT["bf"], w(36), w(35), 4096.0)

    lanes(0)
    awake(0)
    for j in range(4):
        lo, hi = V + GH // 2 * j, V + GH // 2 * (j + 1)
        entry(OPT["xf"][2 + j], S("XF", lo, hi), S("NB", lo, hi), S("X", lo, hi), S(("PA", "PW")[j % 2], 0, GH // 2))
    for t in range(RO):
        last = t == RO - 1
        OJ, OB = fw(t, 0, 16), fw(t, 16, 16)
        gc = "GC" if t else "E"
        for h in range(2):
            kb = "K%d" % h
            k = S(kb, 0, 128)
            act(half("XV", h), IND(S("XR", 0, V), u(16 + 8 * h, 8)), scale=1.0 / 32)
            four("XV", h)
            entries(t, 0, h, VU, S("L", 0, V), "CU", gc)
            mm([(k, S("CB1"), one(128)), spread(k, "XV", h, S("BM8"))], True, False)
            near("DA", gc, h, NC[0][h], kb, 0)
            mm([(k, S("CB0"), one(128))], False, True)
            tt(half("KS", h), k, S("QS", 256 * h, 256 * h + 128), A.add)
            scan(half("KM", h), S("RS"), half("KS", h), 0.0, A.add, A.min)
            tt(half("LH", h), IND(half("KM", h), OMIN), S("MK"), A.mult)
            o = S("PW", 8 * h, 8 * h + 8)
            mm([(o, half("LH", h), G8N), (o, S("CB2"), one(8)), (o, S("CB0"), S("HF", 0, 8)), (o, half("LH", h), G8)], True, True)
            ts(u(32 + 8 * h, 8), o, MID, A.add)
            ts(u(80 + 8 * h, 8), o, MID, A.add, float(V), A.min)
            plus(OPT["bf"], S("w", 176 + 8 * h, 184 + 8 * h), o, MID)
        if last:
            for r in range(4):
                dma("s", lambda r=r: T.FG[:, 64 * r:64 * r + 64], lambda r=r: T.XF[12 + r::16, 0:V], "f%d" % r, 2500,
                    outs=[S("FG", 64 * r, 64 * r + 64)], ins=[S("XF", 0, V)])
        elif OPT["ct"] == "PA":
            row_t(t, "PA")
        if t == 0:
            for j, lo in enumerate(range(0, 2 * GH, GH // 2)):
                src = S("LG", lo, lo + GH // 2)
                if OPT["gl"][j] == "a":
                    mm([(S("PA", 0, GH // 2), S("IF"), src)], True, True)
                    src = S("PA", 0, GH // 2)
                plus(OPT["gl"][j], S("L", V + lo, V + lo + GH // 2), src, V + lo // GH * GH + LO)
        else:
            for d in range(2):
                scat(S("L", V, WD), u(108 - 4 * d, 2), S("LL%d" % (t - 1), 32 * d, 32 * d + 32))
        if OPT["eq"][t] == "v":
            entry("a", S("QV"), S("MV", 0, LN), S("XV"), S("PW", 256, 512))
        for h in range(2):
            y = S("Y%d" % h, 0, 128)
            act(half("XB", h), IND(S("XR", 0, V + 8), u(80 + 8 * h, 8)), scale=1.0 / 32)
            if OPT["z"][h] == "a":
                mm([(y, S("IH"), half("XV", h)), (y, S("IH"), half("XB", h)), (y, one(128), S("HF", 128, 256)),
                    (y, S("CB0"), S("HF", 256, 384)), (y, S("CB0"), S("HF", 384, 512))], True, True)
                act(half("ZZ", h), y)
                act(half("ZF", h), y, scale=32.0)
            else:
                mm([(y, S("I1"), half("XV", h)), (y, S("I1"), half("XB", h))], True, True)
                ts(half("ZT", h), y, 0.5 - 2.0 ** -11, A.mult, 1536.0, A.add)
                ts(half("ZZ", h), half("ZT", h), -1536.0, A.add)
                act(half("ZF", h), half("ZZ", h), scale=32.0)
            four("ZZ", h)
        for h in range(2):
            act(half("MB", h), IND(S("NB", 0, W), u(32 + 8 * h, 8)))
            scat(S("B"), u(48 + 8 * h, 8), half("MB", h))
        act(S("BB"), IND(S("B", 0, V + 8), u(80)))
        act(S("MC"), S("MB", 0, LN), bias=MCB)
        fold(S("PW", 0, 16), "SN", "BB", 0, 16, True, True)
        cp(BBU, S("PW", 0, 16))
        tt(G1, BF, VM, A.is_gt)
        if not last:
            ts(VL, VF, float(GH), A.is_lt)
            tt(G2, G1, VL, A.mult)
        nb = 1 if last else 2
        mm([(step("PA", r, 16 * nb, 16), S("ROWS", 128 * r, 128 * r + 128), S("wb", 0, 16 * nb)) for r in range(16)], True, False)
        if OPT["eq"][t] == "v":
            tt(S("EQ"), IND(S("XF", 0, W), BBU), S("QV"), A.is_equal)
        else:
            o = S("PW", 256, 512)
            act(S("QV"), IND(S("XF", 0, W), BBU))
            mm([(o, S("I1"), S("XV")), (o, S("WPS"), S("MV", 0, LN)), (o, S("IM1F"), S("QV"))], True, True)
            act(S("EQ"), o, bias=PSI, func=F.Abs)
        mm([(S("PA", LN * j, LN * j + LN), S("BD1" if OPT["eq"][t] == "v" else "BM4"), S("EQ")) for j in range(nb)], False, True)
        lift = -16.0 if OPT["eq"][t] == "v" else 0.0
        if not last:
            act(S("TL"), S("PA", LN, 2 * LN), bias=lift, func=F.Relu)
            scan(S("CN"), one(LN), S("TL"), 0.0, A.mult, A.add)
        act(S("JJ"), S("PA", 0, LN), scale=LOW, bias=c(26 if OPT["eq"][t] == "v" else 27), func=F.Relu)
        fold(S("PW", 0, 16), "SA", "JJ", 0, 16, True, True)
        ts(NJ, S("PW", 0, 16), -1.0 / 8, A.mult, 16384.0, A.add)
        if not last:
            act(w(38), S("PW", 0, 16), scale=-1.0 / 4, bias=24576.0)
        tt(w(16), NJ, VF, A.add)
        tt(w(17), NJ, BF, A.add)
        tt(w(18, 2), w(16, 2), DUMP, A.min)
        cp(fw(t, 0, 32), w(18, 2))
        for h in range(2):
            th, eb = S("PA", 256 * h, 256 * h + 256), S("PA", 256 * h + 128, 256 * h + 256)
            mm([spread(th, "JJ", h, S("TH")), spread(eb, "XV", h, S("BD4", 0, 128)), spread(eb, "XB", h, S("BM4")), spread(eb, "MC", h, S("RN"))], h == 0, h == 1)
        for h in range(2):
            tt(eu(h, 4), half("KS", h), S("PA", 256 * h, 256 * h + 128), A.is_ge)
            tt(eu(h, 1), S("QS", 256 * h, 256 * h + 128), S("PA", 256 * h + 128, 256 * h + 256), A.is_equal)

        def close(k, h, i):
            mm([(k, S("CB0"), one(128)), spread(k, "XV", h, S("BM4")), spread(k, "ZZ", h, S("BM4")),
                (k, S("I1F"), S("QS", 256 * h + 128 * i, 256 * h + 128 * i + 128))], False, True)

        for h in range(2):
            entries(t, 1, h, BU, S("L", 0, W), "OU", "GO")
        if last:
            ts(S("L", 0, V), S("L", 0, V), 1.5 * 2 ** 23 - LO, A.add, 1.5 * 2 ** 23, A.subtract)
        for h in range(2):
            kb = "K%d" % h
            k = S(kb, 0, 128)
            mm([(k, S("CB1"), one(128))], True, False)
            near("DB", gc, h, NC[1][h], kb, 0)
            mm([(k, S("IBIG"), eu(h, j)) for j in (1, 4)], False, False, True)
            close(k, h, 0)
            tt(half("KC", h), k, half("CL", h), A.min)
        if not last:
            entry("a", S("MZ", 0, LN), S("MV", 0, LN), S("ZZ"), S("PW", 256, 512))
            me, le, ml, ll = "ME%d" % t, "LE%d" % t, "ML%d" % t, "LL%d" % t
            for j in range(2):
                act(S("HB", 256 * j, 256 * j + 256), S("CN"), bias=c(18 + j), scale=-1.0, func=F.Sign, accum=S("q", 192 + j, 193 + j))
            ts(u(96, 2), S("q", 192, 194), 0.5, A.mult, 128.0, A.add)
            ts(u(98, 2), S("q", 192, 194), 0.5, A.mult, 128.0, A.add)
            s2 = u(96, 2)
            for j, src in enumerate(("MV", "MB")):
                act(S("MS", 32 * j, 32 * j + 32), IND(S(src), s2))
            act(S(me, 0, 64), IND(S("MZ"), SU), bias=R4A)
            act(S(me, 68, 132), IND(S("MZ"), SU), bias=R4B)
            fold(S("PW", 0, 4), "SN", "MS", 0, 4, True, True)
            ts(S("q", 0, 4), S("PW", 0, 4), GH - 0.5, A.subtract, 8192.0, A.mult)
            tt(S(me, 64, 68), S("q", 0, 4), S("PW", 0, 4), A.max)
            exchange([S(me, 0, 68), S(me, 64, 132)], [S(le, 68, 136), S(le, 0, 68)], "te%d" % t, "re%d" % t, 2500)
            mm([(S("PW", 0, 32), S("RN"), S("MS", 0, 32))], True, True)
            act(S("q", 32, 64), S("PW", 0, 32), bias=LO)
            if OPT["ct"] != "PA":
                row_t(t, OPT["ct"])
            ts(w(32), BF, V - 0.5, A.subtract, 32768.0, A.mult)
            tt(w(34), w(32), BF, A.max)
            tt(w(37), w(36), w(34), A.min)
            tt(w(39), w(38), AW, A.add)
            tt(wi(64), w(39), w(37), A.min)
            ts(wi(80), wi(64), 4095, A.bitwise_and)
            cp(PU, wi(80))
            scat(S("M"), OB, S("MF"))
            scat(S("XR"), OJ, S("ZF"))
            cp(IND(S("XF"), OJ), S("MZ", 0, LN))
            cp(IND(S("XF"), OB), S("MZ", 0, LN))
            for e in range(t - 1, -1, -1):
                act(S("FG", 0, LN), IND(S("XF"), fw(e, 0, 16)))
                cp(IND(S("XF"), fw(e, 16, 16)), S("FG", 0, LN))
            tt(S("q", 8, 12), S(le, 132, 136), c(112, 4), A.min)
            tt(S("q", 12, 16), S(le, 0, 4), c(120, 4), A.min)
            cp(u(108, 4), S("q", 8, 12))
            ts(u(104, 4), S("q", 12, 16), float(GH), A.add)
            cp(IND(S("XF", V, WD), u(104, 8)), S(le, 4, 132))
            if t < RO - 2:
                for d in range(2):
                    cp(fw(t, 32 + 2 * d, 2), u(104 + 4 * d, 2))
                    cp(fw(t, 36 + 2 * d, 2), u(106 + 4 * d, 2))
            for e in range(t - 1, -1, -1):
                (cp if OPT["fg"] == "v" else act)(S("FG", 256, 320), IND(S("XF", V, WD), fw(e, 32, 4)))
                cp(IND(S("XF", V, WD), fw(e, 36, 4)), S("FG", 256, 320))
            lanes(t + 1)
        else:
            scat(S("XR"), OJ, S("ZF"))
            act(S("X", 0, V), S("XR", 0, V), scale=1.0 / 32)
            dma("a", lambda: T.yx[:], lambda: T.X[:, 0:V], "ox", 3000, ins=[S("X", 0, V)])
            act(S("MF"), S("MV", 0, LN))
            scat(S("M"), OB, S("MF"))
            mm([(S("PW", 0, 64), S("IM1F"), S("FG", 64 * r, 64 * r + 64)) for r in range(4)], True, True)
            ts(wi(96, 64), S("PW", 0, 64), 4096.0, A.mult, MID, A.add)
            ts(wi(160, 64), wi(96, 64), 4095, A.bitwise_and)
            cp(S("FW"), wi(160, 64))
            act(S("MH"), IND(S("M", 0, V), S("FW")))
            fold(S("PW", 0, 64), "SN", "MH", 0, 64, True, True)
            act(S("YF"), S("PW", 0, 64))
            dma("s", lambda: T.yf[:], lambda: T.YF[:], "of", 2500, ins=[S("YF")])
        for h in range(2):
            kb = "K%d" % h
            k = S(kb, 128, 256)
            mm([(k, S("CB1"), one(128)), spread(k, "JJ", h, S("TH", 128, 256))], True, False)
            tt(eu(h, 3), S("QS", 256 * h + 128, 256 * h + 256), S("PA", 256 * h + 128, 256 * h + 256), A.is_equal)
            near("DC", "GO", h, NC[2][h], kb, 128)
            mm([(k, S("IMB"), eu(h, 4)), (k, S("IBIG"), eu(h, 3))], False, False, True)
            close(k, h, 1)
            tt(half("RF", h), k, half("KC", h), A.min)
            y = S("Y%d" % h, 0, 128)
            mm([(y, half("RF", h), S("IM1F")), (y, S("CB2"), one(128)), (y, S("CB0"), S("HF", 0, 128)), (y, half("RF", h), S("I1F"))], True, True)
            act(half("NL", h), y, bias=MID + (0.0 if last else LO))
            if last:
                cp(IND(S("L"), u(48 + 8 * h, 8)), half("NL", h))
            else:
                scat(S("L"), u(48 + 8 * h, 8), half("NL", h))
        if last:
            break
        ts(S("q", 0, 32), IND(S("NL"), s2), GH + LO, A.is_lt, 8192.0, A.mult)
        tt(S("q", 64, 96), S("q", 0, 32), S("q", 32, 64), A.add)
        tt(S("q", 160, 192), IND(S("NL"), s2), S("q", 64, 96), A.min)
        for d in range(2):
            act(S(ml, 32 * d, 32 * d + 32), S("q", 160, 192), bias=float(V + d * GH))
        exchange([S(ml, 0, 32), S(ml, 32, 64)], [S(ll, 0, 32), S(ll, 32, 64)], "tm%d" % t, "rm%d" % t, 2500)
        awake(t + 1)
    dma("s", lambda: T.yl[:], lambda: T.L[:, 0:V], "ol", 4000, ins=[S("L", 0, V)])
    return nodes, eng


def order(nodes):
    n = len(nodes)
    hist = {}
    deps = []
    for i, x in enumerate(nodes):
        d = {}
        acc = [(y, False) for y in x["rd"]] + [(y, True) for y in x["wr"]]
        for y, wr in acc:
            bank = SCRATCH[y[0]][0] == "psum"
            for (j, lo, hi, w2) in hist.get(y[0], ()):
                meet = lo < y[2] and y[1] < hi
                if SCRATCH[y[0]][0] == "sbuf" and (nodes[j]["sem"] or x["sem"]) and wr and w2:
                    q = 8 if SCRATCH[y[0]][2] in SHORT else 4
                    meet = lo // q * q < y[2] and y[1] // q * q < hi
                if bank and wr and w2 and x["free"] and nodes[j]["free"]:
                    continue
                if bank and (nodes[j]["e"] != x["e"] or wr or w2):
                    d[j] = d.get(j, False) or (w2 and not wr and meet)
                elif meet and (wr or w2):
                    d[j] = True
        for y, wr in acc:
            h = hist.setdefault(y[0], [])
            if SCRATCH[y[0]][0] == "psum":
                if not (wr and x["free"]):
                    h[:] = [z for z in h if z[0] == i or (not wr and (z[3] or nodes[z[0]]["e"] == x["e"]))]
            elif wr and y[3] == 1 and y[4] is None:
                h[:] = [z for z in h if z[0] == i or not (y[1] <= z[1] and z[2] <= y[2])]
            h.append((i, y[1], y[2], wr))
        d.pop(i, None)
        deps.append(d)
    pre = [sorted(set(list(deps[i]) + nodes[i]["after"])) for i in range(n)]
    queue = ["vapgsR".index(x["e"]) for x in nodes]
    ends = sorted(set(range(n)) - set(j for p in pre for j in p))
    zero = [0.0] * n

    def case(gather, scatter, pe, hop, far):
        cost = [max(1.0, x["cost"] * (pe / PEC if x["e"] == "p" else 1.0) + (gather - 1.56) * x["ind"][0] + (scatter - 3.8) * x["ind"][1]) for x in nodes]
        lats = [far * x["lat"] for x in nodes]
        fore, back = [[] for _ in range(n)], [[] for _ in range(n)]
        for i in range(n):
            for j in pre[i]:
                same = queue[i] == queue[j] and not deps[i].get(j, False)
                dl = (lats[j] if j in deps[i] or queue[i] == 5 else 0.0) + (0.0 if same else hop)
                fore[i].append((j, cost[j] + dl))
                back[j].append((i, cost[i] + dl))
        return cost, lats, fore, back
    cases = [case(*x) for x in CASES]

    def place(lst, cost, before, tail, at=None):
        at = at or [0.0] * n
        los, his = [[] for _ in range(6)], [[] for _ in range(6)]
        for k in lst:
            st = tail[k]
            for j, dl in before[k]:
                if at[j] + dl > st:
                    st = at[j] + dl
            lo, hi, c = los[queue[k]], his[queue[k]], cost[k]
            i = m = len(hi)
            while i and hi[i - 1] > st:
                i -= 1
            while i < m and lo[i] < st + c:
                if hi[i] > st:
                    st = hi[i]
                i += 1
            lo.insert(i, st)
            hi.insert(i, st + c)
            at[k] = st
        return at

    def replay(seq, cost, lats, fore, back):
        at = [0.0] * n
        free = [0.0] * 6
        for k in seq:
            st = free[queue[k]]
            for j, dl in fore[k]:
                if at[j] + dl > st:
                    st = at[j] + dl
            at[k] = st
            if queue[k] < 5:
                free[queue[k]] = st + cost[k]
        return at, max(at[i] + cost[i] + lats[i] for i in ends)

    def packed(key, cost, lats, fore, back):
        at = place(sorted(range(n), key=lambda i: key[i]), cost, fore, zero)
        rev = place(sorted(range(n), key=lambda i: -at[i] - cost[i]), cost, back, lats)
        at = place(sorted(range(n), key=lambda i: -rev[i] - cost[i]), cost, fore, zero)
        return sorted(range(n), key=lambda i: at[i])

    def judged(seq, bound=BIG):
        runs = [replay(seq, *cases[0])]
        if runs[0][1] > bound:
            return BIG, seq, runs
        runs += [replay(seq, *x) for x in cases[1:]]
        return sum(r[1] / u for r, u in zip(runs, unit)), seq, runs
    cost, lats, fore, back = cases[0]
    prio = [0.0] * n
    for i in range(n - 1, -1, -1):
        prio[i] = max([prio[k] - cost[k] + dl for k, dl in back[i]] + [lats[i]]) + cost[i]
    seq = packed([-x for x in prio], *cases[0])
    unit = [replay(seq, *x)[1] for x in cases]
    unit[0] /= 2.5
    best = judged(seq)
    rnd = 12345
    for it in range(PASSES):
        old, end = best[2][0]
        rnd = (rnd * 1103515245 + 12345) % 2147483648
        mid = end * (rnd / 2147483648.0)
        amp = AMP * (1 + rnd // 1024 % 4)
        key = list(old)
        for i in range(n):
            x = old[i]
            if x >= mid - SPAN:
                if x < mid + SPAN:
                    rnd = (rnd * 1103515245 + 12345) % 2147483648
                    x += amp * (rnd / 2147483648.0 - 0.5)
                for j in pre[i]:
                    if key[j] >= x:
                        x = key[j] + 1.0
                key[i] = x
        new = judged(packed(key, *cases[0]), 1.006 * end)
        if new[0] <= best[0]:
            best = new
    cur, late = best, None
    for it in range(LOCAL):
        score, seq, runs = cur
        old = runs[0][0]
        rnd = (rnd * 1103515245 + 12345) % 2147483648
        m = 20 + rnd // 64 % WIDE
        a = rnd // 16384 % (n - 10)
        amp = AMP * (0.25, 0.5, 1.0, 2.0)[rnd // 16 % 4]
        part = seq[a:a + m]
        key = {}
        for i in part:
            rnd = (rnd * 1103515245 + 12345) % 2147483648
            x = old[i] + amp * (rnd / 2147483648.0 - 0.5)
            for j in pre[i]:
                if key.get(j, -BIG) >= x:
                    x = key[j] + 1.0
            key[i] = x
        free = [0.0] * 6
        for k in seq[max(0, a - 200):a]:
            free[queue[k]] = old[k] + cost[k]
        free[5] = 0.0
        head = [free[q] for q in queue]
        at = place(sorted(part, key=key.get), cost, fore, head, list(old))
        if late is None:
            late, free = [0.0] * n, [0.0] * 6
            for k in reversed(seq):
                st = max(free[queue[k]], lats[k])
                for j, dl in back[k]:
                    if late[j] + dl > st:
                        st = late[j] + dl
                late[k] = st
                if queue[k] < 5:
                    free[queue[k]] = st + cost[k]
        free = [0.0] * 6
        for k in reversed(seq[a + m:a + m + 200]):
            free[queue[k]] = late[k] + cost[k]
        free[5] = 0.0
        rev = place(sorted(part, key=lambda i: -at[i] - cost[i]), cost, back, [max(free[queue[i]], lats[i]) for i in range(n)], list(late))
        at = place(sorted(part, key=lambda i: -rev[i] - cost[i]), cost, fore, head, at)
        new = judged(seq[:a] + sorted(part, key=lambda i: at[i]) + seq[a + m:], 1.004 * runs[0][1])
        if new[0] <= score + WARM * (1.0 - it / LOCAL) * (rnd // 256 % 1024) / 1024.0:
            cur, late = new, None
            if new[0] <= best[0]:
                best = new
    chains = {}
    for it in range(SWAPS):
        score, seq, runs = best
        rnd = (rnd * 1103515245 + 12345) % 2147483648
        c = rnd // 64 % len(cases)
        if c not in chains:
            cost, lats, fore, back = cases[c]
            at = runs[c][0]
            prev, last = {}, {}
            for k in seq:
                prev[k] = last.get(queue[k])
                last[queue[k]] = k
            k = max(ends, key=lambda i: at[i] + cost[i] + lats[i])
            chains[c] = []
            while k is not None:
                p = prev[k]
                if p is not None and queue[k] < 5 and at[p] + cost[p] >= at[k] - 0.5 and p not in pre[k]:
                    chains[c].append((p, k))
                    k = p
                else:
                    k = max(fore[k], key=lambda z: at[z[0]] + z[1])[0] if fore[k] else None
        if not chains[c]:
            continue
        a, b = chains[c][rnd // 4096 % len(chains[c])]
        lo, hi = seq.index(a), seq.index(b)
        for hop in range(rnd // 16 % 4 if rnd // 8 % 2 else 0):
            z = lo - 1
            while z >= 0 and queue[seq[z]] != queue[b]:
                z -= 1
            lo = z if z >= 0 else lo
        need, part = set(pre[b]), [b]
        for k in reversed(seq[lo:hi]):
            if k in need:
                part.append(k)
                need.update(pre[k])
        if seq[lo] in need:
            continue
        gone = set(part)
        new = judged(seq[:lo] + part[::-1] + [k for k in seq[lo:hi] if k not in gone] + seq[hi + 1:], 1.003 * runs[0][1])
        if new[0] <= score:
            best = new
            chains = {}
    return deps, best[1], best[2][0][0]


def rank_program(g, core, T, topo):
    if T.rank_of(core) is None:
        return
    nodes, eng = build(g, core, T, topo)
    if not PLAN:
        PLAN.append(order(nodes))
    deps, seq, times = PLAN[0]
    qsem = {"v": "sv", "a": "sa", "p": "sp", "g": "sg"}
    pos = {k: j for j, k in enumerate(seq)}
    know = {e: {} for e in "vapgs"}
    snap = {}
    waits = {}
    for k in seq:
        x = nodes[k]
        e = x["e"]
        if e == "R":
            snap[k] = {}
            continue
        need = []
        for j, hard in sorted(deps[k].items(), key=lambda z: -pos[z[0]]):
            y = nodes[j]
            if y["e"] == e and not hard:
                continue
            key = y["sem"] or y["e"]
            if know[e].get(key, -1) >= pos[j]:
                continue
            need.append(j)
            know[e][key] = pos[j]
            for a, b in snap[j].items():
                if know[e].get(a, -1) < b:
                    know[e][a] = b
        waits[k] = need
        snap[k] = dict(know[e])
    marked = set(j for k in waits for j in waits[k])
    lastof = {}
    for k in seq:
        if not nodes[k]["sem"]:
            lastof[nodes[k]["e"]] = k
    marked |= set(lastof.values())
    count = {}
    val = {}
    for k in seq:
        x = nodes[k]
        if x["sem"]:
            val[k] = (x["sem"], x["inc"])
        elif k in marked:
            count[x["e"]] = count.get(x["e"], 0) + 1
            val[k] = (qsem[x["e"]], count[x["e"]])
    for k in seq:
        x = nodes[k]
        if x["e"] == "R":
            continue
        for j in waits[k]:
            eng[x["e"]].wait_ge(T.sem[val[j][0]], val[j][1])
        r = x["fn"]()
        if r is not None and k in val:
            r.then_inc(T.sem[val[k][0]], 16 if x["sem"] else 1)
    for k in seq:
        if nodes[k]["sem"] or k in lastof.values():
            g.wait_ge(T.sem[val[k][0]], val[k][1])
